import numpy as np
import ml_dtypes


def mxq(x, axis, fmt="e4m3"):
    dtype, down = {"e4m3": (ml_dtypes.float8_e4m3fn, 7), "e5m2": (ml_dtypes.float8_e5m2, 14)}[fmt]
    v = np.moveaxis(np.asarray(x, np.float32).astype(ml_dtypes.bfloat16).astype(np.float64), axis, -1)
    blocks = v.reshape(v.shape[:-1] + (-1, 32))
    amax = np.abs(blocks).max(-1, keepdims=True)
    byte = np.maximum(np.where(amax > 0, np.frexp(amax)[1] - 1 + 127, 0) - down, 1)
    scale = np.exp2(byte - 127.0)
    codes = (blocks / scale).astype(np.float32).astype(dtype).astype(np.float64)
    return np.moveaxis((codes * scale).reshape(v.shape), -1, axis)


WIDE = False


def mx_kscale(k):
    if not WIDE:
        return np.ones(k)
    levels = np.array([24, -24, 12, -12, 0])
    if k % 512:
        return np.exp2(np.random.permutation(np.resize(levels, k // 32))).repeat(32)
    a = np.empty((k // 512, 16))
    for p in range(k // 512):
        a[p, :8] = np.random.permutation(np.resize(levels, 8))
        for g in range(8):
            far = levels[np.abs(levels - a[p, g]) >= 10]
            a[p, g + 8] = far[np.random.randint(len(far))]
    return np.exp2(a.ravel()).repeat(32)


def f64(x):
    return np.asarray(x).astype(np.float64)


def striped8(idx):
    return np.concatenate([v.reshape(-1, 16).T for v in idx]).astype(np.uint16)


def unstriped8(offs):
    return np.stack([offs[16 * g:16 * g + 16].T.reshape(-1) for g in range(8)]).astype(np.int64)


E2M1 = np.array([0.0, 0.5, 1.0, 1.5, 2.0, 3.0, 4.0, 6.0, -0.0, -0.5, -1.0, -1.5, -2.0, -3.0, -4.0, -6.0])


def pack_weight(w, fmt):
    k, n = w.shape
    w = f64(np.asarray(w, np.float32).astype(ml_dtypes.bfloat16)).reshape(k // 32, 32, n)
    amax = np.abs(w).max(1)
    if fmt == "e4m3":
        byte = np.frexp(amax)[1] - 1 + 127 - 7
    else:
        mant, ex = np.frexp(amax / 6.0)
        byte = np.where(mant > 0.5, ex, ex - 1) + 127
    byte = np.clip(np.where(amax > 0, byte, 1), 1, 254)
    scaled = (w * np.exp2(127.0 - byte)[:, None, :]).reshape(k, n).astype(np.float32)
    by_word = np.ascontiguousarray(scaled.reshape(k // 512, 128, 4, n).transpose(0, 1, 3, 2))
    if fmt == "e4m3":
        words = by_word.astype(ml_dtypes.float8_e4m3fn).view(np.uint8)
    else:
        c = by_word.astype(ml_dtypes.float4_e2m1fn).view(np.uint8) & 0xF
        words = (c[..., 0::2] | (c[..., 1::2] << 4)).reshape(k // 512, 128, 2 * n)
    return np.ascontiguousarray(words), np.ascontiguousarray(byte.astype(np.uint8).reshape(k // 512, 16, n))


def unpack_weight(words, scales, fmt):
    g, _, n = scales.shape
    words = np.ascontiguousarray(words).reshape(g, 128, n, -1)
    if fmt == "e4m3":
        vals = words.view(ml_dtypes.float8_e4m3fn).astype(np.float64)
    else:
        nib = np.empty((g, 128, n, 4), np.uint8)
        nib[..., 0::2] = words & 0xF
        nib[..., 1::2] = words >> 4
        vals = E2M1[nib]
    vals = vals * np.repeat(np.exp2(scales.astype(np.float64) - 127.0), 8, axis=1)[..., None]
    return vals.transpose(0, 1, 3, 2).reshape(g * 512, n)


def sigm(f):
    return 1.0 / (1.0 + np.exp(-np.maximum(f, -700.0)))


K, R, N, T, J = 512, 1024, 512, 2048, 1024


def setup_inputs():
    n = np.random.standard_normal
    s = mx_kscale(K)[:, None]
    u = mx_kscale(R)[:, None]
    p_wd = pack_weight(n((R, N)) / np.sqrt(R) / u, "e4m3")
    return {
        "xT": (n((K, T)) * s).astype(np.float32),
        "wgt": np.repeat(np.random.uniform(0.5, 2.0, (8, J)), 16, axis=0).astype(np.float32),
        "wg": (n((K, R)) / np.sqrt(K) / s).astype(np.float32),
        "wu": (n((K, R)) / np.sqrt(K) / s * u.T).astype(np.float32),
        "wd_words": p_wd[0],
        "wd_scales": p_wd[1],
        "wgo": np.repeat(np.random.uniform(0.5, 2.0, (8, J)), 16, axis=0).astype(np.float32),
        "offs": striped8(np.stack([np.random.permutation(T)[:J] for _ in range(8)])),
        "offs2": striped8(np.stack([np.random.permutation(T)[:J] for _ in range(8)])),
    }


def reference(xT, wgt, wg, wu, wd_words, wd_scales, wgo, offs, offs2):
    idx = unstriped8(offs)
    idx2 = unstriped8(offs2)
    rows = np.arange(K)
    xg = f64(wgt)[rows // 4 % 128] * f64(xT)[rows[:, None], idx[rows % 512 // 64]]
    xT_ = mxq(xg, 0, "e4m3")
    wg_ = mxq(f64(wg), 0, "e4m3")
    wu_ = mxq(f64(wu), 0, "e4m3")
    ga = wg_.T @ xT_
    ub = wu_.T @ xT_
    h = sigm(ga) * ub
    h_ = mxq(h, 0, "e4m3")
    wd_ = unpack_weight(wd_words, wd_scales, "e4m3")
    y = wd_.T @ h_
    out = np.zeros((N, T))
    rows = np.arange(N)
    out[rows[:, None], idx2[rows % 128 // 16]] = f64(wgo)[rows % 128] * (y)
    return out

@@ -1,0 +1,214 @@
+from contextlib import ExitStack
+
+import concourse.mybir as mybir
+
+K, R, N, T, J = 512, 1024, 512, 2048, 1024
+FLOPS = 2 * K * R * J * 2 + 2 * R * N * J
+
+F32 = mybir.dt.float32
+BF16 = mybir.dt.bfloat16
+I32 = mybir.dt.int32
+U32 = mybir.dt.uint32
+U16 = mybir.dt.uint16
+U8 = mybir.dt.uint8
+FP8X4 = mybir.dt.float8_e4m3fn_x4
+MULT = mybir.AluOpType.mult
+SIGMOID = mybir.ActivationFunctionType.Sigmoid
+
+P = 128
+PACK = 4
+PASS = P * PACK
+HALF = J // 2
+LIST_COLS = HALF // 16
+
+
+def tile_list_sigm_scat_kernel(
+    tc, xT, wgt, wg, wu, wd_words, wd_scales, wgo, offs, offs2, out
+):
+    nc = tc.nc
+    with ExitStack() as ctx:
+        keep = ctx.enter_context(tc.tile_pool(name="keep", bufs=1))
+        ring = ctx.enter_context(tc.tile_pool(name="ring", bufs=8))
+        psum = ctx.enter_context(tc.psum_pool(name="psum", bufs=3))
+
+        pick_list = keep.tile([P, J // 16], U16, name="pick_list")
+        put_list = keep.tile([P, J // 16], U16, name="put_list")
+        planes = [keep.tile([P, T], F32, name=f"plane{i}") for i in range(PACK)]
+        wgt_sb = [keep.tile([P, HALF], F32, name=f"wgt{h}") for h in range(2)]
+        wgo_sb = keep.tile([P, J], F32, name="wgo_sb")
+        w_raw = {(w, a): keep.tile([P, PACK, PASS], F32, name=f"raw{w}{a}") for w in "gu" for a in range(2)}
+        wd_codes = keep.tile([P, 2, N], U32, name="wd_codes", align_bytes=64)
+        wd_sc = keep.tile([P, 2, N], U8, name="wd_sc", align_bytes=64)
+        pages = [keep.tile([P, T], F32, name=f"page{n}") for n in range(N // P)]
+        warm = keep.tile([P, 8], F32, name="warm")
+        warm_out = keep.tile([P, 8], F32, name="warm_out")
+
+        x_rows = xT.rearrange("(p i) t -> p i t", i=PACK)
+        w_rows = {"g": wg.rearrange("(p i) r -> p i r", i=PACK), "u": wu.rearrange("(p i) r -> p i r", i=PACK)}
+
+        nc.gpsimd.memset(warm[:], 0.0)
+        nc.gpsimd.memset(wd_sc[:].rearrange("p a n -> p (a n)").bitcast(U32), 0)
+        nc.scalar.activation(warm_out[:], warm[:], SIGMOID)
+
+        nc.sync.dma_start(pick_list[:], offs)
+        nc.sync.dma_start(wgt_sb[0][:], wgt[:, 0:HALF])
+        nc.sync.dma_start(planes[0][:], x_rows[:, 0, :])
+        nc.sync.dma_start(wgt_sb[1][:], wgt[:, HALF:J])
+        for i in range(1, PACK):
+            nc.sync.dma_start(planes[i][:], x_rows[:, i, :])
+        for a in range(2):
+            for w in "gu":
+                nc.sync.dma_start(w_raw[w, a][:], w_rows[w][:, :, a * PASS : (a + 1) * PASS])
+        nc.sync.dma_start(wd_codes[:].bitcast(I32), wd_words.rearrange("a p n t -> p a (n t)").bitcast(I32))
+        nc.sync.dma_start(put_list[:], offs2)
+        nc.sync.dma_start(wgo_sb[:], wgo)
+        sc_rows = wd_scales.bitcast(I32).rearrange("a q n -> q a n")
+        for quad in range(4):
+            nc.sync.dma_start(
+                wd_sc[32 * quad : 32 * quad + 4, :, :].bitcast(I32), sc_rows[4 * quad : 4 * quad + 4, :, :]
+            )
+
+        for page in pages:
+            nc.gpsimd.memset(page[:], 0.0)
+
+        picked = {(h, pr): keep.tile([P, 2, HALF], F32, name=f"picked{h}{pr}") for h in range(2) for pr in range(2)}
+        x_bf = [keep.tile([P, HALF, PACK], BF16, name=f"x_bf{h}", align_bytes=64) for h in range(2)]
+        for pr in range(2):
+            for e in range(2):
+                for h in range(2):
+                    nc.vector.tensor_tensor(
+                        picked[h, pr][:, e, :],
+                        planes[2 * pr + e][:].indirect(pick_list[:, h * LIST_COLS : (h + 1) * LIST_COLS]),
+                        wgt_sb[h][:],
+                        MULT,
+                    )
+            for h in range(2):
+                nc.scalar.copy(
+                    x_bf[h][:, :, 2 * pr : 2 * pr + 2].rearrange("p (c f) e -> p c e f", f=4),
+                    picked[h, pr][:].rearrange("p e (c f) -> p c e f", f=4),
+                )
+
+        def quantize(name, src, words):
+            codes = keep.tile([P, words], U32, name=f"codes_{name}", align_bytes=64)
+            scales = keep.tile([P, words], U8, name=f"scales_{name}", align_bytes=64)
+            nc.vector.quantize_mx(out=codes[:].bitcast(FP8X4), scales=scales[:], in_=src)
+            return codes, scales
+
+        w_bf = {}
+
+        def interleave_w(w, a, tp, engine):
+            tile = keep.tile([P, 2, P, PACK], BF16, name=f"w_bf{w}{a}{tp}", align_bytes=64)
+            dst = tile[:].rearrange("p t m i -> p m i t")
+            src = w_raw[w, a][:].rearrange("p i (m t) -> p m i t", t=PACK)[:, :, :, 2 * tp : 2 * tp + 2]
+            if engine == "vector":
+                nc.vector.tensor_copy(dst, src)
+            else:
+                nc.scalar.copy(dst, src)
+            w_bf[w, a, tp] = tile
+
+        w_q = {}
+
+        def quantize_w(w, a, tp):
+            w_q[w, a, tp] = quantize(f"{w}{a}{tp}", w_bf[w, a, tp][:].rearrange("p t m i -> p (t m i)"), 2 * P)
+
+        x_q = {}
+
+        def quantize_x(h):
+            x_q[h] = quantize(f"x{h}", x_bf[h][:].rearrange("p j i -> p (j i)"), HALF)
+
+        def first_product(w, a, h, c):
+            bank = psum.tile([P, PACK, P], F32, name=f"bank_{w}", tag=f"bank_{w}")
+            cols = slice(c * P, (c + 1) * P)
+            for t in range(PACK):
+                codes, scales = w_q[w, a, t // 2]
+                m = slice((t % 2) * P, (t % 2 + 1) * P)
+                nc.tensor.matmul_mx(
+                    out=bank[:, t, :],
+                    lhsT=codes[:, m].bitcast(FP8X4),
+                    lhsT_scale=scales[:, m],
+                    rhs=x_q[h][0][:, cols].bitcast(FP8X4),
+                    rhs_scale=x_q[h][1][:, cols],
+                    start=True,
+                    stop=True,
+                )
+            return bank[:].rearrange("p t j -> p j t")
+
+        gates = {}
+
+        def gate(a, h, c):
+            sig = ring.tile([P, P, PACK], F32, name="sig")
+            nc.scalar.activation(sig[:], first_product("g", a, h, c), SIGMOID)
+            gates[a, h, c] = sig
+
+        h_bf = {(a, h): keep.tile([P, 4, P, PACK], BF16, name=f"h_bf{a}{h}", align_bytes=64) for a in range(2) for h in range(2)}
+
+        def hidden(a, h, c):
+            nc.vector.tensor_tensor(h_bf[a, h][:, c, :, :], first_product("u", a, h, c), gates[a, h, c][:], MULT)
+
+        h_q = {}
+
+        def quantize_h(a, h):
+            h_q[a, h] = quantize(f"h{a}{h}", h_bf[a, h][:].rearrange("p c j t -> p (c j t)"), HALF)
+
+        def put(n, h):
+            bank = psum.tile([P, HALF], F32, name="bank_y", tag="bank_y", bufs=2)
+            m = slice(n * P, (n + 1) * P)
+            for a in range(2):
+                nc.tensor.matmul_mx(
+                    out=bank[:],
+                    lhsT=wd_codes[:, a, m].bitcast(FP8X4),
+                    lhsT_scale=wd_sc[:, a, m],
+                    rhs=h_q[a, h][0][:].bitcast(FP8X4),
+                    rhs_scale=h_q[a, h][1][:],
+                    start=(a == 0),
+                    stop=(a == 1),
+                )
+            y = ring.tile([P, HALF], F32, name="y", bufs=4)
+            nc.scalar.copy(y[:], bank[:])
+            nc.vector.tensor_tensor(
+                pages[n][:].indirect(put_list[:, h * LIST_COLS : (h + 1) * LIST_COLS]),
+                y[:],
+                wgo_sb[:, h * HALF : (h + 1) * HALF],
+                MULT,
+            )
+
+        interleave_w("g", 0, 0, "vector")
+        interleave_w("g", 0, 1, "vector")
+        quantize_x(0)
+        quantize_w("g", 0, 0)
+        quantize_w("g", 0, 1)
+        interleave_w("u", 0, 1, "scalar")
+        interleave_w("u", 0, 0, "vector")
+        quantize_x(1)
+        quantize_w("u", 0, 0)
+        quantize_w("u", 0, 1)
+        for c in range(4):
+            gate(0, 0, c)
+            hidden(0, 0, c)
+        for tp in range(2):
+            interleave_w("g", 1, tp, "scalar")
+        for c in range(4):
+            gate(0, 1, c)
+            hidden(0, 1, c)
+            if c == 0:
+                quantize_h(0, 0)
+        for tp in range(2):
+            interleave_w("u", 1, tp, "scalar")
+        for tp in range(2):
+            quantize_w("g", 1, tp)
+        quantize_h(0, 1)
+        for tp in range(2):
+            quantize_w("u", 1, tp)
+        for h in range(2):
+            for c in range(4):
+                gate(1, h, c)
+                hidden(1, h, c)
+                if (h, c) == (1, 0):
+                    quantize_h(1, 0)
+        put(0, 0)
+        quantize_h(1, 1)
+        for n in range(1, N // P):
+            put(n, 0)
+        for n in range(N // P):
+            put(n, 1)
+            nc.sync.dma_start(out[n * P : (n + 1) * P, :], pages[n][:])

@@ -28,27 +28,39 @@ def tile_list_sigm_scat_kernel(
     nc = tc.nc
     with ExitStack() as ctx:
         keep = ctx.enter_context(tc.tile_pool(name="keep", bufs=1))
-        ring = ctx.enter_context(tc.tile_pool(name="ring", bufs=8))
-        psum = ctx.enter_context(tc.psum_pool(name="psum", bufs=3))
+        psum = ctx.enter_context(tc.psum_pool(name="psum", bufs=1))
 
         pick_list = keep.tile([P, J // 16], U16, name="pick_list")
         put_list = keep.tile([P, J // 16], U16, name="put_list")
         planes = [keep.tile([P, T], F32, name=f"plane{i}") for i in range(PACK)]
         wgt_sb = [keep.tile([P, HALF], F32, name=f"wgt{h}") for h in range(2)]
         wgo_sb = keep.tile([P, J], F32, name="wgo_sb")
-        w_raw = {(w, a): keep.tile([P, PACK, PASS], F32, name=f"raw{w}{a}") for w in "gu" for a in range(2)}
+        w_raw = {
+            (w, a): keep.tile([P, PACK, PASS], F32, name=f"raw{w}{a}", tag=f"raw{w}{a}", align_bytes=64)
+            for w in "gu"
+            for a in range(2)
+        }
         wd_codes = keep.tile([P, 2, N], U32, name="wd_codes", align_bytes=64)
         wd_sc = keep.tile([P, 2, N], U8, name="wd_sc", align_bytes=64)
-        pages = [keep.tile([P, T], F32, name=f"page{n}") for n in range(N // P)]
+        pages = [keep.tile([P, T], F32, name=f"page{n}") for n in range(3)]
         warm = keep.tile([P, 8], F32, name="warm")
         warm_out = keep.tile([P, 8], F32, name="warm_out")
+        banks = [psum.tile([P, PASS], F32, name=f"bank{b}") for b in range(8)]
+        gates = [keep.tile([P, P, PACK], F32, name=f"gate{b}") for b in range(6)]
+        ups = [keep.tile([P, P, PACK], F32, name=f"up{b}") for b in range(0)]
+        ys = [keep.tile([P, HALF], F32, name=f"y{b}") for b in range(3)]
+        yws = [keep.tile([P, HALF], F32, name=f"yw{b}") for b in range(0)]
 
         x_rows = xT.rearrange("(p i) t -> p i t", i=PACK)
         w_rows = {"g": wg.rearrange("(p i) r -> p i r", i=PACK), "u": wu.rearrange("(p i) r -> p i r", i=PACK)}
 
         nc.gpsimd.memset(warm[:], 0.0)
-        nc.gpsimd.memset(wd_sc[:].rearrange("p a n -> p (a n)").bitcast(U32), 0)
         nc.scalar.activation(warm_out[:], warm[:], SIGMOID)
+        for page in pages[:2]:
+            nc.vector.memset(page[:], 0.0)
+        for page in pages[2:]:
+            nc.gpsimd.memset(page[:], 0.0)
+        nc.vector.memset(wd_sc[:].rearrange("p a n -> p (a n)").bitcast(U32), 0)
 
         nc.sync.dma_start(pick_list[:], offs)
         nc.sync.dma_start(wgt_sb[0][:], wgt[:, 0:HALF])
@@ -68,11 +80,17 @@ def tile_list_sigm_scat_kernel(
                 wd_sc[32 * quad : 32 * quad + 4, :, :].bitcast(I32), sc_rows[4 * quad : 4 * quad + 4, :, :]
             )
 
-        for page in pages:
-            nc.gpsimd.memset(page[:], 0.0)
-
         picked = {(h, pr): keep.tile([P, 2, HALF], F32, name=f"picked{h}{pr}") for h in range(2) for pr in range(2)}
         x_bf = [keep.tile([P, HALF, PACK], BF16, name=f"x_bf{h}", align_bytes=64) for h in range(2)]
+
+        def weave_x(h, pr, engine):
+            dst = x_bf[h][:, :, 2 * pr : 2 * pr + 2].rearrange("p (c f) e -> p c e f", f=4)
+            src = picked[h, pr][:].rearrange("p e (c f) -> p c e f", f=4)
+            if engine == "vector":
+                nc.vector.tensor_copy(dst, src)
+            else:
+                nc.scalar.copy(dst, src)
+
         for pr in range(2):
             for e in range(2):
                 for h in range(2):
@@ -83,13 +101,11 @@ def tile_list_sigm_scat_kernel(
                         MULT,
                     )
             for h in range(2):
-                nc.scalar.copy(
-                    x_bf[h][:, :, 2 * pr : 2 * pr + 2].rearrange("p (c f) e -> p c e f", f=4),
-                    picked[h, pr][:].rearrange("p e (c f) -> p c e f", f=4),
-                )
+                if (pr, h) != (1, 1):
+                    weave_x(h, pr, "scalar")
 
-        def quantize(name, src, words):
-            codes = keep.tile([P, words], U32, name=f"codes_{name}", align_bytes=64)
+        def quantize(name, src, words, tag=None):
+            codes = keep.tile([P, words], U32, name=f"codes_{name}", tag=tag or f"codes_{name}", align_bytes=64)
             scales = keep.tile([P, words], U8, name=f"scales_{name}", align_bytes=64)
             nc.vector.quantize_mx(out=codes[:].bitcast(FP8X4), scales=scales[:], in_=src)
             return codes, scales
@@ -102,6 +118,8 @@ def tile_list_sigm_scat_kernel(
             src = w_raw[w, a][:].rearrange("p i (m t) -> p m i t", t=PACK)[:, :, :, 2 * tp : 2 * tp + 2]
             if engine == "vector":
                 nc.vector.tensor_copy(dst, src)
+            elif engine == "gpsimd":
+                nc.gpsimd.tensor_copy(dst, src)
             else:
                 nc.scalar.copy(dst, src)
             w_bf[w, a, tp] = tile
@@ -113,45 +131,58 @@ def tile_list_sigm_scat_kernel(
 
         x_q = {}
 
-        def quantize_x(h):
-            x_q[h] = quantize(f"x{h}", x_bf[h][:].rearrange("p j i -> p (j i)"), HALF)
+        def quantize_x(h, tag=None):
+            x_q[h] = quantize(f"x{h}", x_bf[h][:].rearrange("p j i -> p (j i)"), HALF, tag)
 
-        def first_product(w, a, h, c):
-            bank = psum.tile([P, PACK, P], F32, name=f"bank_{w}", tag=f"bank_{w}")
-            cols = slice(c * P, (c + 1) * P)
+        def first_product(w, a, c, bank):
+            cols = slice((c % 4) * P, (c % 4 + 1) * P)
             for t in range(PACK):
                 codes, scales = w_q[w, a, t // 2]
                 m = slice((t % 2) * P, (t % 2 + 1) * P)
                 nc.tensor.matmul_mx(
-                    out=bank[:, t, :],
+                    out=bank[:, t * P : (t + 1) * P],
                     lhsT=codes[:, m].bitcast(FP8X4),
                     lhsT_scale=scales[:, m],
-                    rhs=x_q[h][0][:, cols].bitcast(FP8X4),
-                    rhs_scale=x_q[h][1][:, cols],
+                    rhs=x_q[c // 4][0][:, cols].bitcast(FP8X4),
+                    rhs_scale=x_q[c // 4][1][:, cols],
                     start=True,
                     stop=True,
                 )
-            return bank[:].rearrange("p t j -> p j t")
+            return bank[:].rearrange("p (t j) -> p j t", t=PACK)
 
-        gates = {}
+        h_bf = {
+            (a, h): keep.tile([P, 4, P, PACK], BF16, name=f"h_bf{a}{h}", align_bytes=64)
+            for a in range(2)
+            for h in range(2)
+        }
+        made = []
+        lifted = []
 
-        def gate(a, h, c):
-            sig = ring.tile([P, P, PACK], F32, name="sig")
-            nc.scalar.activation(sig[:], first_product("g", a, h, c), SIGMOID)
-            gates[a, h, c] = sig
-
-        h_bf = {(a, h): keep.tile([P, 4, P, PACK], BF16, name=f"h_bf{a}{h}", align_bytes=64) for a in range(2) for h in range(2)}
-
-        def hidden(a, h, c):
-            nc.vector.tensor_tensor(h_bf[a, h][:, c, :, :], first_product("u", a, h, c), gates[a, h, c][:], MULT)
+        def hidden(a, c, engine="vector"):
+            step = len(made)
+            made.append(c)
+            sig = gates[step % len(gates)]
+            nc.scalar.activation(sig[:], first_product("g", a, c, banks[step % 3]), SIGMOID)
+            dst = h_bf[a, c // 4][:, c % 4, :, :]
+            up = first_product("u", a, c, banks[3 + step % 3])
+            if engine == "vector":
+                nc.vector.tensor_tensor(dst, up, sig[:], MULT)
+            else:
+                up_sb = ups[len(lifted) % len(ups)]
+                lifted.append(c)
+                nc.scalar.copy(up_sb[:], up)
+                nc.gpsimd.tensor_tensor(dst, up_sb[:], sig[:], MULT)
 
         h_q = {}
 
         def quantize_h(a, h):
             h_q[a, h] = quantize(f"h{a}{h}", h_bf[a, h][:].rearrange("p c j t -> p (c j t)"), HALF)
 
-        def put(n, h):
-            bank = psum.tile([P, HALF], F32, name="bank_y", tag="bank_y", bufs=2)
+        sums = []
+
+        def second_product(n, h):
+            bank = banks[6 + len(sums) % 2]
+            sums.append(n)
             m = slice(n * P, (n + 1) * P)
             for a in range(2):
                 nc.tensor.matmul_mx(
@@ -163,52 +194,69 @@ def tile_list_sigm_scat_kernel(
                     start=(a == 0),
                     stop=(a == 1),
                 )
-            y = ring.tile([P, HALF], F32, name="y", bufs=4)
-            nc.scalar.copy(y[:], bank[:])
-            nc.vector.tensor_tensor(
-                pages[n][:].indirect(put_list[:, h * LIST_COLS : (h + 1) * LIST_COLS]),
-                y[:],
-                wgo_sb[:, h * HALF : (h + 1) * HALF],
-                MULT,
-            )
+            return bank
 
+        def put(n, h, engine="fused"):
+            y = ys[len(sums) % len(ys)]
+            bank = second_product(n, h)
+            places = pages[n % len(pages)][:].indirect(put_list[:, h * LIST_COLS : (h + 1) * LIST_COLS])
+            weights = wgo_sb[:, h * HALF : (h + 1) * HALF]
+            if engine == "vector":
+                nc.vector.tensor_tensor(y[:], bank[:], weights, MULT)
+                nc.vector.tensor_copy(places, y[:])
+                return
+            nc.scalar.copy(y[:], bank[:])
+            if engine == "gpsimd":
+                yw = yws[len(sums) % len(yws)]
+                nc.gpsimd.tensor_tensor(yw[:], y[:], weights, MULT)
+                nc.vector.tensor_copy(places, yw[:])
+            else:
+                nc.vector.tensor_tensor(places, y[:], weights, MULT)
+
+        def put_whole(n):
+            y = keep.tile([P, J], F32, name=f"y_whole{n}")
+            for h in range(2):
+                nc.scalar.copy(y[:, h * HALF : (h + 1) * HALF], second_product(n, h)[:])
+            nc.vector.tensor_tensor(pages[n % len(pages)][:].indirect(put_list[:]), y[:], wgo_sb[:], MULT)
+
+        def store(n):
+            nc.sync.dma_start(out[n * P : (n + 1) * P, :], pages[n % len(pages)][:])
+
+        weave_x(1, 1, "scalar")
         interleave_w("g", 0, 0, "vector")
         interleave_w("g", 0, 1, "vector")
-        quantize_x(0)
+        quantize_x(0, "rawg0")
         quantize_w("g", 0, 0)
         quantize_w("g", 0, 1)
         interleave_w("u", 0, 1, "scalar")
         interleave_w("u", 0, 0, "vector")
-        quantize_x(1)
         quantize_w("u", 0, 0)
+        quantize_x(1)
         quantize_w("u", 0, 1)
+        interleave_w("g", 1, 0, "vector")
         for c in range(4):
-            gate(0, 0, c)
-            hidden(0, 0, c)
-        for tp in range(2):
-            interleave_w("g", 1, tp, "scalar")
-        for c in range(4):
-            gate(0, 1, c)
-            hidden(0, 1, c)
-            if c == 0:
-                quantize_h(0, 0)
-        for tp in range(2):
-            interleave_w("u", 1, tp, "scalar")
-        for tp in range(2):
-            quantize_w("g", 1, tp)
+            hidden(0, c)
+        interleave_w("g", 1, 1, "scalar")
+        quantize_w("g", 1, 0)
+        hidden(0, 4)
+        quantize_w("g", 1, 1)
+        for c in range(5, 8):
+            hidden(0, c)
+        interleave_w("u", 1, 1, "scalar")
+        interleave_w("u", 1, 0, "vector")
+        quantize_w("u", 1, 1)
+        quantize_w("u", 1, 0)
+        quantize_h(0, 0)
         quantize_h(0, 1)
-        for tp in range(2):
-            quantize_w("u", 1, tp)
-        for h in range(2):
-            for c in range(4):
-                gate(1, h, c)
-                hidden(1, h, c)
-                if (h, c) == (1, 0):
-                    quantize_h(1, 0)
-        put(0, 0)
+        for c in range(8):
+            hidden(1, c)
+            if c == 4:
+                quantize_h(1, 0)
         quantize_h(1, 1)
-        for n in range(1, N // P):
-            put(n, 0)
-        for n in range(N // P):
-            put(n, 1)
-            nc.sync.dma_start(out[n * P : (n + 1) * P, :], pages[n][:])
+        for h in range(2):
+            for n in range(3):
+                put(n, h)
+                if h == 1:
+                    store(n)
+        put_whole(3)
+        store(3)

@@ -20,6 +20,7 @@ PACK = 4
 PASS = P * PACK
 HALF = J // 2
 LIST_COLS = HALF // 16
+POOL_PIECE = 64
 
 
 def tile_list_sigm_scat_kernel(
@@ -47,9 +48,8 @@ def tile_list_sigm_scat_kernel(
         warm_out = keep.tile([P, 8], F32, name="warm_out")
         banks = [psum.tile([P, PASS], F32, name=f"bank{b}") for b in range(8)]
         gates = [keep.tile([P, P, PACK], F32, name=f"gate{b}") for b in range(6)]
-        ups = [keep.tile([P, P, PACK], F32, name=f"up{b}") for b in range(0)]
+        ups = [keep.tile([P, P, PACK], F32, name=f"up{b}") for b in range(4)]
         ys = [keep.tile([P, HALF], F32, name=f"y{b}") for b in range(3)]
-        yws = [keep.tile([P, HALF], F32, name=f"yw{b}") for b in range(0)]
 
         x_rows = xT.rearrange("(p i) t -> p i t", i=PACK)
         w_rows = {"g": wg.rearrange("(p i) r -> p i r", i=PACK), "u": wu.rearrange("(p i) r -> p i r", i=PACK)}
@@ -150,19 +150,24 @@ def tile_list_sigm_scat_kernel(
                 )
             return bank[:].rearrange("p (t j) -> p j t", t=PACK)
 
-        h_bf = {
-            (a, h): keep.tile([P, 4, P, PACK], BF16, name=f"h_bf{a}{h}", align_bytes=64)
-            for a in range(2)
-            for h in range(2)
-        }
-        made = []
+        h_rest = keep.tile([P, 2 * HALF * PACK], BF16, name="h_rest", align_bytes=64)
+        h_bf = {(a, 0): keep.tile([P, 4, P, PACK], BF16, name=f"h_bf{a}", align_bytes=64)[:] for a in range(2)}
+        for a in range(2):
+            part = h_rest[:, a * HALF * PACK : (a + 1) * HALF * PACK]
+            h_bf[a, 1] = part.rearrange("p (c j t) -> p c j t", c=4, t=PACK)
+        made = {}
         lifted = []
 
-        def hidden(a, c, engine="vector"):
+        def gate(a, c):
             step = len(made)
-            made.append(c)
+            made[a, c] = step
+            nc.scalar.activation(gates[step % len(gates)][:], first_product("g", a, c, banks[step % 3]), SIGMOID)
+
+        def hidden(a, c, engine="vector"):
+            if (a, c) not in made:
+                gate(a, c)
+            step = made[a, c]
             sig = gates[step % len(gates)]
-            nc.scalar.activation(sig[:], first_product("g", a, c, banks[step % 3]), SIGMOID)
             dst = h_bf[a, c // 4][:, c % 4, :, :]
             up = first_product("u", a, c, banks[3 + step % 3])
             if engine == "vector":
@@ -171,12 +176,20 @@ def tile_list_sigm_scat_kernel(
                 up_sb = ups[len(lifted) % len(ups)]
                 lifted.append(c)
                 nc.scalar.copy(up_sb[:], up)
-                nc.gpsimd.tensor_tensor(dst, up_sb[:], sig[:], MULT)
+                for j0 in range(0, P, POOL_PIECE):
+                    cols = slice(j0, j0 + POOL_PIECE)
+                    nc.gpsimd.tensor_tensor(dst[:, cols, :], up_sb[:, cols, :], sig[:, cols, :], MULT)
 
         h_q = {}
 
         def quantize_h(a, h):
-            h_q[a, h] = quantize(f"h{a}{h}", h_bf[a, h][:].rearrange("p c j t -> p (c j t)"), HALF)
+            codes, scales = quantize(f"h{a}{h}", h_bf[a, h].rearrange("p c j t -> p (c j t)"), HALF)
+            h_q[a, h] = codes[:], scales[:]
+
+        def quantize_rest():
+            codes, scales = quantize("h_rest", h_rest[:], J)
+            for a in range(2):
+                h_q[a, 1] = codes[:, a * HALF : (a + 1) * HALF], scales[:, a * HALF : (a + 1) * HALF]
 
         sums = []
 
@@ -189,29 +202,21 @@ def tile_list_sigm_scat_kernel(
                     out=bank[:],
                     lhsT=wd_codes[:, a, m].bitcast(FP8X4),
                     lhsT_scale=wd_sc[:, a, m],
-                    rhs=h_q[a, h][0][:].bitcast(FP8X4),
-                    rhs_scale=h_q[a, h][1][:],
+                    rhs=h_q[a, h][0].bitcast(FP8X4),
+                    rhs_scale=h_q[a, h][1],
                     start=(a == 0),
                     stop=(a == 1),
                 )
             return bank
 
-        def put(n, h, engine="fused"):
-            y = ys[len(sums) % len(ys)]
+        def put(n, h, y=None):
+            if y is None:
+                y = ys[len(sums) % len(ys)]
             bank = second_product(n, h)
             places = pages[n % len(pages)][:].indirect(put_list[:, h * LIST_COLS : (h + 1) * LIST_COLS])
             weights = wgo_sb[:, h * HALF : (h + 1) * HALF]
-            if engine == "vector":
-                nc.vector.tensor_tensor(y[:], bank[:], weights, MULT)
-                nc.vector.tensor_copy(places, y[:])
-                return
             nc.scalar.copy(y[:], bank[:])
-            if engine == "gpsimd":
-                yw = yws[len(sums) % len(yws)]
-                nc.gpsimd.tensor_tensor(yw[:], y[:], weights, MULT)
-                nc.vector.tensor_copy(places, yw[:])
-            else:
-                nc.vector.tensor_tensor(places, y[:], weights, MULT)
+            nc.vector.tensor_tensor(places, y[:], weights, MULT)
 
         def put_whole(n):
             y = keep.tile([P, J], F32, name=f"y_whole{n}")
@@ -234,29 +239,39 @@ def tile_list_sigm_scat_kernel(
         quantize_x(1)
         quantize_w("u", 0, 1)
         interleave_w("g", 1, 0, "vector")
-        for c in range(4):
-            hidden(0, c)
-        interleave_w("g", 1, 1, "scalar")
+        hidden(0, 0)
         quantize_w("g", 1, 0)
-        hidden(0, 4)
-        quantize_w("g", 1, 1)
-        for c in range(5, 8):
-            hidden(0, c)
-        interleave_w("u", 1, 1, "scalar")
+        gate(0, 1)
+        gate(0, 2)
+        interleave_w("g", 1, 1, "scalar")
         interleave_w("u", 1, 0, "vector")
-        quantize_w("u", 1, 1)
+        hidden(0, 1)
+        quantize_w("g", 1, 1)
+        hidden(0, 2)
+        gate(0, 3)
+        interleave_w("u", 1, 1, "scalar")
         quantize_w("u", 1, 0)
+        quantize_w("u", 1, 1)
+        hidden(0, 3)
+        hidden(0, 4)
         quantize_h(0, 0)
-        quantize_h(0, 1)
-        for c in range(8):
+        for c in range(4):
             hidden(1, c)
-            if c == 4:
-                quantize_h(1, 0)
-        quantize_h(1, 1)
-        for h in range(2):
-            for n in range(3):
-                put(n, h)
-                if h == 1:
-                    store(n)
+        hidden(0, 5)
+        quantize_h(1, 0)
+        first = [second_product(n, 0) for n in range(2)]
+        hidden(0, 6)
+        hidden(0, 7)
+        for n in range(2):
+            nc.vector.tensor_tensor(ys[n][:], first[n][:], wgo_sb[:, 0:HALF], MULT)
+        for c in range(4, 8):
+            hidden(1, c, "gpsimd")
+        for n in range(2):
+            nc.vector.tensor_copy(pages[n][:].indirect(put_list[:, 0:LIST_COLS]), ys[n][:])
+        quantize_rest()
+        put(2, 0, y=ups[len(lifted) - 1][:].rearrange("p j t -> p (j t)"))
+        for n in range(3):
+            put(n, 1)
+            store(n)
         put_whole(3)
         store(3)

@@ -43,7 +43,7 @@ def tile_list_sigm_scat_kernel(
         }
         wd_codes = keep.tile([P, 2, N], U32, name="wd_codes", align_bytes=64)
         wd_sc = keep.tile([P, 2, N], U8, name="wd_sc", align_bytes=64)
-        pages = [keep.tile([P, T], F32, name=f"page{n}") for n in range(3)]
+        pages = [keep.tile([P, T], F32, name=f"page{n}") for n in range(4)]
         warm = keep.tile([P, 8], F32, name="warm")
         warm_out = keep.tile([P, 8], F32, name="warm_out")
         banks = [psum.tile([P, PASS], F32, name=f"bank{b}") for b in range(8)]
@@ -51,14 +51,14 @@ def tile_list_sigm_scat_kernel(
         ups = [keep.tile([P, P, PACK], F32, name=f"up{b}") for b in range(4)]
         ys = [keep.tile([P, HALF], F32, name=f"y{b}") for b in range(3)]
 
+        weighed = [keep.tile([P, HALF], F32, name=f"weighed{b}") for b in range(3)]
+
         x_rows = xT.rearrange("(p i) t -> p i t", i=PACK)
         w_rows = {"g": wg.rearrange("(p i) r -> p i r", i=PACK), "u": wu.rearrange("(p i) r -> p i r", i=PACK)}
 
         nc.gpsimd.memset(warm[:], 0.0)
         nc.scalar.activation(warm_out[:], warm[:], SIGMOID)
-        for page in pages[:2]:
-            nc.vector.memset(page[:], 0.0)
-        for page in pages[2:]:
+        for page in pages:
             nc.gpsimd.memset(page[:], 0.0)
         nc.vector.memset(wd_sc[:].rearrange("p a n -> p (a n)").bitcast(U32), 0)
 
@@ -150,11 +150,9 @@ def tile_list_sigm_scat_kernel(
                 )
             return bank[:].rearrange("p (t j) -> p j t", t=PACK)
 
-        h_rest = keep.tile([P, 2 * HALF * PACK], BF16, name="h_rest", align_bytes=64)
         h_bf = {(a, 0): keep.tile([P, 4, P, PACK], BF16, name=f"h_bf{a}", align_bytes=64)[:] for a in range(2)}
-        for a in range(2):
-            part = h_rest[:, a * HALF * PACK : (a + 1) * HALF * PACK]
-            h_bf[a, 1] = part.rearrange("p (c j t) -> p c j t", c=4, t=PACK)
+        h_rest = keep.tile([P, 4, P, PACK], BF16, name="h_rest", align_bytes=64)
+        h_bf[0, 1] = h_bf[1, 1] = h_rest[:]
         made = {}
         lifted = []
 
@@ -186,10 +184,6 @@ def tile_list_sigm_scat_kernel(
             codes, scales = quantize(f"h{a}{h}", h_bf[a, h].rearrange("p c j t -> p (c j t)"), HALF)
             h_q[a, h] = codes[:], scales[:]
 
-        def quantize_rest():
-            codes, scales = quantize("h_rest", h_rest[:], J)
-            for a in range(2):
-                h_q[a, 1] = codes[:, a * HALF : (a + 1) * HALF], scales[:, a * HALF : (a + 1) * HALF]
 
         sums = []
 
@@ -217,12 +211,6 @@ def tile_list_sigm_scat_kernel(
             weights = wgo_sb[:, h * HALF : (h + 1) * HALF]
             nc.scalar.copy(y[:], bank[:])
             nc.vector.tensor_tensor(places, y[:], weights, MULT)
-
-        def put_whole(n):
-            y = keep.tile([P, J], F32, name=f"y_whole{n}")
-            for h in range(2):
-                nc.scalar.copy(y[:, h * HALF : (h + 1) * HALF], second_product(n, h)[:])
-            nc.vector.tensor_tensor(pages[n % len(pages)][:].indirect(put_list[:]), y[:], wgo_sb[:], MULT)
 
         def store(n):
             nc.sync.dma_start(out[n * P : (n + 1) * P, :], pages[n % len(pages)][:])
@@ -262,16 +250,20 @@ def tile_list_sigm_scat_kernel(
         first = [second_product(n, 0) for n in range(2)]
         hidden(0, 6)
         hidden(0, 7)
-        for n in range(2):
-            nc.vector.tensor_tensor(ys[n][:], first[n][:], wgo_sb[:, 0:HALF], MULT)
+        nc.vector.tensor_tensor(weighed[0][:], first[0][:], wgo_sb[:, 0:HALF], MULT)
+        quantize_h(0, 1)
+        first.append(second_product(2, 0))
+        for n in range(1, 3):
+            nc.scalar.copy(ys[n][:], first[n][:])
+            for j0 in range(0, HALF, PACK * POOL_PIECE):
+                cols = slice(j0, j0 + PACK * POOL_PIECE)
+                nc.gpsimd.tensor_tensor(weighed[n][:, cols], ys[n][:, cols], wgo_sb[:, cols], MULT)
         for c in range(4, 8):
             hidden(1, c, "gpsimd")
-        for n in range(2):
-            nc.vector.tensor_copy(pages[n][:].indirect(put_list[:, 0:LIST_COLS]), ys[n][:])
-        quantize_rest()
-        put(2, 0, y=ups[len(lifted) - 1][:].rearrange("p j t -> p (j t)"))
         for n in range(3):
+            nc.vector.tensor_copy(pages[n][:].indirect(put_list[:, 0:LIST_COLS]), weighed[n][:])
+        quantize_h(1, 1)
+        put(3, 0, y=ups[len(lifted) - 1][:].rearrange("p j t -> p (j t)"))
+        for n in range(4):
             put(n, 1)
             store(n)
-        put_whole(3)
-        store(3)

@@ -58,9 +58,9 @@ def tile_list_sigm_scat_kernel(
 
         nc.gpsimd.memset(warm[:], 0.0)
         nc.scalar.activation(warm_out[:], warm[:], SIGMOID)
+        nc.gpsimd.memset(wd_sc[:].rearrange("p a n -> p (a n)").bitcast(U32), 0)
         for page in pages:
             nc.gpsimd.memset(page[:], 0.0)
-        nc.vector.memset(wd_sc[:].rearrange("p a n -> p (a n)").bitcast(U32), 0)
 
         nc.sync.dma_start(pick_list[:], offs)
         nc.sync.dma_start(wgt_sb[0][:], wgt[:, 0:HALF])

@@ -20,7 +20,7 @@ PACK = 4
 PASS = P * PACK
 HALF = J // 2
 LIST_COLS = HALF // 16
-POOL_PIECE = 64
+POOL_PIECE = 128
 
 
 def tile_list_sigm_scat_kernel(
@@ -167,7 +167,7 @@ def tile_list_sigm_scat_kernel(
             step = made[a, c]
             sig = gates[step % len(gates)]
             dst = h_bf[a, c // 4][:, c % 4, :, :]
-            up = first_product("u", a, c, banks[3 + step % 3])
+            up = first_product("u", a, c, banks[7 if step == 3 else 3 + (step - (step > 3)) % 3])
             if engine == "vector":
                 nc.vector.tensor_tensor(dst, up, sig[:], MULT)
             else:

@@ -20,7 +20,6 @@ PACK = 4
 PASS = P * PACK
 HALF = J // 2
 LIST_COLS = HALF // 16
-POOL_PIECE = 128
 
 
 def tile_list_sigm_scat_kernel(
@@ -34,7 +33,10 @@ def tile_list_sigm_scat_kernel(
         pick_list = keep.tile([P, J // 16], U16, name="pick_list")
         put_list = keep.tile([P, J // 16], U16, name="put_list")
         planes = [keep.tile([P, T], F32, name=f"plane{i}") for i in range(PACK)]
-        wgt_sb = [keep.tile([P, HALF], F32, name=f"wgt{h}") for h in range(2)]
+        wgt_sb = [keep.tile([P, HALF], F32, name=f"wgt{h}", align_bytes=64) for h in range(2)]
+        wgt_rows = keep.tile([P, 64], F32, name="wgt_rows", align_bytes=64)
+        wgt_turned = keep.tile([P, 64], F32, name="wgt_turned", align_bytes=64)
+        wgt_wide = [keep.tile([P, HALF], F32, name=f"wgt_wide{h}", align_bytes=64) for h in range(2)]
         wgo_sb = keep.tile([P, J], F32, name="wgo_sb")
         w_raw = {
             (w, a): keep.tile([P, PACK, PASS], F32, name=f"raw{w}{a}", tag=f"raw{w}{a}", align_bytes=64)
@@ -47,11 +49,12 @@ def tile_list_sigm_scat_kernel(
         warm = keep.tile([P, 8], F32, name="warm")
         warm_out = keep.tile([P, 8], F32, name="warm_out")
         banks = [psum.tile([P, PASS], F32, name=f"bank{b}") for b in range(8)]
-        gates = [keep.tile([P, P, PACK], F32, name=f"gate{b}") for b in range(6)]
-        ups = [keep.tile([P, P, PACK], F32, name=f"up{b}") for b in range(4)]
-        ys = [keep.tile([P, HALF], F32, name=f"y{b}") for b in range(3)]
-
-        weighed = [keep.tile([P, HALF], F32, name=f"weighed{b}") for b in range(3)]
+        strips = {b: keep.tile([P, PASS], F32, name=f"strip{b}") for b in (0, 2, 3, 4, 5, 6, 7, 8, 9)}
+        gate_ring = [strips[b] for b in (0, 2, 5, 6, 7)]
+        ups = []
+        ys = [keep.tile([P, 3 * P], F32, name=f"y{b}") for b in range(3)]
+        weighed = [keep.tile([P, PASS], F32, name=f"weighed{b}") for b in range(2)]
+        h_bf = keep.tile([P, 6 * PASS], BF16, name="h_bf", align_bytes=64)
 
         x_rows = xT.rearrange("(p i) t -> p i t", i=PACK)
         w_rows = {"g": wg.rearrange("(p i) r -> p i r", i=PACK), "u": wu.rearrange("(p i) r -> p i r", i=PACK)}
@@ -62,34 +65,39 @@ def tile_list_sigm_scat_kernel(
         for page in pages:
             nc.gpsimd.memset(page[:], 0.0)
 
+        nc.sync.dma_start(wgt_rows[:], wgt.rearrange("(g s) (c e) -> g s c e", s=16, e=64)[:, 0, :, :])
         nc.sync.dma_start(pick_list[:], offs)
-        nc.sync.dma_start(wgt_sb[0][:], wgt[:, 0:HALF])
-        nc.sync.dma_start(planes[0][:], x_rows[:, 0, :])
-        nc.sync.dma_start(wgt_sb[1][:], wgt[:, HALF:J])
-        for i in range(1, PACK):
+        for i in range(PACK):
             nc.sync.dma_start(planes[i][:], x_rows[:, i, :])
         for a in range(2):
             for w in "gu":
                 nc.sync.dma_start(w_raw[w, a][:], w_rows[w][:, :, a * PASS : (a + 1) * PASS])
-        nc.sync.dma_start(wd_codes[:].bitcast(I32), wd_words.rearrange("a p n t -> p a (n t)").bitcast(I32))
-        nc.sync.dma_start(put_list[:], offs2)
-        nc.sync.dma_start(wgo_sb[:], wgo)
         sc_rows = wd_scales.bitcast(I32).rearrange("a q n -> q a n")
         for quad in range(4):
             nc.sync.dma_start(
                 wd_sc[32 * quad : 32 * quad + 4, :, :].bitcast(I32), sc_rows[4 * quad : 4 * quad + 4, :, :]
             )
+        nc.sync.dma_start(wd_codes[:].bitcast(I32), wd_words.rearrange("a p n t -> p a (n t)").bitcast(I32))
+        nc.sync.dma_start(put_list[:], offs2)
+        nc.sync.dma_start(wgo_sb[:], wgo)
+
+        for u in range(2):
+            nc.vector.transpose(wgt_turned[:, 32 * u : 32 * u + 32], wgt_rows[:, 32 * u : 32 * u + 32])
+        by_block = wgt_turned[:].rearrange("p (u g c) -> p c u g", u=2, g=2)
+        for h in range(2):
+            nc.scalar.copy(
+                wgt_wide[h][:].rearrange("p (c u g i) -> p c u g i", u=2, g=2, i=16),
+                by_block[:, 8 * h : 8 * h + 8, :, :].unsqueeze(4).to_broadcast([P, 8, 2, 2, 16]),
+            )
+            nc.vector.transpose(wgt_sb[h][:], wgt_wide[h][:])
 
         picked = {(h, pr): keep.tile([P, 2, HALF], F32, name=f"picked{h}{pr}") for h in range(2) for pr in range(2)}
         x_bf = [keep.tile([P, HALF, PACK], BF16, name=f"x_bf{h}", align_bytes=64) for h in range(2)]
 
-        def weave_x(h, pr, engine):
+        def weave_x(h, pr):
             dst = x_bf[h][:, :, 2 * pr : 2 * pr + 2].rearrange("p (c f) e -> p c e f", f=4)
             src = picked[h, pr][:].rearrange("p e (c f) -> p c e f", f=4)
-            if engine == "vector":
-                nc.vector.tensor_copy(dst, src)
-            else:
-                nc.scalar.copy(dst, src)
+            nc.scalar.copy(dst, src)
 
         for pr in range(2):
             for e in range(2):
@@ -101,8 +109,7 @@ def tile_list_sigm_scat_kernel(
                         MULT,
                     )
             for h in range(2):
-                if (pr, h) != (1, 1):
-                    weave_x(h, pr, "scalar")
+                weave_x(h, pr)
 
         def quantize(name, src, words, tag=None):
             codes = keep.tile([P, words], U32, name=f"codes_{name}", tag=tag or f"codes_{name}", align_bytes=64)
@@ -110,32 +117,30 @@ def tile_list_sigm_scat_kernel(
             nc.vector.quantize_mx(out=codes[:].bitcast(FP8X4), scales=scales[:], in_=src)
             return codes, scales
 
-        w_bf = {}
+        w_bf = {("u", 1, 1): h_bf[:, 0 : 2 * PASS], ("u", 1, 0): h_bf[:, 2 * PASS : 4 * PASS]}
 
-        def interleave_w(w, a, tp, engine):
-            tile = keep.tile([P, 2, P, PACK], BF16, name=f"w_bf{w}{a}{tp}", align_bytes=64)
-            dst = tile[:].rearrange("p t m i -> p m i t")
-            src = w_raw[w, a][:].rearrange("p i (m t) -> p m i t", t=PACK)[:, :, :, 2 * tp : 2 * tp + 2]
+        def interleave_w(w, a, tp, engine, m=slice(0, P)):
+            if (w, a, tp) not in w_bf:
+                w_bf[w, a, tp] = keep.tile([P, 2 * PASS], BF16, name=f"w_bf{w}{a}{tp}", align_bytes=64)[:]
+            dst = w_bf[w, a, tp].rearrange("p (t m i) -> p m i t", t=2, i=PACK)[:, m, :, :]
+            src = w_raw[w, a][:].rearrange("p i (m t) -> p m i t", t=PACK)[:, m, :, 2 * tp : 2 * tp + 2]
             if engine == "vector":
                 nc.vector.tensor_copy(dst, src)
-            elif engine == "gpsimd":
-                nc.gpsimd.tensor_copy(dst, src)
             else:
                 nc.scalar.copy(dst, src)
-            w_bf[w, a, tp] = tile
 
         w_q = {}
 
         def quantize_w(w, a, tp):
-            w_q[w, a, tp] = quantize(f"{w}{a}{tp}", w_bf[w, a, tp][:].rearrange("p t m i -> p (t m i)"), 2 * P)
+            w_q[w, a, tp] = quantize(f"{w}{a}{tp}", w_bf[w, a, tp], 2 * P)
 
         x_q = {}
 
         def quantize_x(h, tag=None):
             x_q[h] = quantize(f"x{h}", x_bf[h][:].rearrange("p j i -> p (j i)"), HALF, tag)
 
-        def first_product(w, a, c, bank):
-            cols = slice((c % 4) * P, (c % 4 + 1) * P)
+        def first_product(w, a, s, bank):
+            cols = slice((s % 4) * P, (s % 4 + 1) * P)
             for t in range(PACK):
                 codes, scales = w_q[w, a, t // 2]
                 m = slice((t % 2) * P, (t % 2 + 1) * P)
@@ -143,79 +148,91 @@ def tile_list_sigm_scat_kernel(
                     out=bank[:, t * P : (t + 1) * P],
                     lhsT=codes[:, m].bitcast(FP8X4),
                     lhsT_scale=scales[:, m],
-                    rhs=x_q[c // 4][0][:, cols].bitcast(FP8X4),
-                    rhs_scale=x_q[c // 4][1][:, cols],
+                    rhs=x_q[s // 4][0][:, cols].bitcast(FP8X4),
+                    rhs_scale=x_q[s // 4][1][:, cols],
                     start=True,
                     stop=True,
                 )
             return bank[:].rearrange("p (t j) -> p j t", t=PACK)
 
-        h_bf = {(a, 0): keep.tile([P, 4, P, PACK], BF16, name=f"h_bf{a}", align_bytes=64)[:] for a in range(2)}
-        h_rest = keep.tile([P, 4, P, PACK], BF16, name="h_rest", align_bytes=64)
-        h_bf[0, 1] = h_bf[1, 1] = h_rest[:]
+        def woven(ap):
+            return ap.rearrange("p (j t) -> p j t", t=PACK)
+
         made = {}
+        multiplied = []
         lifted = []
 
-        def gate(a, c):
-            step = len(made)
-            made[a, c] = step
-            nc.scalar.activation(gates[step % len(gates)][:], first_product("g", a, c, banks[step % 3]), SIGMOID)
+        ringed = []
 
-        def hidden(a, c, engine="vector"):
-            if (a, c) not in made:
-                gate(a, c)
-            step = made[a, c]
-            sig = gates[step % len(gates)]
-            dst = h_bf[a, c // 4][:, c % 4, :, :]
-            up = first_product("u", a, c, banks[7 if step == 3 else 3 + (step - (step > 3)) % 3])
+        def gate(a, s, sig=None):
+            if sig is None:
+                sig = gate_ring[len(ringed) % len(gate_ring)]
+                ringed.append(s)
+            bank = banks[len(made) % 2]
+            made[a, s] = sig
+            nc.scalar.activation(woven(sig[:]), first_product("g", a, s, bank), SIGMOID)
+
+        def hidden(a, s, slot, engine):
+            if (a, s) not in made:
+                gate(a, s)
+            sig = made[a, s]
+            dst = h_bf[:, slot * PASS : (slot + 1) * PASS]
+            up = first_product("u", a, s, banks[2 + len(multiplied) % 4])
+            multiplied.append(s)
             if engine == "vector":
-                nc.vector.tensor_tensor(dst, up, sig[:], MULT)
+                nc.vector.tensor_tensor(woven(dst), up, woven(sig[:]), MULT)
             else:
                 up_sb = ups[len(lifted) % len(ups)]
-                lifted.append(c)
-                nc.scalar.copy(up_sb[:], up)
-                for j0 in range(0, P, POOL_PIECE):
-                    cols = slice(j0, j0 + POOL_PIECE)
-                    nc.gpsimd.tensor_tensor(dst[:, cols, :], up_sb[:, cols, :], sig[:, cols, :], MULT)
+                lifted.append(s)
+                nc.scalar.copy(woven(up_sb[:]), up)
+                nc.gpsimd.tensor_tensor(dst, up_sb[:], sig[:], MULT)
 
         h_q = {}
 
-        def quantize_h(a, h):
-            codes, scales = quantize(f"h{a}{h}", h_bf[a, h].rearrange("p c j t -> p (c j t)"), HALF)
-            h_q[a, h] = codes[:], scales[:]
+        def quantize_h(slot, strips):
+            count = len(strips)
+            codes, scales = quantize(f"h{strips[0][0]}{strips[0][1]}", h_bf[:, slot * PASS : (slot + count) * PASS], count * P)
+            for k, strip in enumerate(strips):
+                h_q[strip] = codes, scales, k * P
 
-
-        sums = []
-
-        def second_product(n, h):
-            bank = banks[6 + len(sums) % 2]
-            sums.append(n)
+        def down_pass(bank, col, n, a, s, count, start, stop):
+            codes, scales, first = h_q[a, s]
             m = slice(n * P, (n + 1) * P)
-            for a in range(2):
-                nc.tensor.matmul_mx(
-                    out=bank[:],
-                    lhsT=wd_codes[:, a, m].bitcast(FP8X4),
-                    lhsT_scale=wd_sc[:, a, m],
-                    rhs=h_q[a, h][0].bitcast(FP8X4),
-                    rhs_scale=h_q[a, h][1],
-                    start=(a == 0),
-                    stop=(a == 1),
-                )
-            return bank
+            cols = slice(first, first + count * P)
+            nc.tensor.matmul_mx(
+                out=bank[:, col : col + count * P],
+                lhsT=wd_codes[:, a, m].bitcast(FP8X4),
+                lhsT_scale=wd_sc[:, a, m],
+                rhs=codes[:, cols].bitcast(FP8X4),
+                rhs_scale=scales[:, cols],
+                start=start,
+                stop=stop,
+            )
 
-        def put(n, h, y=None):
-            if y is None:
-                y = ys[len(sums) % len(ys)]
-            bank = second_product(n, h)
-            places = pages[n % len(pages)][:].indirect(put_list[:, h * LIST_COLS : (h + 1) * LIST_COLS])
-            weights = wgo_sb[:, h * HALF : (h + 1) * HALF]
-            nc.scalar.copy(y[:], bank[:])
-            nc.vector.tensor_tensor(places, y[:], weights, MULT)
+        def down(bank, rows, s, count, a):
+            for k, n in enumerate(rows):
+                down_pass(bank, k * count * P, n, a, s, count, a == 0 and k == 0, a == 1 and k == len(rows) - 1)
 
-        def store(n):
-            nc.sync.dma_start(out[n * P : (n + 1) * P, :], pages[n % len(pages)][:])
+        def places(n, s, count):
+            return pages[n][:].indirect(put_list[:, s * 8 : (s + count) * 8])
 
-        weave_x(1, 1, "scalar")
+        def weigh(dst, place, bank, first, blocks, s, count):
+            width = count * P
+            nc.vector.tensor_tensor(
+                dst[:, place * width : (place + blocks) * width].rearrange("p (n j) -> p n j", n=blocks),
+                bank[:, first * width : (first + blocks) * width].rearrange("p (n j) -> p n j", n=blocks),
+                wgo_sb[:, s * P : s * P + width].unsqueeze(1).to_broadcast([P, blocks, width]),
+                MULT,
+            )
+
+        def put_weighed(src, rows, s, count):
+            width = count * P
+            for k, n in enumerate(rows):
+                nc.vector.tensor_copy(places(n, s, count), src[:, k * width : (k + 1) * width])
+
+        def put_fused(y, n, s, count):
+            nc.vector.tensor_tensor(places(n, s, count), y, wgo_sb[:, s * P : (s + count) * P], MULT)
+
         interleave_w("g", 0, 0, "vector")
         interleave_w("g", 0, 1, "vector")
         quantize_x(0, "rawg0")
@@ -226,44 +243,82 @@ def tile_list_sigm_scat_kernel(
         quantize_w("u", 0, 0)
         quantize_x(1)
         quantize_w("u", 0, 1)
-        interleave_w("g", 1, 0, "vector")
-        hidden(0, 0)
-        quantize_w("g", 1, 0)
-        gate(0, 1)
-        gate(0, 2)
+        gate(0, 0)
         interleave_w("g", 1, 1, "scalar")
-        interleave_w("u", 1, 0, "vector")
-        hidden(0, 1)
+        interleave_w("g", 1, 0, "vector")
+        late_gate = keep.tile([P, PASS], F32, name="late_gate", tag="rawg1", align_bytes=64)
+        ups.extend([late_gate, strips[3], strips[4]])
+        gate(0, 1, late_gate)
+        quantize_w("g", 1, 0)
         quantize_w("g", 1, 1)
-        hidden(0, 2)
-        gate(0, 3)
-        interleave_w("u", 1, 1, "scalar")
-        quantize_w("u", 1, 0)
+        interleave_w("u", 1, 1, "scalar", slice(P // 2, P))
+        interleave_w("u", 1, 1, "vector", slice(0, P // 2))
+        interleave_w("u", 1, 0, "vector")
         quantize_w("u", 1, 1)
-        hidden(0, 3)
-        hidden(0, 4)
-        quantize_h(0, 0)
-        for c in range(4):
-            hidden(1, c)
-        hidden(0, 5)
-        quantize_h(1, 0)
-        first = [second_product(n, 0) for n in range(2)]
-        hidden(0, 6)
-        hidden(0, 7)
-        nc.vector.tensor_tensor(weighed[0][:], first[0][:], wgo_sb[:, 0:HALF], MULT)
-        quantize_h(0, 1)
-        first.append(second_product(2, 0))
-        for n in range(1, 3):
-            nc.scalar.copy(ys[n][:], first[n][:])
-            for j0 in range(0, HALF, PACK * POOL_PIECE):
-                cols = slice(j0, j0 + PACK * POOL_PIECE)
-                nc.gpsimd.tensor_tensor(weighed[n][:, cols], ys[n][:, cols], wgo_sb[:, cols], MULT)
-        for c in range(4, 8):
-            hidden(1, c, "gpsimd")
-        for n in range(3):
-            nc.vector.tensor_copy(pages[n][:].indirect(put_list[:, 0:LIST_COLS]), weighed[n][:])
-        quantize_h(1, 1)
-        put(3, 0, y=ups[len(lifted) - 1][:].rearrange("p j t -> p (j t)"))
+        quantize_w("u", 1, 0)
+        gate(1, 0)
+        gate(1, 1, strips[3])
+        gate(0, 2, strips[4])
+        hidden(0, 0, 0, "vector")
+        hidden(0, 1, 2, "vector")
+        hidden(1, 0, 1, "vector")
+        quantize_h(0, [(0, 0)])
+        down(banks[6], range(4), 0, 1, 0)
+        hidden(1, 1, 3, "vector")
+        quantize_h(1, [(1, 0)])
+        down(banks[6], range(4), 0, 1, 1)
+        hidden(0, 2, 0, "vector")
+        quantize_h(2, [(0, 1), (1, 1)])
+        for a in range(2):
+            down(banks[7], range(4), 1, 1, a)
+
+        weigh(weighed[0], 0, banks[6], 0, 1, 0, 1)
+        weigh(weighed[0], 1, banks[6], 1, 3, 0, 1)
+        put_weighed(weighed[0], range(4), 0, 1)
+        weigh(weighed[1], 0, banks[7], 0, 1, 1, 1)
+        put_weighed(weighed[1], range(1), 1, 1)
+        for a, s, slot in ((1, 2, 2), (1, 3, 3)):
+            hidden(a, s, slot, "gpsimd")
+        gate(0, 3, strips[8])
+        hidden(0, 3, 1, "gpsimd")
+        hidden(0, 5, 4, "gpsimd")
+
+        weigh(strips[8], 0, banks[7], 1, 3, 1, 1)
+        quantize_h(0, [(0, 2), (0, 3), (1, 2), (1, 3)])
+        for a in range(2):
+            down(banks[6], (0, 1), 2, 2, a)
+        put_weighed(strips[8], (1, 2, 3), 1, 1)
+        for a in range(2):
+            down(banks[7], (2, 3), 2, 2, a)
+        for k in range(2):
+            weigh(weighed[0], k, banks[6], k, 1, 2, 2)
+        put_weighed(weighed[0], (0, 1), 2, 2)
+        for a, s, slot in ((0, 6, 2), (0, 7, 3), (0, 4, 0), (1, 5, 5)):
+            hidden(a, s, slot, "gpsimd")
+        gate(1, 4, strips[9])
+        hidden(1, 4, 1, "gpsimd")
+
+        quantize_h(2, [(0, 6), (0, 7), (0, 5), (1, 5)])
+        weigh(strips[9], 0, banks[7], 0, 2, 2, 2)
+        quantize_h(0, [(0, 4), (1, 4)])
+        for a in range(2):
+            down(banks[6], range(4), 4, 1, a)
+        put_weighed(strips[9], (2, 3), 2, 2)
+        for s in range(6, 8):
+            hidden(1, s, s - 6, "gpsimd")
+        held = ups[(len(lifted) - 1) % len(ups)]
+
+        quantize_h(0, [(1, 6), (1, 7)])
+        nc.scalar.copy(held[:, 0:P], banks[6][:, 0:P])
+        nc.scalar.copy(held[:, P:PASS], banks[6][:, P:PASS])
         for n in range(4):
-            put(n, 1)
-            store(n)
+            put_fused(held[:, n * P : (n + 1) * P], n, 4, 1)
+        for n in range(4):
+            bank = banks[(7 + n) % 8]
+            for a in range(2):
+                down_pass(bank, 0, n, a, 5, 1, a == 0, False)
+                down_pass(bank, P, n, a, 6, 2, False, a == 1)
+            y = ys[n % len(ys)]
+            nc.scalar.copy(y[:], bank[:, 0 : 3 * P])
+            put_fused(y[:], n, 5, 3)
+            nc.sync.dma_start(out[n * P : (n + 1) * P, :], pages[n][:])

@@ -54,7 +54,7 @@ def tile_list_sigm_scat_kernel(
         ups = []
         ys = [keep.tile([P, 3 * P], F32, name=f"y{b}") for b in range(3)]
         weighed = [keep.tile([P, PASS], F32, name=f"weighed{b}") for b in range(2)]
-        h_bf = keep.tile([P, 6 * PASS], BF16, name="h_bf", align_bytes=64)
+        h_bf = keep.tile([P, 8 * PASS], BF16, name="h_bf", align_bytes=64)
 
         x_rows = xT.rearrange("(p i) t -> p i t", i=PACK)
         w_rows = {"g": wg.rearrange("(p i) r -> p i r", i=PACK), "u": wu.rearrange("(p i) r -> p i r", i=PACK)}
@@ -117,7 +117,11 @@ def tile_list_sigm_scat_kernel(
             nc.vector.quantize_mx(out=codes[:].bitcast(FP8X4), scales=scales[:], in_=src)
             return codes, scales
 
-        w_bf = {("u", 1, 1): h_bf[:, 0 : 2 * PASS], ("u", 1, 0): h_bf[:, 2 * PASS : 4 * PASS]}
+        w_bf = {
+            ("u", 1, 1): h_bf[:, 2 * PASS : 4 * PASS],
+            ("u", 1, 0): h_bf[:, 4 * PASS : 6 * PASS],
+            ("g", 1, 0): h_bf[:, 6 * PASS : 8 * PASS],
+        }
 
         def interleave_w(w, a, tp, engine, m=slice(0, P)):
             if (w, a, tp) not in w_bf:
@@ -163,22 +167,27 @@ def tile_list_sigm_scat_kernel(
         lifted = []
 
         ringed = []
+        opened = []
 
-        def gate(a, s, sig=None):
+        def gate(a, s, sig=None, bank=None):
             if sig is None:
                 sig = gate_ring[len(ringed) % len(gate_ring)]
                 ringed.append(s)
-            bank = banks[len(made) % 2]
+            if bank is None:
+                bank = banks[len(opened) % 2]
+                opened.append(s)
             made[a, s] = sig
             nc.scalar.activation(woven(sig[:]), first_product("g", a, s, bank), SIGMOID)
 
-        def hidden(a, s, slot, engine):
+        def hidden(a, s, slot, engine, bank=None):
             if (a, s) not in made:
                 gate(a, s)
             sig = made[a, s]
             dst = h_bf[:, slot * PASS : (slot + 1) * PASS]
-            up = first_product("u", a, s, banks[2 + len(multiplied) % 4])
-            multiplied.append(s)
+            if bank is None:
+                bank = banks[2 + len(multiplied) % 3]
+                multiplied.append(s)
+            up = first_product("u", a, s, bank)
             if engine == "vector":
                 nc.vector.tensor_tensor(woven(dst), up, woven(sig[:]), MULT)
             else:
@@ -251,73 +260,83 @@ def tile_list_sigm_scat_kernel(
         gate(0, 1, late_gate)
         quantize_w("g", 1, 0)
         quantize_w("g", 1, 1)
+        hidden(0, 0, 6, "vector")
         interleave_w("u", 1, 1, "scalar", slice(P // 2, P))
         interleave_w("u", 1, 1, "vector", slice(0, P // 2))
         interleave_w("u", 1, 0, "vector")
         quantize_w("u", 1, 1)
         quantize_w("u", 1, 0)
-        gate(1, 0)
-        gate(1, 1, strips[3])
-        gate(0, 2, strips[4])
-        hidden(0, 0, 0, "vector")
-        hidden(0, 1, 2, "vector")
-        hidden(1, 0, 1, "vector")
-        quantize_h(0, [(0, 0)])
-        down(banks[6], range(4), 0, 1, 0)
-        hidden(1, 1, 3, "vector")
-        quantize_h(1, [(1, 0)])
-        down(banks[6], range(4), 0, 1, 1)
-        hidden(0, 2, 0, "vector")
-        quantize_h(2, [(0, 1), (1, 1)])
+        gate(1, 0, None, banks[0])
+        gate(0, 3, None, banks[1])
+        gate(1, 1, strips[3], banks[0])
+        gate(0, 2, strips[4], banks[1])
+        hidden(0, 1, 4, "vector", banks[6])
+        hidden(0, 3, 3, "vector")
+        hidden(1, 0, 7, "vector")
+        quantize_h(6, [(0, 0)])
+        down(banks[6], range(3), 0, 1, 0)
+        hidden(1, 1, 5, "vector", banks[5])
+        quantize_h(7, [(1, 0)])
+        down(banks[6], range(3), 0, 1, 1)
+        hidden(0, 2, 2, "vector")
         for a in range(2):
-            down(banks[7], range(4), 1, 1, a)
+            down_pass(banks[7], 0, 3, a, 0, 1, a == 0, False)
+        quantize_h(4, [(0, 1), (1, 1)])
+        for a in range(2):
+            for n in range(2):
+                down_pass(banks[7], (1 + n) * P, n, a, 1, 1, False, a == 1 and n == 1)
+        for a in range(2):
+            down(banks[5], (2, 3), 1, 1, a)
 
         weigh(weighed[0], 0, banks[6], 0, 1, 0, 1)
-        weigh(weighed[0], 1, banks[6], 1, 3, 0, 1)
-        put_weighed(weighed[0], range(4), 0, 1)
-        weigh(weighed[1], 0, banks[7], 0, 1, 1, 1)
-        put_weighed(weighed[1], range(1), 1, 1)
-        for a, s, slot in ((1, 2, 2), (1, 3, 3)):
-            hidden(a, s, slot, "gpsimd")
-        gate(0, 3, strips[8])
-        hidden(0, 3, 1, "gpsimd")
+        weigh(weighed[0], 1, banks[6], 1, 2, 0, 1)
+        put_weighed(weighed[0], range(3), 0, 1)
+        weigh(weighed[0], 3, banks[7], 0, 1, 0, 1)
+        weigh(weighed[1], 0, banks[7], 1, 2, 1, 1)
+        put_weighed(weighed[0][:, 3 * P : PASS], (3,), 0, 1)
+        put_weighed(weighed[1], range(2), 1, 1)
         hidden(0, 5, 4, "gpsimd")
+        hidden(0, 6, 5, "gpsimd")
+        hidden(1, 2, 0, "gpsimd")
+        gate(1, 3, strips[8])
+        hidden(1, 3, 1, "gpsimd")
 
-        weigh(strips[8], 0, banks[7], 1, 3, 1, 1)
-        quantize_h(0, [(0, 2), (0, 3), (1, 2), (1, 3)])
+        weigh(strips[8], 0, banks[5], 0, 2, 1, 1)
+        quantize_h(0, [(1, 2), (1, 3), (0, 2), (0, 3)])
         for a in range(2):
             down(banks[6], (0, 1), 2, 2, a)
-        put_weighed(strips[8], (1, 2, 3), 1, 1)
+        put_weighed(strips[8], (2, 3), 1, 1)
         for a in range(2):
             down(banks[7], (2, 3), 2, 2, a)
         for k in range(2):
             weigh(weighed[0], k, banks[6], k, 1, 2, 2)
         put_weighed(weighed[0], (0, 1), 2, 2)
-        for a, s, slot in ((0, 6, 2), (0, 7, 3), (0, 4, 0), (1, 5, 5)):
+        for a, s, slot in ((0, 7, 2), (1, 5, 3), (0, 4, 0)):
             hidden(a, s, slot, "gpsimd")
         gate(1, 4, strips[9])
         hidden(1, 4, 1, "gpsimd")
 
-        quantize_h(2, [(0, 6), (0, 7), (0, 5), (1, 5)])
+        quantize_h(2, [(0, 7), (1, 5), (0, 5), (0, 6)])
         weigh(strips[9], 0, banks[7], 0, 2, 2, 2)
         quantize_h(0, [(0, 4), (1, 4)])
         for a in range(2):
-            down(banks[6], range(4), 4, 1, a)
+            down(banks[5], range(4), 4, 1, a)
         put_weighed(strips[9], (2, 3), 2, 2)
         for s in range(6, 8):
             hidden(1, s, s - 6, "gpsimd")
         held = ups[(len(lifted) - 1) % len(ups)]
 
         quantize_h(0, [(1, 6), (1, 7)])
-        nc.scalar.copy(held[:, 0:P], banks[6][:, 0:P])
-        nc.scalar.copy(held[:, P:PASS], banks[6][:, P:PASS])
+        nc.scalar.copy(held[:, 0:P], banks[5][:, 0:P])
+        nc.scalar.copy(held[:, P:PASS], banks[5][:, P:PASS])
         for n in range(4):
             put_fused(held[:, n * P : (n + 1) * P], n, 4, 1)
         for n in range(4):
-            bank = banks[(7 + n) % 8]
-            for a in range(2):
-                down_pass(bank, 0, n, a, 5, 1, a == 0, False)
-                down_pass(bank, P, n, a, 6, 2, False, a == 1)
+            bank = banks[(6 + n) % 8]
+            down_pass(bank, 0, n, 0, 5, 2, True, False)
+            down_pass(bank, 2 * P, n, 0, 7, 1, False, False)
+            down_pass(bank, 0, n, 1, 5, 1, False, False)
+            down_pass(bank, P, n, 1, 6, 2, False, True)
             y = ys[n % len(ys)]
             nc.scalar.copy(y[:], bank[:, 0 : 3 * P])
             put_fused(y[:], n, 5, 3)

@@ -36,7 +36,7 @@ def tile_list_sigm_scat_kernel(
         wgt_sb = [keep.tile([P, HALF], F32, name=f"wgt{h}", align_bytes=64) for h in range(2)]
         wgt_rows = keep.tile([P, 64], F32, name="wgt_rows", align_bytes=64)
         wgt_turned = keep.tile([P, 64], F32, name="wgt_turned", align_bytes=64)
-        wgt_wide = [keep.tile([P, HALF], F32, name=f"wgt_wide{h}", align_bytes=64) for h in range(2)]
+        wgt_wide = [keep.tile([P, J // 4], F32, name=f"wgt_wide{q}", align_bytes=64) for q in range(4)]
         wgo_sb = keep.tile([P, J], F32, name="wgo_sb")
         w_raw = {
             (w, a): keep.tile([P, PACK, PASS], F32, name=f"raw{w}{a}", tag=f"raw{w}{a}", align_bytes=64)
@@ -49,10 +49,9 @@ def tile_list_sigm_scat_kernel(
         warm = keep.tile([P, 8], F32, name="warm")
         warm_out = keep.tile([P, 8], F32, name="warm_out")
         banks = [psum.tile([P, PASS], F32, name=f"bank{b}") for b in range(8)]
-        strips = {b: keep.tile([P, PASS], F32, name=f"strip{b}") for b in (0, 2, 3, 4, 5, 6, 7, 8, 9)}
-        gate_ring = [strips[b] for b in (0, 2, 5, 6, 7)]
-        ups = []
-        ys = [keep.tile([P, 3 * P], F32, name=f"y{b}") for b in range(3)]
+        gates = [keep.tile([P, 3 * PASS], F32, name=f"gates{b}") for b in range(2)]
+        ups = [keep.tile([P, 3 * PASS], F32, name=f"ups{b}") for b in range(2)]
+        ys = [keep.tile([P, PASS], F32, name=f"y{b}") for b in range(3)]
         weighed = [keep.tile([P, PASS], F32, name=f"weighed{b}") for b in range(2)]
         h_bf = keep.tile([P, 8 * PASS], BF16, name="h_bf", align_bytes=64)
 
@@ -84,12 +83,12 @@ def tile_list_sigm_scat_kernel(
         for u in range(2):
             nc.vector.transpose(wgt_turned[:, 32 * u : 32 * u + 32], wgt_rows[:, 32 * u : 32 * u + 32])
         by_block = wgt_turned[:].rearrange("p (u g c) -> p c u g", u=2, g=2)
-        for h in range(2):
+        for q in range(4):
             nc.scalar.copy(
-                wgt_wide[h][:].rearrange("p (c u g i) -> p c u g i", u=2, g=2, i=16),
-                by_block[:, 8 * h : 8 * h + 8, :, :].unsqueeze(4).to_broadcast([P, 8, 2, 2, 16]),
+                wgt_wide[q][:].rearrange("p (c u g i) -> p c u g i", u=2, g=2, i=16),
+                by_block[:, 4 * q : 4 * q + 4, :, :].unsqueeze(4).to_broadcast([P, 4, 2, 2, 16]),
             )
-            nc.vector.transpose(wgt_sb[h][:], wgt_wide[h][:])
+            nc.vector.transpose(wgt_sb[q // 2][:, q % 2 * 256 : (q % 2 + 1) * 256], wgt_wide[q][:])
 
         picked = {(h, pr): keep.tile([P, 2, HALF], F32, name=f"picked{h}{pr}") for h in range(2) for pr in range(2)}
         x_bf = [keep.tile([P, HALF, PACK], BF16, name=f"x_bf{h}", align_bytes=64) for h in range(2)]
@@ -162,39 +161,32 @@ def tile_list_sigm_scat_kernel(
         def woven(ap):
             return ap.rearrange("p (j t) -> p j t", t=PACK)
 
+        def part(tile, first, count=1):
+            return tile[:, first * PASS : (first + count) * PASS]
+
         made = {}
-        multiplied = []
+
+        def gate(a, s, sig, bank):
+            made[a, s] = sig
+            nc.scalar.activation(woven(sig), first_product("g", a, s, bank), SIGMOID)
+
+        def hidden_on_vector(a, s, slot, bank):
+            up = first_product("u", a, s, bank)
+            nc.vector.tensor_tensor(woven(part(h_bf, slot)), up, woven(made[a, s]), MULT)
+
         lifted = []
 
-        ringed = []
-        opened = []
+        def lift(a, s, dst, bank):
+            nc.scalar.copy(woven(dst), first_product("u", a, s, bank))
 
-        def gate(a, s, sig=None, bank=None):
-            if sig is None:
-                sig = gate_ring[len(ringed) % len(gate_ring)]
-                ringed.append(s)
-            if bank is None:
-                bank = banks[len(opened) % 2]
-                opened.append(s)
-            made[a, s] = sig
-            nc.scalar.activation(woven(sig[:]), first_product("g", a, s, bank), SIGMOID)
-
-        def hidden(a, s, slot, engine, bank=None):
-            if (a, s) not in made:
-                gate(a, s)
-            sig = made[a, s]
-            dst = h_bf[:, slot * PASS : (slot + 1) * PASS]
-            if bank is None:
-                bank = banks[2 + len(multiplied) % 3]
-                multiplied.append(s)
-            up = first_product("u", a, s, bank)
-            if engine == "vector":
-                nc.vector.tensor_tensor(woven(dst), up, woven(sig[:]), MULT)
-            else:
-                up_sb = ups[len(lifted) % len(ups)]
-                lifted.append(s)
-                nc.scalar.copy(woven(up_sb[:]), up)
-                nc.gpsimd.tensor_tensor(dst, up_sb[:], sig[:], MULT)
+        def hidden_on_gpsimd(group, slot, side, ready=False):
+            for k, (a, s) in enumerate(group):
+                if not ready:
+                    gate(a, s, part(gates[side], k), banks[len(lifted) % 2])
+                    lift(a, s, part(ups[side], k), banks[2 + (len(lifted) + 2) % 3])
+                    lifted.append(s)
+            count = len(group)
+            nc.gpsimd.tensor_tensor(part(h_bf, slot, count), part(ups[side], 0, count), part(gates[side], 0, count), MULT)
 
         h_q = {}
 
@@ -234,6 +226,15 @@ def tile_list_sigm_scat_kernel(
                 MULT,
             )
 
+        def weigh_on_gpsimd(dst, y, blocks, s, count):
+            width = count * P
+            nc.gpsimd.tensor_tensor(
+                dst.rearrange("p (n j) -> p n j", n=blocks),
+                y.rearrange("p (n j) -> p n j", n=blocks),
+                wgo_sb[:, s * P : s * P + width].unsqueeze(1).to_broadcast([P, blocks, width]),
+                MULT,
+            )
+
         def put_weighed(src, rows, s, count):
             width = count * P
             for k, n in enumerate(rows):
@@ -252,41 +253,42 @@ def tile_list_sigm_scat_kernel(
         quantize_w("u", 0, 0)
         quantize_x(1)
         quantize_w("u", 0, 1)
-        gate(0, 0)
+        gate(0, 0, part(gates[0], 2), banks[0])
         interleave_w("g", 1, 1, "scalar")
         interleave_w("g", 1, 0, "vector")
         late_gate = keep.tile([P, PASS], F32, name="late_gate", tag="rawg1", align_bytes=64)
-        ups.extend([late_gate, strips[3], strips[4]])
-        gate(0, 1, late_gate)
+        gate(0, 1, late_gate[:], banks[1])
         quantize_w("g", 1, 0)
         quantize_w("g", 1, 1)
-        hidden(0, 0, 6, "vector")
+        hidden_on_vector(0, 0, 6, banks[2])
         interleave_w("u", 1, 1, "scalar", slice(P // 2, P))
         interleave_w("u", 1, 1, "vector", slice(0, P // 2))
         interleave_w("u", 1, 0, "vector")
         quantize_w("u", 1, 1)
         quantize_w("u", 1, 0)
-        gate(1, 0, None, banks[0])
-        gate(0, 3, None, banks[1])
-        gate(1, 1, strips[3], banks[0])
-        gate(0, 2, strips[4], banks[1])
-        hidden(0, 1, 4, "vector", banks[6])
-        hidden(0, 3, 3, "vector")
-        hidden(1, 0, 7, "vector")
+        gate(1, 0, part(gates[1], 2), banks[0])
+        gate(0, 3, part(ups[0], 2), banks[1])
+        gate(1, 1, part(ups[1], 2), banks[2])
+        gate(0, 2, part(ups[1], 1), banks[0])
+        gate(0, 5, part(gates[0], 0), banks[1])
+        hidden_on_vector(0, 1, 4, banks[6])
+        hidden_on_vector(0, 3, 3, banks[3])
+        hidden_on_vector(1, 0, 2, banks[4])
         quantize_h(6, [(0, 0)])
         down(banks[6], range(3), 0, 1, 0)
-        hidden(1, 1, 5, "vector", banks[5])
-        quantize_h(7, [(1, 0)])
+        hidden_on_vector(1, 1, 5, banks[5])
+        quantize_h(2, [(1, 0)])
         down(banks[6], range(3), 0, 1, 1)
-        hidden(0, 2, 2, "vector")
+        lift(0, 5, part(ups[0], 0), banks[3])
+        gate(0, 6, part(gates[0], 1), banks[2])
+        lift(0, 6, part(ups[0], 1), banks[0])
+        quantize_h(4, [(0, 1), (1, 1)])
+        hidden_on_vector(0, 2, 2, banks[7])
         for a in range(2):
             down_pass(banks[7], 0, 3, a, 0, 1, a == 0, False)
-        quantize_h(4, [(0, 1), (1, 1)])
         for a in range(2):
             for n in range(2):
                 down_pass(banks[7], (1 + n) * P, n, a, 1, 1, False, a == 1 and n == 1)
-        for a in range(2):
-            down(banks[5], (2, 3), 1, 1, a)
 
         weigh(weighed[0], 0, banks[6], 0, 1, 0, 1)
         weigh(weighed[0], 1, banks[6], 1, 2, 0, 1)
@@ -295,41 +297,40 @@ def tile_list_sigm_scat_kernel(
         weigh(weighed[1], 0, banks[7], 1, 2, 1, 1)
         put_weighed(weighed[0][:, 3 * P : PASS], (3,), 0, 1)
         put_weighed(weighed[1], range(2), 1, 1)
-        hidden(0, 5, 4, "gpsimd")
-        hidden(0, 6, 5, "gpsimd")
-        hidden(1, 2, 0, "gpsimd")
-        gate(1, 3, strips[8])
-        hidden(1, 3, 1, "gpsimd")
+        hidden_on_gpsimd([(0, 5), (0, 6)], 4, 0, True)
+        hidden_on_gpsimd([(1, 2), (1, 3)], 0, 1)
+        for a in range(2):
+            down(banks[2], (2, 3), 1, 1, a)
+        nc.scalar.copy(ys[0][:, 0 : 2 * P], banks[2][:, 0 : 2 * P])
+        weigh_on_gpsimd(weighed[1][:, 2 * P : PASS], ys[0][:, 0 : 2 * P], 2, 1, 1)
 
-        weigh(strips[8], 0, banks[5], 0, 2, 1, 1)
         quantize_h(0, [(1, 2), (1, 3), (0, 2), (0, 3)])
         for a in range(2):
             down(banks[6], (0, 1), 2, 2, a)
-        put_weighed(strips[8], (2, 3), 1, 1)
+        put_weighed(weighed[1][:, 2 * P : PASS], (2, 3), 1, 1)
         for a in range(2):
             down(banks[7], (2, 3), 2, 2, a)
         for k in range(2):
             weigh(weighed[0], k, banks[6], k, 1, 2, 2)
         put_weighed(weighed[0], (0, 1), 2, 2)
-        for a, s, slot in ((0, 7, 2), (1, 5, 3), (0, 4, 0)):
-            hidden(a, s, slot, "gpsimd")
-        gate(1, 4, strips[9])
-        hidden(1, 4, 1, "gpsimd")
+        hidden_on_gpsimd([(0, 4), (1, 4), (0, 7)], 1, 0)
+        nc.scalar.copy(ys[1][:], banks[7][:])
+        weigh_on_gpsimd(late_gate[:], ys[1][:], 2, 2, 2)
 
-        quantize_h(2, [(0, 7), (1, 5), (0, 5), (0, 6)])
-        weigh(strips[9], 0, banks[7], 0, 2, 2, 2)
-        quantize_h(0, [(0, 4), (1, 4)])
+        quantize_h(1, [(0, 4), (1, 4)])
         for a in range(2):
             down(banks[5], range(4), 4, 1, a)
-        put_weighed(strips[9], (2, 3), 2, 2)
-        for s in range(6, 8):
-            hidden(1, s, s - 6, "gpsimd")
-        held = ups[(len(lifted) - 1) % len(ups)]
+        put_weighed(late_gate, (2,), 2, 2)
+        weigh(weighed[1], 0, banks[5], 0, 1, 4, 1)
+        put_weighed(late_gate[:, 2 * P : PASS], (3,), 2, 2)
+        put_weighed(weighed[1], (0,), 4, 1)
+        hidden_on_gpsimd([(1, 6), (1, 7), (1, 5)], 0, 1)
+        held = ups[1]
 
+        quantize_h(2, [(1, 5), (0, 7), (0, 5), (0, 6)])
         quantize_h(0, [(1, 6), (1, 7)])
-        nc.scalar.copy(held[:, 0:P], banks[5][:, 0:P])
         nc.scalar.copy(held[:, P:PASS], banks[5][:, P:PASS])
-        for n in range(4):
+        for n in range(1, 4):
             put_fused(held[:, n * P : (n + 1) * P], n, 4, 1)
         for n in range(4):
             bank = banks[(6 + n) % 8]
@@ -337,7 +338,7 @@ def tile_list_sigm_scat_kernel(
             down_pass(bank, 2 * P, n, 0, 7, 1, False, False)
             down_pass(bank, 0, n, 1, 5, 1, False, False)
             down_pass(bank, P, n, 1, 6, 2, False, True)
-            y = ys[n % len(ys)]
-            nc.scalar.copy(y[:], bank[:, 0 : 3 * P])
-            put_fused(y[:], n, 5, 3)
+            y = ys[n % len(ys)][:, 0 : 3 * P]
+            nc.scalar.copy(y, bank[:, 0 : 3 * P])
+            put_fused(y, n, 5, 3)
             nc.sync.dma_start(out[n * P : (n + 1) * P, :], pages[n][:])

@@ -53,7 +53,7 @@ def tile_list_sigm_scat_kernel(
         ups = [keep.tile([P, 3 * PASS], F32, name=f"ups{b}") for b in range(2)]
         ys = [keep.tile([P, PASS], F32, name=f"y{b}") for b in range(3)]
         weighed = [keep.tile([P, PASS], F32, name=f"weighed{b}") for b in range(2)]
-        h_bf = keep.tile([P, 8 * PASS], BF16, name="h_bf", align_bytes=64)
+        h_bf = keep.tile([P, 7 * PASS], BF16, name="h_bf", align_bytes=64)
 
         x_rows = xT.rearrange("(p i) t -> p i t", i=PACK)
         w_rows = {"g": wg.rearrange("(p i) r -> p i r", i=PACK), "u": wu.rearrange("(p i) r -> p i r", i=PACK)}
@@ -117,9 +117,9 @@ def tile_list_sigm_scat_kernel(
             return codes, scales
 
         w_bf = {
+            ("g", 1, 0): h_bf[:, 0 : 2 * PASS],
             ("u", 1, 1): h_bf[:, 2 * PASS : 4 * PASS],
             ("u", 1, 0): h_bf[:, 4 * PASS : 6 * PASS],
-            ("g", 1, 0): h_bf[:, 6 * PASS : 8 * PASS],
         }
 
         def interleave_w(w, a, tp, engine, m=slice(0, P)):
@@ -179,14 +179,22 @@ def tile_list_sigm_scat_kernel(
         def lift(a, s, dst, bank):
             nc.scalar.copy(woven(dst), first_product("u", a, s, bank))
 
-        def hidden_on_gpsimd(group, slot, side, ready=False):
+        def supply(group, side, last_bank=None):
             for k, (a, s) in enumerate(group):
-                if not ready:
-                    gate(a, s, part(gates[side], k), banks[len(lifted) % 2])
-                    lift(a, s, part(ups[side], k), banks[2 + (len(lifted) + 2) % 3])
-                    lifted.append(s)
-            count = len(group)
-            nc.gpsimd.tensor_tensor(part(h_bf, slot, count), part(ups[side], 0, count), part(gates[side], 0, count), MULT)
+                gate(a, s, part(gates[side], k), banks[len(lifted) % 2])
+                bank = banks[2 + (len(lifted) + 2) % 3]
+                lift(a, s, part(ups[side], k), last_bank if last_bank is not None and k == len(group) - 1 else bank)
+                lifted.append(s)
+
+        def hidden_on_gpsimd(slots, side):
+            dst = h_bf[:].rearrange("p (k e) -> p k e", e=PASS)[:, slots, :]
+            count = dst.shape[1]
+            nc.gpsimd.tensor_tensor(
+                dst,
+                part(ups[side], 0, count).rearrange("p (k e) -> p k e", e=PASS),
+                part(gates[side], 0, count).rearrange("p (k e) -> p k e", e=PASS),
+                MULT,
+            )
 
         h_q = {}
 
@@ -260,7 +268,7 @@ def tile_list_sigm_scat_kernel(
         gate(0, 1, late_gate[:], banks[1])
         quantize_w("g", 1, 0)
         quantize_w("g", 1, 1)
-        hidden_on_vector(0, 0, 6, banks[2])
+        hidden_on_vector(0, 0, 0, banks[2])
         interleave_w("u", 1, 1, "scalar", slice(P // 2, P))
         interleave_w("u", 1, 1, "vector", slice(0, P // 2))
         interleave_w("u", 1, 0, "vector")
@@ -270,20 +278,21 @@ def tile_list_sigm_scat_kernel(
         gate(0, 3, part(ups[0], 2), banks[1])
         gate(1, 1, part(ups[1], 2), banks[2])
         gate(0, 2, part(ups[1], 1), banks[0])
-        gate(0, 5, part(gates[0], 0), banks[1])
-        hidden_on_vector(0, 1, 4, banks[6])
-        hidden_on_vector(0, 3, 3, banks[3])
-        hidden_on_vector(1, 0, 2, banks[4])
-        quantize_h(6, [(0, 0)])
-        down(banks[6], range(3), 0, 1, 0)
-        hidden_on_vector(1, 1, 5, banks[5])
-        quantize_h(2, [(1, 0)])
-        down(banks[6], range(3), 0, 1, 1)
-        lift(0, 5, part(ups[0], 0), banks[3])
-        gate(0, 6, part(gates[0], 1), banks[2])
-        lift(0, 6, part(ups[0], 1), banks[0])
-        quantize_h(4, [(0, 1), (1, 1)])
-        hidden_on_vector(0, 2, 2, banks[7])
+        gate(0, 4, part(gates[0], 0), banks[1])
+        hidden_on_vector(0, 1, 2, banks[6])
+        hidden_on_vector(0, 3, 5, banks[3])
+        hidden_on_vector(1, 0, 1, banks[4])
+        hidden_on_vector(1, 1, 3, banks[5])
+        quantize_h(0, [(0, 0), (1, 0)])
+        for a in range(2):
+            down(banks[6], (0,), 0, 1, a)
+        for a in range(2):
+            down(banks[5], (1, 2), 0, 1, a)
+        lift(0, 4, part(ups[0], 0), banks[3])
+        gate(1, 3, part(gates[0], 1), banks[2])
+        lift(1, 3, part(ups[0], 1), banks[0])
+        quantize_h(2, [(0, 1), (1, 1)])
+        hidden_on_vector(0, 2, 4, banks[7])
         for a in range(2):
             down_pass(banks[7], 0, 3, a, 0, 1, a == 0, False)
         for a in range(2):
@@ -291,53 +300,54 @@ def tile_list_sigm_scat_kernel(
                 down_pass(banks[7], (1 + n) * P, n, a, 1, 1, False, a == 1 and n == 1)
 
         weigh(weighed[0], 0, banks[6], 0, 1, 0, 1)
-        weigh(weighed[0], 1, banks[6], 1, 2, 0, 1)
+        weigh(weighed[0], 1, banks[5], 0, 2, 0, 1)
         put_weighed(weighed[0], range(3), 0, 1)
         weigh(weighed[0], 3, banks[7], 0, 1, 0, 1)
         weigh(weighed[1], 0, banks[7], 1, 2, 1, 1)
         put_weighed(weighed[0][:, 3 * P : PASS], (3,), 0, 1)
         put_weighed(weighed[1], range(2), 1, 1)
-        hidden_on_gpsimd([(0, 5), (0, 6)], 4, 0, True)
-        hidden_on_gpsimd([(1, 2), (1, 3)], 0, 1)
+        hidden_on_gpsimd(slice(0, 4, 3), 0)
+        supply([(1, 4), (1, 2)], 1)
+        hidden_on_gpsimd(slice(1, 3), 1)
         for a in range(2):
             down(banks[2], (2, 3), 1, 1, a)
         nc.scalar.copy(ys[0][:, 0 : 2 * P], banks[2][:, 0 : 2 * P])
         weigh_on_gpsimd(weighed[1][:, 2 * P : PASS], ys[0][:, 0 : 2 * P], 2, 1, 1)
 
-        quantize_h(0, [(1, 2), (1, 3), (0, 2), (0, 3)])
+        quantize_h(2, [(1, 2), (1, 3), (0, 2), (0, 3)])
+        quantize_h(0, [(0, 4), (1, 4)])
         for a in range(2):
             down(banks[6], (0, 1), 2, 2, a)
         put_weighed(weighed[1][:, 2 * P : PASS], (2, 3), 1, 1)
         for a in range(2):
             down(banks[7], (2, 3), 2, 2, a)
+        for a in range(2):
+            down(banks[5], range(4), 4, 1, a)
         for k in range(2):
             weigh(weighed[0], k, banks[6], k, 1, 2, 2)
         put_weighed(weighed[0], (0, 1), 2, 2)
-        hidden_on_gpsimd([(0, 4), (1, 4), (0, 7)], 1, 0)
+        supply([(0, 5), (0, 7), (1, 6)], 0)
+        hidden_on_gpsimd(slice(1, 6, 2), 0)
         nc.scalar.copy(ys[1][:], banks[7][:])
         weigh_on_gpsimd(late_gate[:], ys[1][:], 2, 2, 2)
-
-        quantize_h(1, [(0, 4), (1, 4)])
-        for a in range(2):
-            down(banks[5], range(4), 4, 1, a)
-        put_weighed(late_gate, (2,), 2, 2)
-        weigh(weighed[1], 0, banks[5], 0, 1, 4, 1)
-        put_weighed(late_gate[:, 2 * P : PASS], (3,), 2, 2)
-        put_weighed(weighed[1], (0,), 4, 1)
-        hidden_on_gpsimd([(1, 6), (1, 7), (1, 5)], 0, 1)
+        nc.scalar.copy(ys[2][:, 0:P], banks[5][:, 0:P])
+        weigh_on_gpsimd(weighed[1][:, 0:P], ys[2][:, 0:P], 1, 4, 1)
+        put_weighed(late_gate, (2, 3), 2, 2)
+        put_weighed(weighed[1], range(1), 4, 1)
+        supply([(0, 6), (1, 5), (1, 7)], 1)
+        hidden_on_gpsimd(slice(2, 7, 2), 1)
         held = ups[1]
 
-        quantize_h(2, [(1, 5), (0, 7), (0, 5), (0, 6)])
-        quantize_h(0, [(1, 6), (1, 7)])
+        quantize_h(1, [(0, 5), (0, 6), (0, 7)])
+        quantize_h(4, [(1, 5), (1, 6), (1, 7)])
         nc.scalar.copy(held[:, P:PASS], banks[5][:, P:PASS])
         for n in range(1, 4):
             put_fused(held[:, n * P : (n + 1) * P], n, 4, 1)
         for n in range(4):
             bank = banks[(6 + n) % 8]
-            down_pass(bank, 0, n, 0, 5, 2, True, False)
-            down_pass(bank, 2 * P, n, 0, 7, 1, False, False)
-            down_pass(bank, 0, n, 1, 5, 1, False, False)
-            down_pass(bank, P, n, 1, 6, 2, False, True)
+            for a in range(2):
+                down_pass(bank, 0, n, a, 5, 2, a == 0, False)
+                down_pass(bank, 2 * P, n, a, 7, 1, False, a == 1)
             y = ys[n % len(ys)][:, 0 : 3 * P]
             nc.scalar.copy(y, bank[:, 0 : 3 * P])
             put_fused(y, n, 5, 3)

@@ -38,6 +38,7 @@ def tile_list_sigm_scat_kernel(
         wgt_turned = keep.tile([P, 64], F32, name="wgt_turned", align_bytes=64)
         wgt_wide = [keep.tile([P, J // 4], F32, name=f"wgt_wide{q}", align_bytes=64) for q in range(4)]
         wgo_sb = keep.tile([P, J], F32, name="wgo_sb")
+        wgo_twice = {s: keep.tile([P, 2, s * P], F32, name=f"wgo_twice{s}") for s in (1, 2)}
         w_raw = {
             (w, a): keep.tile([P, PACK, PASS], F32, name=f"raw{w}{a}", tag=f"raw{w}{a}", align_bytes=64)
             for w in "gu"
@@ -51,6 +52,7 @@ def tile_list_sigm_scat_kernel(
         banks = [psum.tile([P, PASS], F32, name=f"bank{b}") for b in range(8)]
         gates = [keep.tile([P, 3 * PASS], F32, name=f"gates{b}") for b in range(2)]
         ups = [keep.tile([P, 3 * PASS], F32, name=f"ups{b}") for b in range(2)]
+        ups_once = keep.tile([P, 2 * PASS], F32, name="ups_once", tag="ups_once", align_bytes=64)
         ys = [keep.tile([P, PASS], F32, name=f"y{b}") for b in range(3)]
         weighed = [keep.tile([P, PASS], F32, name=f"weighed{b}") for b in range(2)]
         h_bf = keep.tile([P, 7 * PASS], BF16, name="h_bf", align_bytes=64)
@@ -79,6 +81,8 @@ def tile_list_sigm_scat_kernel(
         nc.sync.dma_start(wd_codes[:].bitcast(I32), wd_words.rearrange("a p n t -> p a (n t)").bitcast(I32))
         nc.sync.dma_start(put_list[:], offs2)
         nc.sync.dma_start(wgo_sb[:], wgo)
+        for s, tile in wgo_twice.items():
+            nc.sync.dma_start(tile[:], wgo[:, s * P : 2 * s * P].unsqueeze(1).to_broadcast([P, 2, s * P]))
 
         for u in range(2):
             nc.vector.transpose(wgt_turned[:, 32 * u : 32 * u + 32], wgt_rows[:, 32 * u : 32 * u + 32])
@@ -117,8 +121,8 @@ def tile_list_sigm_scat_kernel(
             return codes, scales
 
         w_bf = {
-            ("g", 1, 0): h_bf[:, 0 : 2 * PASS],
-            ("u", 1, 1): h_bf[:, 2 * PASS : 4 * PASS],
+            ("u", 1, 1): h_bf[:, 0 : 2 * PASS],
+            ("g", 1, 0): h_bf[:, 2 * PASS : 4 * PASS],
             ("u", 1, 0): h_bf[:, 4 * PASS : 6 * PASS],
         }
 
@@ -179,28 +183,20 @@ def tile_list_sigm_scat_kernel(
         def lift(a, s, dst, bank):
             nc.scalar.copy(woven(dst), first_product("u", a, s, bank))
 
-        def supply(group, side, last_bank=None):
+        def supply(group, gate_tile, up_tile):
             for k, (a, s) in enumerate(group):
-                gate(a, s, part(gates[side], k), banks[len(lifted) % 2])
-                bank = banks[2 + (len(lifted) + 2) % 3]
-                lift(a, s, part(ups[side], k), last_bank if last_bank is not None and k == len(group) - 1 else bank)
+                gate(a, s, part(gate_tile, k), banks[len(lifted) % 2])
+                lift(a, s, part(up_tile, k), banks[2 + (len(lifted) + 2) % 3])
                 lifted.append(s)
 
-        def hidden_on_gpsimd(slots, side):
-            dst = h_bf[:].rearrange("p (k e) -> p k e", e=PASS)[:, slots, :]
-            count = dst.shape[1]
-            nc.gpsimd.tensor_tensor(
-                dst,
-                part(ups[side], 0, count).rearrange("p (k e) -> p k e", e=PASS),
-                part(gates[side], 0, count).rearrange("p (k e) -> p k e", e=PASS),
-                MULT,
-            )
+        def hidden_on_gpsimd(slot, count, gate_tile, up_tile):
+            nc.gpsimd.tensor_tensor(part(h_bf, slot, count), part(up_tile, 0, count), part(gate_tile, 0, count), MULT)
 
         h_q = {}
 
-        def quantize_h(slot, strips):
+        def quantize_h(slot, strips, tag=None):
             count = len(strips)
-            codes, scales = quantize(f"h{strips[0][0]}{strips[0][1]}", h_bf[:, slot * PASS : (slot + count) * PASS], count * P)
+            codes, scales = quantize(f"h{strips[0][0]}{strips[0][1]}", part(h_bf, slot, count), count * P, tag)
             for k, strip in enumerate(strips):
                 h_q[strip] = codes, scales, k * P
 
@@ -234,15 +230,6 @@ def tile_list_sigm_scat_kernel(
                 MULT,
             )
 
-        def weigh_on_gpsimd(dst, y, blocks, s, count):
-            width = count * P
-            nc.gpsimd.tensor_tensor(
-                dst.rearrange("p (n j) -> p n j", n=blocks),
-                y.rearrange("p (n j) -> p n j", n=blocks),
-                wgo_sb[:, s * P : s * P + width].unsqueeze(1).to_broadcast([P, blocks, width]),
-                MULT,
-            )
-
         def put_weighed(src, rows, s, count):
             width = count * P
             for k, n in enumerate(rows):
@@ -268,7 +255,7 @@ def tile_list_sigm_scat_kernel(
         gate(0, 1, late_gate[:], banks[1])
         quantize_w("g", 1, 0)
         quantize_w("g", 1, 1)
-        hidden_on_vector(0, 0, 0, banks[2])
+        hidden_on_vector(0, 0, 2, banks[2])
         interleave_w("u", 1, 1, "scalar", slice(P // 2, P))
         interleave_w("u", 1, 1, "vector", slice(0, P // 2))
         interleave_w("u", 1, 0, "vector")
@@ -279,19 +266,19 @@ def tile_list_sigm_scat_kernel(
         gate(1, 1, part(ups[1], 2), banks[2])
         gate(0, 2, part(ups[1], 1), banks[0])
         gate(0, 4, part(gates[0], 0), banks[1])
-        hidden_on_vector(0, 1, 2, banks[6])
+        hidden_on_vector(0, 1, 0, banks[6])
         hidden_on_vector(0, 3, 5, banks[3])
-        hidden_on_vector(1, 0, 1, banks[4])
-        hidden_on_vector(1, 1, 3, banks[5])
-        quantize_h(0, [(0, 0), (1, 0)])
+        hidden_on_vector(1, 0, 3, banks[4])
+        hidden_on_vector(1, 1, 1, banks[5])
+        quantize_h(2, [(0, 0), (1, 0)])
         for a in range(2):
             down(banks[6], (0,), 0, 1, a)
         for a in range(2):
             down(banks[5], (1, 2), 0, 1, a)
         lift(0, 4, part(ups[0], 0), banks[3])
-        gate(1, 3, part(gates[0], 1), banks[2])
-        lift(1, 3, part(ups[0], 1), banks[0])
-        quantize_h(2, [(0, 1), (1, 1)])
+        gate(1, 4, part(gates[0], 1), banks[2])
+        lift(1, 4, part(ups[0], 1), banks[0])
+        quantize_h(0, [(0, 1), (1, 1)])
         hidden_on_vector(0, 2, 4, banks[7])
         for a in range(2):
             down_pass(banks[7], 0, 3, a, 0, 1, a == 0, False)
@@ -306,16 +293,18 @@ def tile_list_sigm_scat_kernel(
         weigh(weighed[1], 0, banks[7], 1, 2, 1, 1)
         put_weighed(weighed[0][:, 3 * P : PASS], (3,), 0, 1)
         put_weighed(weighed[1], range(2), 1, 1)
-        hidden_on_gpsimd(slice(0, 4, 3), 0)
-        supply([(1, 4), (1, 2)], 1)
-        hidden_on_gpsimd(slice(1, 3), 1)
+        hidden_on_gpsimd(0, 2, gates[0], ups[0])
+        supply([(1, 2), (1, 3)], gates[1], ups_once)
+        hidden_on_gpsimd(2, 2, gates[1], ups_once)
         for a in range(2):
             down(banks[2], (2, 3), 1, 1, a)
         nc.scalar.copy(ys[0][:, 0 : 2 * P], banks[2][:, 0 : 2 * P])
-        weigh_on_gpsimd(weighed[1][:, 2 * P : PASS], ys[0][:, 0 : 2 * P], 2, 1, 1)
+        nc.gpsimd.tensor_tensor(
+            weighed[1][:, 2 * P : PASS], ys[0][:, 0 : 2 * P], wgo_twice[1][:].rearrange("p n j -> p (n j)"), MULT
+        )
 
         quantize_h(2, [(1, 2), (1, 3), (0, 2), (0, 3)])
-        quantize_h(0, [(0, 4), (1, 4)])
+        quantize_h(0, [(0, 4), (1, 4)], "ups_once")
         for a in range(2):
             down(banks[6], (0, 1), 2, 2, a)
         put_weighed(weighed[1][:, 2 * P : PASS], (2, 3), 1, 1)
@@ -326,28 +315,29 @@ def tile_list_sigm_scat_kernel(
         for k in range(2):
             weigh(weighed[0], k, banks[6], k, 1, 2, 2)
         put_weighed(weighed[0], (0, 1), 2, 2)
-        supply([(0, 5), (0, 7), (1, 6)], 0)
-        hidden_on_gpsimd(slice(1, 6, 2), 0)
+        supply([(0, 5), (0, 6), (0, 7)], gates[0], ups[0])
+        hidden_on_gpsimd(1, 3, gates[0], ups[0])
         nc.scalar.copy(ys[1][:], banks[7][:])
-        weigh_on_gpsimd(late_gate[:], ys[1][:], 2, 2, 2)
+        nc.gpsimd.tensor_tensor(late_gate[:], ys[1][:], wgo_twice[2][:].rearrange("p n j -> p (n j)"), MULT)
         nc.scalar.copy(ys[2][:, 0:P], banks[5][:, 0:P])
-        weigh_on_gpsimd(weighed[1][:, 0:P], ys[2][:, 0:P], 1, 4, 1)
+        nc.gpsimd.tensor_tensor(weighed[1][:, 0:P], ys[2][:, 0:P], wgo_sb[:, PASS : PASS + P], MULT)
         put_weighed(late_gate, (2, 3), 2, 2)
         put_weighed(weighed[1], range(1), 4, 1)
-        supply([(0, 6), (1, 5), (1, 7)], 1)
-        hidden_on_gpsimd(slice(2, 7, 2), 1)
+        supply([(1, 5), (1, 6), (1, 7)], gates[1], ups[1])
+        hidden_on_gpsimd(4, 3, gates[1], ups[1])
         held = ups[1]
 
-        quantize_h(1, [(0, 5), (0, 6), (0, 7)])
-        quantize_h(4, [(1, 5), (1, 6), (1, 7)])
+        quantize_h(1, [(0, 5), (0, 6), (0, 7), (1, 5)])
+        quantize_h(5, [(1, 6), (1, 7)])
         nc.scalar.copy(held[:, P:PASS], banks[5][:, P:PASS])
         for n in range(1, 4):
             put_fused(held[:, n * P : (n + 1) * P], n, 4, 1)
         for n in range(4):
             bank = banks[(6 + n) % 8]
-            for a in range(2):
-                down_pass(bank, 0, n, a, 5, 2, a == 0, False)
-                down_pass(bank, 2 * P, n, a, 7, 1, False, a == 1)
+            down_pass(bank, 0, n, 0, 5, 2, True, False)
+            down_pass(bank, 2 * P, n, 0, 7, 1, False, False)
+            down_pass(bank, 0, n, 1, 5, 1, False, False)
+            down_pass(bank, P, n, 1, 6, 2, False, True)
             y = ys[n % len(ys)][:, 0 : 3 * P]
             nc.scalar.copy(y, bank[:, 0 : 3 * P])
             put_fused(y, n, 5, 3)

@@ -268,13 +268,12 @@ def tile_list_sigm_scat_kernel(
         gate(0, 4, part(gates[0], 0), banks[1])
         hidden_on_vector(0, 1, 0, banks[6])
         hidden_on_vector(0, 3, 5, banks[3])
-        hidden_on_vector(1, 0, 3, banks[4])
+        hidden_on_vector(1, 0, 4, banks[4])
+        quantize_h(2, [(0, 0)])
+        down(banks[6], range(3), 0, 1, 0)
         hidden_on_vector(1, 1, 1, banks[5])
-        quantize_h(2, [(0, 0), (1, 0)])
-        for a in range(2):
-            down(banks[6], (0,), 0, 1, a)
-        for a in range(2):
-            down(banks[5], (1, 2), 0, 1, a)
+        quantize_h(4, [(1, 0)])
+        down(banks[6], range(3), 0, 1, 1)
         lift(0, 4, part(ups[0], 0), banks[3])
         gate(1, 4, part(gates[0], 1), banks[2])
         lift(1, 4, part(ups[0], 1), banks[0])
@@ -287,7 +286,7 @@ def tile_list_sigm_scat_kernel(
                 down_pass(banks[7], (1 + n) * P, n, a, 1, 1, False, a == 1 and n == 1)
 
         weigh(weighed[0], 0, banks[6], 0, 1, 0, 1)
-        weigh(weighed[0], 1, banks[5], 0, 2, 0, 1)
+        weigh(weighed[0], 1, banks[6], 1, 2, 0, 1)
         put_weighed(weighed[0], range(3), 0, 1)
         weigh(weighed[0], 3, banks[7], 0, 1, 0, 1)
         weigh(weighed[1], 0, banks[7], 1, 2, 1, 1)

@@ -121,9 +121,9 @@ def tile_list_sigm_scat_kernel(
             return codes, scales
 
         w_bf = {
-            ("u", 1, 1): h_bf[:, 0 : 2 * PASS],
+            ("u", 1, 0): h_bf[:, 0 : 2 * PASS],
             ("g", 1, 0): h_bf[:, 2 * PASS : 4 * PASS],
-            ("u", 1, 0): h_bf[:, 4 * PASS : 6 * PASS],
+            ("u", 1, 1): h_bf[:, 4 * PASS : 6 * PASS],
         }
 
         def interleave_w(w, a, tp, engine, m=slice(0, P)):
@@ -266,8 +266,8 @@ def tile_list_sigm_scat_kernel(
         gate(1, 1, part(ups[1], 2), banks[2])
         gate(0, 2, part(ups[1], 1), banks[0])
         gate(0, 4, part(gates[0], 0), banks[1])
-        hidden_on_vector(0, 1, 0, banks[6])
         hidden_on_vector(0, 3, 5, banks[3])
+        hidden_on_vector(0, 1, 0, banks[6])
         hidden_on_vector(1, 0, 4, banks[4])
         quantize_h(2, [(0, 0)])
         down(banks[6], range(3), 0, 1, 0)
@@ -316,12 +316,12 @@ def tile_list_sigm_scat_kernel(
         put_weighed(weighed[0], (0, 1), 2, 2)
         supply([(0, 5), (0, 6), (0, 7)], gates[0], ups[0])
         hidden_on_gpsimd(1, 3, gates[0], ups[0])
-        nc.scalar.copy(ys[1][:], banks[7][:])
-        nc.gpsimd.tensor_tensor(late_gate[:], ys[1][:], wgo_twice[2][:].rearrange("p n j -> p (n j)"), MULT)
         nc.scalar.copy(ys[2][:, 0:P], banks[5][:, 0:P])
         nc.gpsimd.tensor_tensor(weighed[1][:, 0:P], ys[2][:, 0:P], wgo_sb[:, PASS : PASS + P], MULT)
-        put_weighed(late_gate, (2, 3), 2, 2)
         put_weighed(weighed[1], range(1), 4, 1)
+        nc.scalar.copy(ys[1][:], banks[7][:])
+        nc.gpsimd.tensor_tensor(late_gate[:], ys[1][:], wgo_twice[2][:].rearrange("p n j -> p (n j)"), MULT)
+        put_weighed(late_gate, (2, 3), 2, 2)
         supply([(1, 5), (1, 6), (1, 7)], gates[1], ups[1])
         hidden_on_gpsimd(4, 3, gates[1], ups[1])
         held = ups[1]

@@ -19,7 +19,7 @@ P = 128
 PACK = 4
 PASS = P * PACK
 HALF = J // 2
-LIST_COLS = HALF // 16
+LOW, HIGH = slice(0, P // 2), slice(P // 2, P)
 
 
 def tile_list_sigm_scat_kernel(
@@ -30,32 +30,26 @@ def tile_list_sigm_scat_kernel(
         keep = ctx.enter_context(tc.tile_pool(name="keep", bufs=1))
         psum = ctx.enter_context(tc.psum_pool(name="psum", bufs=1))
 
+        def sbuf(name, shape, dtype, tag=None):
+            return keep.tile([P] + shape, dtype, name=name, tag=tag or name, align_bytes=64)
+
         pick_list = keep.tile([P, J // 16], U16, name="pick_list")
         put_list = keep.tile([P, J // 16], U16, name="put_list")
-        planes = [keep.tile([P, T], F32, name=f"plane{i}") for i in range(PACK)]
-        wgt_sb = [keep.tile([P, HALF], F32, name=f"wgt{h}", align_bytes=64) for h in range(2)]
-        wgt_rows = keep.tile([P, 64], F32, name="wgt_rows", align_bytes=64)
-        wgt_turned = keep.tile([P, 64], F32, name="wgt_turned", align_bytes=64)
-        wgt_wide = [keep.tile([P, J // 4], F32, name=f"wgt_wide{q}", align_bytes=64) for q in range(4)]
-        wgo_sb = keep.tile([P, J], F32, name="wgo_sb")
-        wgo_twice = {s: keep.tile([P, 2, s * P], F32, name=f"wgo_twice{s}") for s in (1, 2)}
-        w_raw = {
-            (w, a): keep.tile([P, PACK, PASS], F32, name=f"raw{w}{a}", tag=f"raw{w}{a}", align_bytes=64)
-            for w in "gu"
-            for a in range(2)
-        }
-        wd_codes = keep.tile([P, 2, N], U32, name="wd_codes", align_bytes=64)
-        wd_sc = keep.tile([P, 2, N], U8, name="wd_sc", align_bytes=64)
-        pages = [keep.tile([P, T], F32, name=f"page{n}") for n in range(4)]
-        warm = keep.tile([P, 8], F32, name="warm")
-        warm_out = keep.tile([P, 8], F32, name="warm_out")
+        planes = [sbuf(f"plane{i}", [T], F32) for i in range(PACK)]
+        wgt_sb = sbuf("wgt_sb", [J], F32)
+        wgt_rows = sbuf("wgt_rows", [64], F32)
+        wgt_turned = sbuf("wgt_turned", [64], F32)
+        wgt_wide = [sbuf(f"wgt_wide{q}", [J // 4], F32) for q in range(4)]
+        wgo_sb = sbuf("wgo_sb", [J], F32)
+        w_raw = {(w, a): sbuf(f"raw{w}{a}", [PACK, PASS], F32) for w in "gu" for a in range(2)}
+        wd_codes = sbuf("wd_codes", [2, N], U32)
+        wd_sc = sbuf("wd_sc", [2, N], U8)
+        pages = [sbuf(f"page{n}", [T], F32) for n in range(4)]
+        warm = sbuf("warm", [8], F32)
+        warm_out = sbuf("warm_out", [8], F32)
         banks = [psum.tile([P, PASS], F32, name=f"bank{b}") for b in range(8)]
-        gates = [keep.tile([P, 3 * PASS], F32, name=f"gates{b}") for b in range(2)]
-        ups = [keep.tile([P, 3 * PASS], F32, name=f"ups{b}") for b in range(2)]
-        ups_once = keep.tile([P, 2 * PASS], F32, name="ups_once", tag="ups_once", align_bytes=64)
-        ys = [keep.tile([P, PASS], F32, name=f"y{b}") for b in range(3)]
-        weighed = [keep.tile([P, PASS], F32, name=f"weighed{b}") for b in range(2)]
-        h_bf = keep.tile([P, 7 * PASS], BF16, name="h_bf", align_bytes=64)
+        h_early = sbuf("h_early", [3 * PASS], BF16)
+        h_bf = sbuf("h_bf", [7 * PASS], BF16)
 
         x_rows = xT.rearrange("(p i) t -> p i t", i=PACK)
         w_rows = {"g": wg.rearrange("(p i) r -> p i r", i=PACK), "u": wu.rearrange("(p i) r -> p i r", i=PACK)}
@@ -66,7 +60,8 @@ def tile_list_sigm_scat_kernel(
         for page in pages:
             nc.gpsimd.memset(page[:], 0.0)
 
-        nc.sync.dma_start(wgt_rows[:], wgt.rearrange("(g s) (c e) -> g s c e", s=16, e=64)[:, 0, :, :])
+        half_rows = wgt.rearrange("p (h e) -> (p h) e", h=2)[0 : 2 * P : 17, :]
+        nc.sync.dma_start(wgt_rows[:], half_rows.rearrange("m (c e) -> m c e", e=64))
         nc.sync.dma_start(pick_list[:], offs)
         for i in range(PACK):
             nc.sync.dma_start(planes[i][:], x_rows[:, i, :])
@@ -81,8 +76,6 @@ def tile_list_sigm_scat_kernel(
         nc.sync.dma_start(wd_codes[:].bitcast(I32), wd_words.rearrange("a p n t -> p a (n t)").bitcast(I32))
         nc.sync.dma_start(put_list[:], offs2)
         nc.sync.dma_start(wgo_sb[:], wgo)
-        for s, tile in wgo_twice.items():
-            nc.sync.dma_start(tile[:], wgo[:, s * P : 2 * s * P].unsqueeze(1).to_broadcast([P, 2, s * P]))
 
         for u in range(2):
             nc.vector.transpose(wgt_turned[:, 32 * u : 32 * u + 32], wgt_rows[:, 32 * u : 32 * u + 32])
@@ -92,59 +85,65 @@ def tile_list_sigm_scat_kernel(
                 wgt_wide[q][:].rearrange("p (c u g i) -> p c u g i", u=2, g=2, i=16),
                 by_block[:, 4 * q : 4 * q + 4, :, :].unsqueeze(4).to_broadcast([P, 4, 2, 2, 16]),
             )
-            nc.vector.transpose(wgt_sb[q // 2][:, q % 2 * 256 : (q % 2 + 1) * 256], wgt_wide[q][:])
+            nc.vector.transpose(wgt_sb[:, q * 256 : (q + 1) * 256], wgt_wide[q][:])
 
-        picked = {(h, pr): keep.tile([P, 2, HALF], F32, name=f"picked{h}{pr}") for h in range(2) for pr in range(2)}
-        x_bf = [keep.tile([P, HALF, PACK], BF16, name=f"x_bf{h}", align_bytes=64) for h in range(2)]
+        x_bf = [sbuf(f"x_bf{h}", [HALF, PACK], BF16) for h in range(2)]
+        pairs_of_planes = [sbuf(f"picked{pr}", [2 * J], F32) for pr in range(2)]
+
+        def pick(i, first, count):
+            nc.vector.tensor_tensor(
+                pairs_of_planes[i // 2][:, i % 2 * J + first : i % 2 * J + first + count],
+                planes[i][:].indirect(pick_list[:, first // 16 : (first + count) // 16]),
+                wgt_sb[:, first : first + count],
+                MULT,
+            )
 
         def weave_x(h, pr):
-            dst = x_bf[h][:, :, 2 * pr : 2 * pr + 2].rearrange("p (c f) e -> p c e f", f=4)
-            src = picked[h, pr][:].rearrange("p e (c f) -> p c e f", f=4)
-            nc.scalar.copy(dst, src)
+            both = pairs_of_planes[pr][:].rearrange("p (e h c f) -> p h c e f", e=2, h=2, f=4)
+            nc.scalar.copy(x_bf[h][:, :, 2 * pr : 2 * pr + 2].rearrange("p (c f) e -> p c e f", f=4), both[:, h])
 
-        for pr in range(2):
-            for e in range(2):
-                for h in range(2):
-                    nc.vector.tensor_tensor(
-                        picked[h, pr][:, e, :],
-                        planes[2 * pr + e][:].indirect(pick_list[:, h * LIST_COLS : (h + 1) * LIST_COLS]),
-                        wgt_sb[h][:],
-                        MULT,
-                    )
-            for h in range(2):
-                weave_x(h, pr)
+        pick(0, 0, J)
+        for h in range(2):
+            pick(1, h * HALF, HALF)
+        for h in range(2):
+            weave_x(h, 0)
+        pick(2, 0, J)
+        for h in range(2):
+            pick(3, h * HALF, HALF)
+        for h in range(2):
+            weave_x(h, 1)
+
+        def part(tile, first, count=1):
+            return tile[:, first * PASS : (first + count) * PASS]
 
         def quantize(name, src, words, tag=None):
-            codes = keep.tile([P, words], U32, name=f"codes_{name}", tag=tag or f"codes_{name}", align_bytes=64)
-            scales = keep.tile([P, words], U8, name=f"scales_{name}", align_bytes=64)
+            codes = sbuf(f"codes_{name}", [words], U32, tag)
+            scales = sbuf(f"scales_{name}", [words], U8)
             nc.vector.quantize_mx(out=codes[:].bitcast(FP8X4), scales=scales[:], in_=src)
             return codes, scales
 
-        w_bf = {
-            ("u", 1, 0): h_bf[:, 0 : 2 * PASS],
-            ("g", 1, 0): h_bf[:, 2 * PASS : 4 * PASS],
-            ("u", 1, 1): h_bf[:, 4 * PASS : 6 * PASS],
-        }
+        w_bf = {("u", 1, 1): part(h_bf, 2, 2), ("u", 1, 0): part(h_bf, 0, 2)}
+        for key in (("g", 0, 0), ("g", 0, 1), ("u", 0, 0), ("u", 0, 1), ("g", 1, 0), ("g", 1, 1)):
+            w_bf[key] = sbuf(f"w_bf{key[0]}{key[1]}{key[2]}", [2 * PASS], BF16)[:]
 
-        def interleave_w(w, a, tp, engine, m=slice(0, P)):
-            if (w, a, tp) not in w_bf:
-                w_bf[w, a, tp] = keep.tile([P, 2 * PASS], BF16, name=f"w_bf{w}{a}{tp}", align_bytes=64)[:]
+        def weave_w(copy, w, a, tp, m=slice(0, P)):
             dst = w_bf[w, a, tp].rearrange("p (t m i) -> p m i t", t=2, i=PACK)[:, m, :, :]
             src = w_raw[w, a][:].rearrange("p i (m t) -> p m i t", t=PACK)[:, m, :, 2 * tp : 2 * tp + 2]
-            if engine == "vector":
-                nc.vector.tensor_copy(dst, src)
-            else:
-                nc.scalar.copy(dst, src)
+            copy(dst, src)
 
-        w_q = {}
+        on_vector, on_scalar = nc.vector.tensor_copy, nc.scalar.copy
+        w_q, x_q, h_q = {}, {}, {}
 
         def quantize_w(w, a, tp):
             w_q[w, a, tp] = quantize(f"{w}{a}{tp}", w_bf[w, a, tp], 2 * P)
 
-        x_q = {}
-
         def quantize_x(h, tag=None):
             x_q[h] = quantize(f"x{h}", x_bf[h][:].rearrange("p j i -> p (j i)"), HALF, tag)
+
+        def quantize_h(src, strips, tag=None):
+            codes, scales = quantize(f"h{strips[0][0]}{strips[0][1]}", src, len(strips) * P, tag)
+            for k, strip in enumerate(strips):
+                h_q[strip] = codes, scales, k * P
 
         def first_product(w, a, s, bank):
             cols = slice((s % 4) * P, (s % 4 + 1) * P)
@@ -165,42 +164,21 @@ def tile_list_sigm_scat_kernel(
         def woven(ap):
             return ap.rearrange("p (j t) -> p j t", t=PACK)
 
-        def part(tile, first, count=1):
-            return tile[:, first * PASS : (first + count) * PASS]
+        def gate(a, s, dst, bank):
+            nc.scalar.activation(woven(dst), first_product("g", a, s, bank), SIGMOID)
 
-        made = {}
+        def hidden_on_vector(a, s, dst, sig, bank):
+            nc.vector.tensor_tensor(woven(dst), first_product("u", a, s, bank), woven(sig), MULT)
 
-        def gate(a, s, sig, bank):
-            made[a, s] = sig
-            nc.scalar.activation(woven(sig), first_product("g", a, s, bank), SIGMOID)
+        def supply(strips, gates, ups, gate_banks, up_banks):
+            for k, (a, s) in enumerate(strips):
+                gate(a, s, part(gates, k), banks[gate_banks[k]])
+                nc.scalar.copy(woven(part(ups, k)), first_product("u", a, s, banks[up_banks[k]]))
 
-        def hidden_on_vector(a, s, slot, bank):
-            up = first_product("u", a, s, bank)
-            nc.vector.tensor_tensor(woven(part(h_bf, slot)), up, woven(made[a, s]), MULT)
+        def hidden_on_gpsimd(dst, gates, ups):
+            nc.gpsimd.tensor_tensor(dst, ups[:], gates[:], MULT)
 
-        lifted = []
-
-        def lift(a, s, dst, bank):
-            nc.scalar.copy(woven(dst), first_product("u", a, s, bank))
-
-        def supply(group, gate_tile, up_tile):
-            for k, (a, s) in enumerate(group):
-                gate(a, s, part(gate_tile, k), banks[len(lifted) % 2])
-                lift(a, s, part(up_tile, k), banks[2 + (len(lifted) + 2) % 3])
-                lifted.append(s)
-
-        def hidden_on_gpsimd(slot, count, gate_tile, up_tile):
-            nc.gpsimd.tensor_tensor(part(h_bf, slot, count), part(up_tile, 0, count), part(gate_tile, 0, count), MULT)
-
-        h_q = {}
-
-        def quantize_h(slot, strips, tag=None):
-            count = len(strips)
-            codes, scales = quantize(f"h{strips[0][0]}{strips[0][1]}", part(h_bf, slot, count), count * P, tag)
-            for k, strip in enumerate(strips):
-                h_q[strip] = codes, scales, k * P
-
-        def down_pass(bank, col, n, a, s, count, start, stop):
+        def down(bank, col, n, a, s, count, start, stop):
             codes, scales, first = h_q[a, s]
             m = slice(n * P, (n + 1) * P)
             cols = slice(first, first + count * P)
@@ -214,23 +192,23 @@ def tile_list_sigm_scat_kernel(
                 stop=stop,
             )
 
-        def down(bank, rows, s, count, a):
-            for k, n in enumerate(rows):
-                down_pass(bank, k * count * P, n, a, s, count, a == 0 and k == 0, a == 1 and k == len(rows) - 1)
+        def down_chunk(bank, s, a):
+            for n in range(4):
+                down(bank, n * P, n, a, s, 1, a == 0 and n == 0, a == 1 and n == 3)
 
-        def places(n, s, count):
-            return pages[n][:].indirect(put_list[:, s * 8 : (s + count) * 8])
-
-        def weigh(dst, place, bank, first, blocks, s, count):
+        def weigh(engine, dst, src, blocks, s, count):
             width = count * P
-            nc.vector.tensor_tensor(
-                dst[:, place * width : (place + blocks) * width].rearrange("p (n j) -> p n j", n=blocks),
-                bank[:, first * width : (first + blocks) * width].rearrange("p (n j) -> p n j", n=blocks),
+            engine.tensor_tensor(
+                dst.rearrange("p (n j) -> p n j", n=blocks),
+                src.rearrange("p (n j) -> p n j", n=blocks),
                 wgo_sb[:, s * P : s * P + width].unsqueeze(1).to_broadcast([P, blocks, width]),
                 MULT,
             )
 
-        def put_weighed(src, rows, s, count):
+        def places(n, s, count):
+            return pages[n][:].indirect(put_list[:, s * 8 : (s + count) * 8])
+
+        def put(src, rows, s, count):
             width = count * P
             for k, n in enumerate(rows):
                 nc.vector.tensor_copy(places(n, s, count), src[:, k * width : (k + 1) * width])
@@ -238,105 +216,114 @@ def tile_list_sigm_scat_kernel(
         def put_fused(y, n, s, count):
             nc.vector.tensor_tensor(places(n, s, count), y, wgo_sb[:, s * P : (s + count) * P], MULT)
 
-        interleave_w("g", 0, 0, "vector")
-        interleave_w("g", 0, 1, "vector")
-        quantize_x(0, "rawg0")
+        weave_w(on_vector, "g", 0, 0)
+        weave_w(on_vector, "g", 0, 1)
         quantize_w("g", 0, 0)
+        quantize_x(0, "rawg0")
         quantize_w("g", 0, 1)
-        interleave_w("u", 0, 1, "scalar")
-        interleave_w("u", 0, 0, "vector")
-        quantize_w("u", 0, 0)
-        quantize_x(1)
+        weave_w(on_scalar, "u", 0, 1, HIGH)
+        weave_w(on_vector, "u", 0, 1, LOW)
+        weave_w(on_vector, "u", 0, 0)
         quantize_w("u", 0, 1)
-        gate(0, 0, part(gates[0], 2), banks[0])
-        interleave_w("g", 1, 1, "scalar")
-        interleave_w("g", 1, 0, "vector")
-        late_gate = keep.tile([P, PASS], F32, name="late_gate", tag="rawg1", align_bytes=64)
-        gate(0, 1, late_gate[:], banks[1])
+        quantize_w("u", 0, 0)
+        quantize_x(1, "rawu0")
+        early = sbuf("early", [2 * PASS], F32)
+        for s in range(2):
+            gate(0, s, part(early, s), banks[s])
+        weave_w(on_scalar, "g", 1, 1)
+        weave_w(on_vector, "g", 1, 0)
+        late = sbuf("late", [4 * PASS], F32, "plane0")
+        hidden_on_vector(0, 0, part(h_early, 0), part(early, 0), banks[2])
         quantize_w("g", 1, 0)
         quantize_w("g", 1, 1)
-        hidden_on_vector(0, 0, 2, banks[2])
-        interleave_w("u", 1, 1, "scalar", slice(P // 2, P))
-        interleave_w("u", 1, 1, "vector", slice(0, P // 2))
-        interleave_w("u", 1, 0, "vector")
+        gate(0, 2, part(late, 0), banks[6])
+        gate(0, 3, part(late, 1), banks[7])
+        hidden_on_vector(0, 1, part(h_early, 1), part(early, 1), banks[3])
+        hidden_on_vector(0, 2, part(h_early, 2), part(late, 0), banks[4])
+        weave_w(on_scalar, "u", 1, 1, HIGH)
+        weave_w(on_vector, "u", 1, 1, LOW)
+        weave_w(on_vector, "u", 1, 0)
         quantize_w("u", 1, 1)
         quantize_w("u", 1, 0)
-        gate(1, 0, part(gates[1], 2), banks[0])
-        gate(0, 3, part(ups[0], 2), banks[1])
-        gate(1, 1, part(ups[1], 2), banks[2])
-        gate(0, 2, part(ups[1], 1), banks[0])
-        gate(0, 4, part(gates[0], 0), banks[1])
-        hidden_on_vector(0, 3, 5, banks[3])
-        hidden_on_vector(0, 1, 0, banks[6])
-        hidden_on_vector(1, 0, 4, banks[4])
-        quantize_h(2, [(0, 0)])
-        down(banks[6], range(3), 0, 1, 0)
-        hidden_on_vector(1, 1, 1, banks[5])
-        quantize_h(4, [(1, 0)])
-        down(banks[6], range(3), 0, 1, 1)
-        lift(0, 4, part(ups[0], 0), banks[3])
-        gate(1, 4, part(gates[0], 1), banks[2])
-        lift(1, 4, part(ups[0], 1), banks[0])
-        quantize_h(0, [(0, 1), (1, 1)])
-        hidden_on_vector(0, 2, 4, banks[7])
-        for a in range(2):
-            down_pass(banks[7], 0, 3, a, 0, 1, a == 0, False)
-        for a in range(2):
-            for n in range(2):
-                down_pass(banks[7], (1 + n) * P, n, a, 1, 1, False, a == 1 and n == 1)
+        gate(1, 0, part(late, 2), banks[0])
+        gate(1, 1, part(late, 3), banks[1])
+        gate(1, 2, part(early, 0), banks[6])
+        quantize_h(h_early[:], [(0, 0), (0, 1), (0, 2)], "rawu1")
+        hidden_on_vector(0, 3, part(h_bf, 2), part(late, 1), banks[5])
+        hidden_on_vector(1, 0, part(h_bf, 5), part(late, 2), banks[2])
+        hidden_on_vector(1, 1, part(h_bf, 6), part(late, 3), banks[3])
+        down_chunk(banks[6], 0, 0)
+        quantize_h(part(h_bf, 5), [(1, 0)])
+        down_chunk(banks[6], 0, 1)
+        quantize_h(part(h_bf, 6), [(1, 1)])
+        hidden_on_vector(1, 2, part(h_bf, 3), part(early, 0), banks[4])
 
-        weigh(weighed[0], 0, banks[6], 0, 1, 0, 1)
-        weigh(weighed[0], 1, banks[6], 1, 2, 0, 1)
-        put_weighed(weighed[0], range(3), 0, 1)
-        weigh(weighed[0], 3, banks[7], 0, 1, 0, 1)
-        weigh(weighed[1], 0, banks[7], 1, 2, 1, 1)
-        put_weighed(weighed[0][:, 3 * P : PASS], (3,), 0, 1)
-        put_weighed(weighed[1], range(2), 1, 1)
-        hidden_on_gpsimd(0, 2, gates[0], ups[0])
-        supply([(1, 2), (1, 3)], gates[1], ups_once)
-        hidden_on_gpsimd(2, 2, gates[1], ups_once)
-        for a in range(2):
-            down(banks[2], (2, 3), 1, 1, a)
-        nc.scalar.copy(ys[0][:, 0 : 2 * P], banks[2][:, 0 : 2 * P])
-        nc.gpsimd.tensor_tensor(
-            weighed[1][:, 2 * P : PASS], ys[0][:, 0 : 2 * P], wgo_twice[1][:].rearrange("p n j -> p (n j)"), MULT
-        )
+        def inputs(name, count, gate_tag=None, up_tag=None):
+            return sbuf(f"gates_{name}", [count * PASS], F32, gate_tag), sbuf(f"ups_{name}", [count * PASS], F32, up_tag)
 
-        quantize_h(2, [(1, 2), (1, 3), (0, 2), (0, 3)])
-        quantize_h(0, [(0, 4), (1, 4)], "ups_once")
+        pair = inputs("pair", 2)
+        single = inputs("single", 1)
+        triples = [inputs(f"triple{b}", 3, f"plane{1 + b}", f"picked{b}") for b in range(2)]
+        weighed = [sbuf(f"weighed{b}", [PASS], F32) for b in range(3)]
+        ys = [sbuf(f"y{b}", [PASS], F32) for b in range(3)]
+
+        supply([(0, 4)], *single, (7,), (0,))
         for a in range(2):
-            down(banks[6], (0, 1), 2, 2, a)
-        put_weighed(weighed[1][:, 2 * P : PASS], (2, 3), 1, 1)
+            down_chunk(banks[7], 1, a)
+        weigh(nc.vector, weighed[0][:, 0:P], banks[6][:, 0:P], 1, 0, 1)
+        weigh(nc.vector, weighed[0][:, P:PASS], banks[6][:, P:PASS], 3, 0, 1)
+        put(weighed[0], range(4), 0, 1)
+        hidden_on_gpsimd(part(h_bf, 6), *single)
+        nc.scalar.copy(ys[0][:], banks[7][:])
+        weigh(nc.gpsimd, weighed[1][:, 0 : 2 * P], ys[0][:, 0 : 2 * P], 2, 1, 1)
+        put(weighed[1], (0, 1), 1, 1)
+        supply([(1, 3), (1, 4)], *pair, (1, 0), (5, 4))
+        hidden_on_gpsimd(part(h_bf, 4, 2), *pair)
+        weigh(nc.gpsimd, pair[0][:, 0 : 2 * P], ys[0][:, 2 * P : PASS], 2, 1, 1)
+
+        quantize_h(part(h_bf, 2, 4), [(0, 3), (1, 2), (1, 3), (1, 4)])
+        quantize_h(part(h_bf, 6), [(0, 4)], "ups_pair")
+
+        def down_double(bank, rows):
+            for k, n in enumerate(rows):
+                down(bank, k * 2 * P, n, 1, 2, 2, k == 0, False)
+                down(bank, k * 2 * P, n, 0, 2, 1, False, False)
+                down(bank, k * 2 * P + P, n, 0, 3, 1, False, k == 1)
+
+        down_double(banks[0], (0, 1))
+        supply([(0, 5), (0, 6), (0, 7)], *triples[0], (6, 5, 6), (7, 4, 7))
+        supply([(1, 5)], *triples[1], (5,), (4,))
+        down_double(banks[5], (2, 3))
+        put(pair[0], (2, 3), 1, 1)
         for a in range(2):
-            down(banks[7], (2, 3), 2, 2, a)
-        for a in range(2):
-            down(banks[5], range(4), 4, 1, a)
+            down_chunk(banks[4], 4, a)
         for k in range(2):
-            weigh(weighed[0], k, banks[6], k, 1, 2, 2)
-        put_weighed(weighed[0], (0, 1), 2, 2)
-        supply([(0, 5), (0, 6), (0, 7)], gates[0], ups[0])
-        hidden_on_gpsimd(1, 3, gates[0], ups[0])
-        nc.scalar.copy(ys[2][:, 0:P], banks[5][:, 0:P])
-        nc.gpsimd.tensor_tensor(weighed[1][:, 0:P], ys[2][:, 0:P], wgo_sb[:, PASS : PASS + P], MULT)
-        put_weighed(weighed[1], range(1), 4, 1)
-        nc.scalar.copy(ys[1][:], banks[7][:])
-        nc.gpsimd.tensor_tensor(late_gate[:], ys[1][:], wgo_twice[2][:].rearrange("p n j -> p (n j)"), MULT)
-        put_weighed(late_gate, (2, 3), 2, 2)
-        supply([(1, 5), (1, 6), (1, 7)], gates[1], ups[1])
-        hidden_on_gpsimd(4, 3, gates[1], ups[1])
-        held = ups[1]
+            cols = slice(k * 2 * P, (k + 1) * 2 * P)
+            weigh(nc.vector, weighed[0][:, cols], banks[0][:, cols], 1, 2, 2)
+        put(weighed[0], (0, 1), 2, 2)
+        hidden_on_gpsimd(part(h_bf, 4, 3), *triples[0])
+        y_mid = sbuf("y_mid", [PASS + P], F32)
+        nc.scalar.copy(y_mid[:, 0:PASS], banks[5][:])
+        weigh(nc.gpsimd, weighed[2][:], y_mid[:, 0:PASS], 2, 2, 2)
+        put(weighed[2], (2, 3), 2, 2)
+        nc.scalar.copy(y_mid[:, PASS : PASS + P], banks[4][:, 0:P])
+        weigh(nc.gpsimd, weighed[1][:, 0:P], y_mid[:, PASS : PASS + P], 1, 4, 1)
+        put(weighed[1], (0,), 4, 1)
+        supply([(1, 6), (1, 7)], triples[1][0][:, PASS:], triples[1][1][:, PASS:], (6, 6), (7, 7))
+        h_last = sbuf("h_last", [3 * PASS], BF16, "y_mid")
+        hidden_on_gpsimd(h_last[:], *triples[1])
 
-        quantize_h(1, [(0, 5), (0, 6), (0, 7), (1, 5)])
-        quantize_h(5, [(1, 6), (1, 7)])
-        nc.scalar.copy(held[:, P:PASS], banks[5][:, P:PASS])
+        quantize_h(part(h_bf, 4, 3), [(0, 5), (0, 6), (0, 7)], "picked1")
+        quantize_h(h_last[:], [(1, 5), (1, 6), (1, 7)])
+        held = triples[1][0]
+        nc.scalar.copy(held[:, P:PASS], banks[4][:, P:PASS])
         for n in range(1, 4):
             put_fused(held[:, n * P : (n + 1) * P], n, 4, 1)
         for n in range(4):
-            bank = banks[(6 + n) % 8]
-            down_pass(bank, 0, n, 0, 5, 2, True, False)
-            down_pass(bank, 2 * P, n, 0, 7, 1, False, False)
-            down_pass(bank, 0, n, 1, 5, 1, False, False)
-            down_pass(bank, P, n, 1, 6, 2, False, True)
+            bank = banks[n]
+            for a in range(2):
+                down(bank, 0, n, a, 5, 2, a == 0, False)
+                down(bank, 2 * P, n, a, 7, 1, False, a == 1)
             y = ys[n % len(ys)][:, 0 : 3 * P]
             nc.scalar.copy(y, bank[:, 0 : 3 * P])
             put_fused(y, n, 5, 3)

@@ -13,12 +13,14 @@ U16 = mybir.dt.uint16
 U8 = mybir.dt.uint8
 FP8X4 = mybir.dt.float8_e4m3fn_x4
 MULT = mybir.AluOpType.mult
+MAX = mybir.AluOpType.max
 SIGMOID = mybir.ActivationFunctionType.Sigmoid
 
 P = 128
 PACK = 4
 PASS = P * PACK
 HALF = J // 2
+QUARTER = J // 4
 LOW, HIGH = slice(0, P // 2), slice(P // 2, P)
 
 
@@ -79,12 +81,14 @@ def tile_list_sigm_scat_kernel(
 
         for u in range(2):
             nc.vector.transpose(wgt_turned[:, 32 * u : 32 * u + 32], wgt_rows[:, 32 * u : 32 * u + 32])
-        by_block = wgt_turned[:].rearrange("p (u g c) -> p c u g", u=2, g=2)
+        by_block = wgt_turned[:].rearrange("p (b c) -> p c b", b=4)
         for q in range(4):
-            nc.scalar.copy(
-                wgt_wide[q][:].rearrange("p (c u g i) -> p c u g i", u=2, g=2, i=16),
-                by_block[:, 4 * q : 4 * q + 4, :, :].unsqueeze(4).to_broadcast([P, 4, 2, 2, 16]),
-            )
+            wide = wgt_wide[q][:].rearrange("p (c b i) -> p c b i", b=4, i=16)
+            narrow = by_block[:, 4 * q : 4 * q + 4, :].unsqueeze(3).to_broadcast([P, 4, 4, 16])
+            if q == 0:
+                nc.vector.tensor_tensor(wide, narrow, narrow, MAX)
+            else:
+                nc.scalar.copy(wide, narrow)
             nc.vector.transpose(wgt_sb[:, q * 256 : (q + 1) * 256], wgt_wide[q][:])
 
         x_bf = [sbuf(f"x_bf{h}", [HALF, PACK], BF16) for h in range(2)]
@@ -98,20 +102,18 @@ def tile_list_sigm_scat_kernel(
                 MULT,
             )
 
-        def weave_x(h, pr):
-            both = pairs_of_planes[pr][:].rearrange("p (e h c f) -> p h c e f", e=2, h=2, f=4)
-            nc.scalar.copy(x_bf[h][:, :, 2 * pr : 2 * pr + 2].rearrange("p (c f) e -> p c e f", f=4), both[:, h])
+        def weave_x(pr, first, count):
+            both = pairs_of_planes[pr][:].rearrange("p (e c f) -> p c e f", e=2, f=4)
+            dst = x_bf[first // HALF][:, first % HALF : first % HALF + count, 2 * pr : 2 * pr + 2]
+            nc.scalar.copy(dst.rearrange("p (c f) e -> p c e f", f=4), both[:, first // 4 : (first + count) // 4])
 
-        pick(0, 0, J)
-        for h in range(2):
-            pick(1, h * HALF, HALF)
-        for h in range(2):
-            weave_x(h, 0)
-        pick(2, 0, J)
-        for h in range(2):
-            pick(3, h * HALF, HALF)
-        for h in range(2):
-            weave_x(h, 1)
+        for pr, (even, odd) in enumerate(((HALF, HALF), (J, QUARTER))):
+            for first in range(0, J, even):
+                pick(2 * pr, first, even)
+            for first in range(0, J, odd):
+                pick(2 * pr + 1, first, odd)
+            for first in range(0, J, odd):
+                weave_x(pr, first, odd)
 
         def part(tile, first, count=1):
             return tile[:, first * PASS : (first + count) * PASS]
@@ -122,7 +124,7 @@ def tile_list_sigm_scat_kernel(
             nc.vector.quantize_mx(out=codes[:].bitcast(FP8X4), scales=scales[:], in_=src)
             return codes, scales
 
-        w_bf = {("u", 1, 1): part(h_bf, 2, 2), ("u", 1, 0): part(h_bf, 0, 2)}
+        w_bf = {("u", 1, 1): part(h_early, 1, 2), ("u", 1, 0): part(h_bf, 0, 2)}
         for key in (("g", 0, 0), ("g", 0, 1), ("u", 0, 0), ("u", 0, 1), ("g", 1, 0), ("g", 1, 1)):
             w_bf[key] = sbuf(f"w_bf{key[0]}{key[1]}{key[2]}", [2 * PASS], BF16)[:]
 
@@ -167,13 +169,19 @@ def tile_list_sigm_scat_kernel(
         def gate(a, s, dst, bank):
             nc.scalar.activation(woven(dst), first_product("g", a, s, bank), SIGMOID)
 
-        def hidden_on_vector(a, s, dst, sig, bank):
-            nc.vector.tensor_tensor(woven(dst), first_product("u", a, s, bank), woven(sig), MULT)
+        def hidden_on_vector(dst, up, sig):
+            nc.vector.tensor_tensor(woven(dst), up, woven(sig), MULT)
+
+        def lift(a, s, dst, bank):
+            nc.scalar.copy(woven(dst), first_product("u", a, s, bank))
 
         def supply(strips, gates, ups, gate_banks, up_banks):
             for k, (a, s) in enumerate(strips):
                 gate(a, s, part(gates, k), banks[gate_banks[k]])
-                nc.scalar.copy(woven(part(ups, k)), first_product("u", a, s, banks[up_banks[k]]))
+                lift(a, s, part(ups, k), banks[up_banks[k]])
+
+        def inputs(name, count, gate_tag=None, up_tag=None):
+            return sbuf(f"gates_{name}", [count * PASS], F32, gate_tag), sbuf(f"ups_{name}", [count * PASS], F32, up_tag)
 
         def hidden_on_gpsimd(dst, gates, ups):
             nc.gpsimd.tensor_tensor(dst, ups[:], gates[:], MULT)
@@ -222,67 +230,71 @@ def tile_list_sigm_scat_kernel(
         quantize_x(0, "rawg0")
         quantize_w("g", 0, 1)
         weave_w(on_scalar, "u", 0, 1, HIGH)
+        weave_w(on_scalar, "u", 0, 0)
         weave_w(on_vector, "u", 0, 1, LOW)
-        weave_w(on_vector, "u", 0, 0)
+        quantize_x(1, "w_bfg01")
         quantize_w("u", 0, 1)
-        quantize_w("u", 0, 0)
-        quantize_x(1, "rawu0")
-        early = sbuf("early", [2 * PASS], F32)
-        for s in range(2):
-            gate(0, s, part(early, s), banks[s])
-        weave_w(on_scalar, "g", 1, 1)
+        weave_w(on_scalar, "g", 1, 1, HIGH)
         weave_w(on_vector, "g", 1, 0)
-        late = sbuf("late", [4 * PASS], F32, "plane0")
-        hidden_on_vector(0, 0, part(h_early, 0), part(early, 0), banks[2])
+        weave_w(on_vector, "g", 1, 1, LOW)
+        quantize_w("u", 0, 0)
+        ups = {(0, s): first_product("u", 0, s, banks[2 + s]) for s in range(3)}
         quantize_w("g", 1, 0)
         quantize_w("g", 1, 1)
-        gate(0, 2, part(late, 0), banks[6])
-        gate(0, 3, part(late, 1), banks[7])
-        hidden_on_vector(0, 1, part(h_early, 1), part(early, 1), banks[3])
-        hidden_on_vector(0, 2, part(h_early, 2), part(late, 0), banks[4])
+        first_gate = sbuf("first_gate", [PASS], F32)
+        early = sbuf("early", [2 * PASS], F32, "rawg1")
+        late = sbuf("late", [3 * PASS], F32, "plane0")
+        gate(0, 0, first_gate[:], banks[0])
+        gate(0, 1, part(early, 0), banks[1])
         weave_w(on_scalar, "u", 1, 1, HIGH)
         weave_w(on_vector, "u", 1, 1, LOW)
         weave_w(on_vector, "u", 1, 0)
+        hidden_on_vector(part(h_early, 0), ups[0, 0], first_gate[:])
         quantize_w("u", 1, 1)
         quantize_w("u", 1, 0)
-        gate(1, 0, part(late, 2), banks[0])
-        gate(1, 1, part(late, 3), banks[1])
-        gate(1, 2, part(early, 0), banks[6])
-        quantize_h(h_early[:], [(0, 0), (0, 1), (0, 2)], "rawu1")
-        hidden_on_vector(0, 3, part(h_bf, 2), part(late, 1), banks[5])
-        hidden_on_vector(1, 0, part(h_bf, 5), part(late, 2), banks[2])
-        hidden_on_vector(1, 1, part(h_bf, 6), part(late, 3), banks[3])
+        pairs = [inputs("pair0", 2, "rawu1"), inputs("pair1", 2)]
+        gate(0, 2, part(early, 1), banks[6])
+        gate(1, 0, part(late, 0), banks[7])
+        ups[1, 0] = first_product("u", 1, 0, banks[5])
+        gate(0, 3, part(pairs[0][0], 0), banks[0])
+        gate(1, 1, part(late, 1), banks[6])
+        lift(0, 3, part(pairs[0][1], 0), banks[1])
+        gate(1, 2, part(late, 2), banks[7])
+        gate(0, 4, part(pairs[0][0], 1), banks[0])
+        lift(0, 4, part(pairs[0][1], 1), banks[1])
+        hidden_on_vector(part(h_early, 1), ups[0, 1], part(early, 0))
+        hidden_on_vector(part(h_early, 2), ups[0, 2], part(early, 1))
+        hidden_on_vector(part(h_bf, 5), ups[1, 0], part(late, 0))
+        quantize_h(h_early[:], [(0, 0), (0, 1), (0, 2)])
         down_chunk(banks[6], 0, 0)
         quantize_h(part(h_bf, 5), [(1, 0)])
         down_chunk(banks[6], 0, 1)
+        hidden_on_vector(part(h_bf, 6), first_product("u", 1, 1, banks[2]), part(late, 1))
+        hidden_on_vector(part(h_bf, 2), first_product("u", 1, 2, banks[3]), part(late, 2))
         quantize_h(part(h_bf, 6), [(1, 1)])
-        hidden_on_vector(1, 2, part(h_bf, 3), part(early, 0), banks[4])
 
-        def inputs(name, count, gate_tag=None, up_tag=None):
-            return sbuf(f"gates_{name}", [count * PASS], F32, gate_tag), sbuf(f"ups_{name}", [count * PASS], F32, up_tag)
-
-        pair = inputs("pair", 2)
-        single = inputs("single", 1)
         triples = [inputs(f"triple{b}", 3, f"plane{1 + b}", f"picked{b}") for b in range(2)]
         weighed = [sbuf(f"weighed{b}", [PASS], F32) for b in range(3)]
         ys = [sbuf(f"y{b}", [PASS], F32) for b in range(3)]
 
-        supply([(0, 4)], *single, (7,), (0,))
-        for a in range(2):
-            down_chunk(banks[7], 1, a)
+        for bank, rows in ((banks[7], (0, 1)), (banks[3], (2, 3))):
+            for a in range(2):
+                for k, n in enumerate(rows):
+                    down(bank, k * P, n, a, 1, 1, a == 0 and k == 0, a == 1 and k == 1)
         weigh(nc.vector, weighed[0][:, 0:P], banks[6][:, 0:P], 1, 0, 1)
         weigh(nc.vector, weighed[0][:, P:PASS], banks[6][:, P:PASS], 3, 0, 1)
-        put(weighed[0], range(4), 0, 1)
-        hidden_on_gpsimd(part(h_bf, 6), *single)
-        nc.scalar.copy(ys[0][:], banks[7][:])
-        weigh(nc.gpsimd, weighed[1][:, 0 : 2 * P], ys[0][:, 0 : 2 * P], 2, 1, 1)
+        put(weighed[0], range(3), 0, 1)
+        weigh(nc.vector, weighed[1][:, 0 : 2 * P], banks[7][:, 0 : 2 * P], 2, 1, 1)
+        put(weighed[0][:, 3 * P : PASS], (3,), 0, 1)
         put(weighed[1], (0, 1), 1, 1)
-        supply([(1, 3), (1, 4)], *pair, (1, 0), (5, 4))
-        hidden_on_gpsimd(part(h_bf, 4, 2), *pair)
-        weigh(nc.gpsimd, pair[0][:, 0 : 2 * P], ys[0][:, 2 * P : PASS], 2, 1, 1)
+        hidden_on_gpsimd(part(h_bf, 5, 2), *pairs[0])
+        supply([(1, 3), (1, 4)], *pairs[1], (0, 1), (4, 5))
+        hidden_on_gpsimd(part(h_bf, 3, 2), *pairs[1])
+        nc.scalar.copy(ys[0][:, 0 : 2 * P], banks[3][:, 0 : 2 * P])
+        weigh(nc.gpsimd, pairs[1][0][:, 0 : 2 * P], ys[0][:, 0 : 2 * P], 2, 1, 1)
 
-        quantize_h(part(h_bf, 2, 4), [(0, 3), (1, 2), (1, 3), (1, 4)])
-        quantize_h(part(h_bf, 6), [(0, 4)], "ups_pair")
+        quantize_h(part(h_bf, 2, 3), [(1, 2), (1, 3), (1, 4)])
+        quantize_h(part(h_bf, 5, 2), [(0, 3), (0, 4)], "ups_pair1")
 
         def down_double(bank, rows):
             for k, n in enumerate(rows):
@@ -290,26 +302,26 @@ def tile_list_sigm_scat_kernel(
                 down(bank, k * 2 * P, n, 0, 2, 1, False, False)
                 down(bank, k * 2 * P + P, n, 0, 3, 1, False, k == 1)
 
-        down_double(banks[0], (0, 1))
-        supply([(0, 5), (0, 6), (0, 7)], *triples[0], (6, 5, 6), (7, 4, 7))
-        supply([(1, 5)], *triples[1], (5,), (4,))
-        down_double(banks[5], (2, 3))
-        put(pair[0], (2, 3), 1, 1)
+        down_double(banks[7], (0, 1))
+        supply([(0, 5), (0, 6), (0, 7)], *triples[0], (0, 1, 6), (4, 5, 3))
+        supply([(1, 5)], *triples[1], (0,), (4,))
+        down_double(banks[0], (2, 3))
+        put(pairs[1][0], (2, 3), 1, 1)
         for a in range(2):
             down_chunk(banks[4], 4, a)
         for k in range(2):
             cols = slice(k * 2 * P, (k + 1) * 2 * P)
-            weigh(nc.vector, weighed[0][:, cols], banks[0][:, cols], 1, 2, 2)
+            weigh(nc.vector, weighed[0][:, cols], banks[7][:, cols], 1, 2, 2)
         put(weighed[0], (0, 1), 2, 2)
         hidden_on_gpsimd(part(h_bf, 4, 3), *triples[0])
         y_mid = sbuf("y_mid", [PASS + P], F32)
-        nc.scalar.copy(y_mid[:, 0:PASS], banks[5][:])
+        nc.scalar.copy(y_mid[:, 0:PASS], banks[0][:])
         weigh(nc.gpsimd, weighed[2][:], y_mid[:, 0:PASS], 2, 2, 2)
         put(weighed[2], (2, 3), 2, 2)
         nc.scalar.copy(y_mid[:, PASS : PASS + P], banks[4][:, 0:P])
         weigh(nc.gpsimd, weighed[1][:, 0:P], y_mid[:, PASS : PASS + P], 1, 4, 1)
         put(weighed[1], (0,), 4, 1)
-        supply([(1, 6), (1, 7)], triples[1][0][:, PASS:], triples[1][1][:, PASS:], (6, 6), (7, 7))
+        supply([(1, 6), (1, 7)], triples[1][0][:, PASS:], triples[1][1][:, PASS:], (1, 6), (5, 3))
         h_last = sbuf("h_last", [3 * PASS], BF16, "y_mid")
         hidden_on_gpsimd(h_last[:], *triples[1])
 
@@ -320,7 +332,7 @@ def tile_list_sigm_scat_kernel(
         for n in range(1, 4):
             put_fused(held[:, n * P : (n + 1) * P], n, 4, 1)
         for n in range(4):
-            bank = banks[n]
+            bank = banks[(1, 2, 3, 5)[n]]
             for a in range(2):
                 down(bank, 0, n, a, 5, 2, a == 0, False)
                 down(bank, 2 * P, n, a, 7, 1, False, a == 1)

@@ -13,14 +13,12 @@ U16 = mybir.dt.uint16
 U8 = mybir.dt.uint8
 FP8X4 = mybir.dt.float8_e4m3fn_x4
 MULT = mybir.AluOpType.mult
-MAX = mybir.AluOpType.max
 SIGMOID = mybir.ActivationFunctionType.Sigmoid
 
 P = 128
 PACK = 4
 PASS = P * PACK
 HALF = J // 2
-QUARTER = J // 4
 LOW, HIGH = slice(0, P // 2), slice(P // 2, P)
 
 
@@ -43,14 +41,16 @@ def tile_list_sigm_scat_kernel(
         wgt_turned = sbuf("wgt_turned", [64], F32)
         wgt_wide = [sbuf(f"wgt_wide{q}", [J // 4], F32) for q in range(4)]
         wgo_sb = sbuf("wgo_sb", [J], F32)
-        w_raw = {(w, a): sbuf(f"raw{w}{a}", [PACK, PASS], F32) for w in "gu" for a in range(2)}
+        g_raw = sbuf("rawg", [PACK, R], F32)
+        w_raw = {("g", a): g_raw[:, :, a * PASS : (a + 1) * PASS] for a in range(2)}
+        w_raw.update({("u", a): sbuf(f"rawu{a}", [PACK, PASS], F32)[:] for a in range(2)})
         wd_codes = sbuf("wd_codes", [2, N], U32)
         wd_sc = sbuf("wd_sc", [2, N], U8)
         pages = [sbuf(f"page{n}", [T], F32) for n in range(4)]
         warm = sbuf("warm", [8], F32)
         warm_out = sbuf("warm_out", [8], F32)
         banks = [psum.tile([P, PASS], F32, name=f"bank{b}") for b in range(8)]
-        h_early = sbuf("h_early", [3 * PASS], BF16)
+        h_early = sbuf("h_early", [2 * PASS], BF16)
         h_bf = sbuf("h_bf", [7 * PASS], BF16)
 
         x_rows = xT.rearrange("(p i) t -> p i t", i=PACK)
@@ -67,9 +67,9 @@ def tile_list_sigm_scat_kernel(
         nc.sync.dma_start(pick_list[:], offs)
         for i in range(PACK):
             nc.sync.dma_start(planes[i][:], x_rows[:, i, :])
+        nc.sync.dma_start(g_raw[:], w_rows["g"])
         for a in range(2):
-            for w in "gu":
-                nc.sync.dma_start(w_raw[w, a][:], w_rows[w][:, :, a * PASS : (a + 1) * PASS])
+            nc.sync.dma_start(w_raw["u", a], w_rows["u"][:, :, a * PASS : (a + 1) * PASS])
         sc_rows = wd_scales.bitcast(I32).rearrange("a q n -> q a n")
         for quad in range(4):
             nc.sync.dma_start(
@@ -85,10 +85,7 @@ def tile_list_sigm_scat_kernel(
         for q in range(4):
             wide = wgt_wide[q][:].rearrange("p (c b i) -> p c b i", b=4, i=16)
             narrow = by_block[:, 4 * q : 4 * q + 4, :].unsqueeze(3).to_broadcast([P, 4, 4, 16])
-            if q == 0:
-                nc.vector.tensor_tensor(wide, narrow, narrow, MAX)
-            else:
-                nc.scalar.copy(wide, narrow)
+            nc.scalar.copy(wide, narrow)
             nc.vector.transpose(wgt_sb[:, q * 256 : (q + 1) * 256], wgt_wide[q][:])
 
         x_bf = [sbuf(f"x_bf{h}", [HALF, PACK], BF16) for h in range(2)]
@@ -102,18 +99,20 @@ def tile_list_sigm_scat_kernel(
                 MULT,
             )
 
-        def weave_x(pr, first, count):
-            both = pairs_of_planes[pr][:].rearrange("p (e c f) -> p c e f", e=2, f=4)
-            dst = x_bf[first // HALF][:, first % HALF : first % HALF + count, 2 * pr : 2 * pr + 2]
-            nc.scalar.copy(dst.rearrange("p (c f) e -> p c e f", f=4), both[:, first // 4 : (first + count) // 4])
+        def weave_x(copy, pr, h, c=slice(0, P)):
+            both = pairs_of_planes[pr][:].rearrange("p (e h c f) -> p h c e f", e=2, h=2, f=4)
+            copy(x_bf[h][:, :, 2 * pr : 2 * pr + 2].rearrange("p (c f) e -> p c e f", f=4)[:, c], both[:, h, c])
 
-        for pr, (even, odd) in enumerate(((HALF, HALF), (J, QUARTER))):
-            for first in range(0, J, even):
-                pick(2 * pr, first, even)
-            for first in range(0, J, odd):
-                pick(2 * pr + 1, first, odd)
-            for first in range(0, J, odd):
-                weave_x(pr, first, odd)
+        pick(0, 0, J)
+        pick(1, 0, J)
+        for h in range(2):
+            weave_x(nc.scalar.copy, 0, h)
+        pick(2, 0, J)
+        for h in range(2):
+            pick(3, h * HALF, HALF)
+        weave_x(nc.scalar.copy, 1, 0)
+        weave_x(nc.scalar.copy, 1, 1, LOW)
+        weave_x(nc.vector.tensor_copy, 1, 1, HIGH)
 
         def part(tile, first, count=1):
             return tile[:, first * PASS : (first + count) * PASS]
@@ -124,13 +123,13 @@ def tile_list_sigm_scat_kernel(
             nc.vector.quantize_mx(out=codes[:].bitcast(FP8X4), scales=scales[:], in_=src)
             return codes, scales
 
-        w_bf = {("u", 1, 1): part(h_early, 1, 2), ("u", 1, 0): part(h_bf, 0, 2)}
+        w_bf = {("u", 1, 1): h_early[:], ("u", 1, 0): part(h_bf, 0, 2)}
         for key in (("g", 0, 0), ("g", 0, 1), ("u", 0, 0), ("u", 0, 1), ("g", 1, 0), ("g", 1, 1)):
             w_bf[key] = sbuf(f"w_bf{key[0]}{key[1]}{key[2]}", [2 * PASS], BF16)[:]
 
         def weave_w(copy, w, a, tp, m=slice(0, P)):
             dst = w_bf[w, a, tp].rearrange("p (t m i) -> p m i t", t=2, i=PACK)[:, m, :, :]
-            src = w_raw[w, a][:].rearrange("p i (m t) -> p m i t", t=PACK)[:, m, :, 2 * tp : 2 * tp + 2]
+            src = w_raw[w, a].rearrange("p i (m t) -> p m i t", t=PACK)[:, m, :, 2 * tp : 2 * tp + 2]
             copy(dst, src)
 
         on_vector, on_scalar = nc.vector.tensor_copy, nc.scalar.copy
@@ -224,118 +223,118 @@ def tile_list_sigm_scat_kernel(
         def put_fused(y, n, s, count):
             nc.vector.tensor_tensor(places(n, s, count), y, wgo_sb[:, s * P : (s + count) * P], MULT)
 
+        quantize_x(0)
+        weave_w(on_scalar, "g", 1, 0)
+        weave_w(on_scalar, "g", 1, 1)
         weave_w(on_vector, "g", 0, 0)
         weave_w(on_vector, "g", 0, 1)
         quantize_w("g", 0, 0)
-        quantize_x(0, "rawg0")
+        quantize_x(1, "w_bfg00")
         quantize_w("g", 0, 1)
-        weave_w(on_scalar, "u", 0, 1, HIGH)
-        weave_w(on_scalar, "u", 0, 0)
-        weave_w(on_vector, "u", 0, 1, LOW)
-        quantize_x(1, "w_bfg01")
-        quantize_w("u", 0, 1)
-        weave_w(on_scalar, "g", 1, 1, HIGH)
-        weave_w(on_vector, "g", 1, 0)
-        weave_w(on_vector, "g", 1, 1, LOW)
-        quantize_w("u", 0, 0)
-        ups = {(0, s): first_product("u", 0, s, banks[2 + s]) for s in range(3)}
         quantize_w("g", 1, 0)
+        weave_w(on_scalar, "u", 0, 1, HIGH)
+        weave_w(on_vector, "u", 0, 1, LOW)
         quantize_w("g", 1, 1)
-        first_gate = sbuf("first_gate", [PASS], F32)
-        early = sbuf("early", [2 * PASS], F32, "rawg1")
-        late = sbuf("late", [3 * PASS], F32, "plane0")
-        gate(0, 0, first_gate[:], banks[0])
-        gate(0, 1, part(early, 0), banks[1])
+        weave_w(on_vector, "u", 0, 0)
+        quantize_w("u", 0, 1)
+        quantize_w("u", 0, 0)
+        early = sbuf("early", [3 * PASS], F32, "w_bfg10")
+        late = sbuf("late", [3 * PASS], F32, "rawu1")
+        pairs = [inputs("pair0", 2, "w_bfu00"), inputs("pair1", 2)]
+        gate(0, 0, part(early, 0), banks[0])
+        gate(0, 1, part(early, 1), banks[1])
+        gate(1, 0, part(early, 2), banks[6])
+        ups = {(0, s): first_product("u", 0, s, banks[2 + s]) for s in range(3)}
         weave_w(on_scalar, "u", 1, 1, HIGH)
         weave_w(on_vector, "u", 1, 1, LOW)
         weave_w(on_vector, "u", 1, 0)
-        hidden_on_vector(part(h_early, 0), ups[0, 0], first_gate[:])
         quantize_w("u", 1, 1)
         quantize_w("u", 1, 0)
-        pairs = [inputs("pair0", 2, "rawu1"), inputs("pair1", 2)]
-        gate(0, 2, part(early, 1), banks[6])
-        gate(1, 0, part(late, 0), banks[7])
+        gate(1, 1, part(late, 0), banks[7])
         ups[1, 0] = first_product("u", 1, 0, banks[5])
-        gate(0, 3, part(pairs[0][0], 0), banks[0])
-        gate(1, 1, part(late, 1), banks[6])
-        lift(0, 3, part(pairs[0][1], 0), banks[1])
-        gate(1, 2, part(late, 2), banks[7])
-        gate(0, 4, part(pairs[0][0], 1), banks[0])
-        lift(0, 4, part(pairs[0][1], 1), banks[1])
-        hidden_on_vector(part(h_early, 1), ups[0, 1], part(early, 0))
-        hidden_on_vector(part(h_early, 2), ups[0, 2], part(early, 1))
-        hidden_on_vector(part(h_bf, 5), ups[1, 0], part(late, 0))
-        quantize_h(h_early[:], [(0, 0), (0, 1), (0, 2)])
-        down_chunk(banks[6], 0, 0)
+        hidden_on_vector(part(h_early, 0), ups[0, 0], part(early, 0))
+        hidden_on_vector(part(h_early, 1), ups[0, 1], part(early, 1))
+        ups[1, 1] = first_product("u", 1, 1, banks[2])
+        gate(0, 2, part(late, 1), banks[0])
+        supply([(0, 3), (0, 4)], *pairs[0], (1, 7), (6, 0))
+        hidden_on_vector(part(h_bf, 5), ups[1, 0], part(early, 2))
+        quantize_h(h_early[:], [(0, 0), (0, 1)])
+        down_chunk(banks[1], 0, 0)
         quantize_h(part(h_bf, 5), [(1, 0)])
-        down_chunk(banks[6], 0, 1)
-        hidden_on_vector(part(h_bf, 6), first_product("u", 1, 1, banks[2]), part(late, 1))
-        hidden_on_vector(part(h_bf, 2), first_product("u", 1, 2, banks[3]), part(late, 2))
+        down_chunk(banks[1], 0, 1)
+        hidden_on_vector(part(h_bf, 6), ups[1, 1], part(late, 0))
+        hidden_on_vector(part(h_bf, 4), ups[0, 2], part(late, 1))
         quantize_h(part(h_bf, 6), [(1, 1)])
+        gate(1, 2, part(late, 2), banks[6])
+        ups[1, 2] = first_product("u", 1, 2, banks[3])
 
         triples = [inputs(f"triple{b}", 3, f"plane{1 + b}", f"picked{b}") for b in range(2)]
         weighed = [sbuf(f"weighed{b}", [PASS], F32) for b in range(3)]
         ys = [sbuf(f"y{b}", [PASS], F32) for b in range(3)]
 
-        for bank, rows in ((banks[7], (0, 1)), (banks[3], (2, 3))):
+        for bank, rows in ((banks[7], (0, 1)), (banks[5], (2, 3))):
             for a in range(2):
                 for k, n in enumerate(rows):
-                    down(bank, k * P, n, a, 1, 1, a == 0 and k == 0, a == 1 and k == 1)
-        weigh(nc.vector, weighed[0][:, 0:P], banks[6][:, 0:P], 1, 0, 1)
-        weigh(nc.vector, weighed[0][:, P:PASS], banks[6][:, P:PASS], 3, 0, 1)
-        put(weighed[0], range(3), 0, 1)
-        weigh(nc.vector, weighed[1][:, 0 : 2 * P], banks[7][:, 0 : 2 * P], 2, 1, 1)
-        put(weighed[0][:, 3 * P : PASS], (3,), 0, 1)
-        put(weighed[1], (0, 1), 1, 1)
+                    down(bank, k * P, n, 1 - a, 1, 1, a == 0 and k == 0, a == 1 and k == 1)
+        weigh(nc.vector, weighed[0][:, 0:P], banks[1][:, 0:P], 1, 0, 1)
+        weigh(nc.vector, weighed[0][:, P:PASS], banks[1][:, P:PASS], 3, 0, 1)
+        hidden_on_vector(part(h_bf, 3), ups[1, 2], part(late, 2))
+        put(weighed[0], range(4), 0, 1)
         hidden_on_gpsimd(part(h_bf, 5, 2), *pairs[0])
-        supply([(1, 3), (1, 4)], *pairs[1], (0, 1), (4, 5))
-        hidden_on_gpsimd(part(h_bf, 3, 2), *pairs[1])
-        nc.scalar.copy(ys[0][:, 0 : 2 * P], banks[3][:, 0 : 2 * P])
+        y_early = sbuf("y_early", [2 * P], F32)
+        nc.scalar.copy(y_early[:], banks[7][:, 0 : 2 * P])
+        weigh(nc.gpsimd, weighed[1][:, 0 : 2 * P], y_early[:], 2, 1, 1)
+        put(weighed[1], (0, 1), 1, 1)
+        supply([(1, 3), (1, 4)], *pairs[1], (0, 4), (2, 6))
+        h_pair = sbuf("h_pair", [2 * PASS], BF16, "y_early")
+        hidden_on_gpsimd(h_pair[:], *pairs[1])
+        nc.scalar.copy(ys[0][:, 0 : 2 * P], banks[5][:, 0 : 2 * P])
         weigh(nc.gpsimd, pairs[1][0][:, 0 : 2 * P], ys[0][:, 0 : 2 * P], 2, 1, 1)
 
-        quantize_h(part(h_bf, 2, 3), [(1, 2), (1, 3), (1, 4)])
-        quantize_h(part(h_bf, 5, 2), [(0, 3), (0, 4)], "ups_pair1")
+        quantize_h(h_pair[:], [(1, 3), (1, 4)])
+        quantize_h(part(h_bf, 3, 4), [(1, 2), (0, 2), (0, 3), (0, 4)], "ups_pair1")
 
         def down_double(bank, rows):
             for k, n in enumerate(rows):
-                down(bank, k * 2 * P, n, 1, 2, 2, k == 0, False)
-                down(bank, k * 2 * P, n, 0, 2, 1, False, False)
-                down(bank, k * 2 * P + P, n, 0, 3, 1, False, k == 1)
+                down(bank, k * 2 * P, n, 0, 2, 2, k == 0, False)
+                down(bank, k * 2 * P, n, 1, 2, 1, False, False)
+                down(bank, k * 2 * P + P, n, 1, 3, 1, False, k == 1)
 
-        down_double(banks[7], (0, 1))
-        supply([(0, 5), (0, 6), (0, 7)], *triples[0], (0, 1, 6), (4, 5, 3))
-        supply([(1, 5)], *triples[1], (0,), (4,))
+        supply([(0, 5), (0, 6), (0, 7)], *triples[0], (0, 4, 0), (2, 6, 2))
+        supply([(1, 5), (1, 6)], *triples[1], (4, 0), (6, 2))
+        gate(1, 7, part(triples[1][0], 2), banks[4])
+        down_double(banks[6], (0, 1))
         down_double(banks[0], (2, 3))
         put(pairs[1][0], (2, 3), 1, 1)
         for a in range(2):
-            down_chunk(banks[4], 4, a)
+            down_chunk(banks[2], 4, a)
         for k in range(2):
             cols = slice(k * 2 * P, (k + 1) * 2 * P)
-            weigh(nc.vector, weighed[0][:, cols], banks[7][:, cols], 1, 2, 2)
+            weigh(nc.vector, weighed[0][:, cols], banks[6][:, cols], 1, 2, 2)
         put(weighed[0], (0, 1), 2, 2)
         hidden_on_gpsimd(part(h_bf, 4, 3), *triples[0])
         y_mid = sbuf("y_mid", [PASS + P], F32)
         nc.scalar.copy(y_mid[:, 0:PASS], banks[0][:])
         weigh(nc.gpsimd, weighed[2][:], y_mid[:, 0:PASS], 2, 2, 2)
         put(weighed[2], (2, 3), 2, 2)
-        nc.scalar.copy(y_mid[:, PASS : PASS + P], banks[4][:, 0:P])
+        nc.scalar.copy(y_mid[:, PASS : PASS + P], banks[2][:, 0:P])
         weigh(nc.gpsimd, weighed[1][:, 0:P], y_mid[:, PASS : PASS + P], 1, 4, 1)
         put(weighed[1], (0,), 4, 1)
-        supply([(1, 6), (1, 7)], triples[1][0][:, PASS:], triples[1][1][:, PASS:], (1, 6), (5, 3))
+        lift(1, 7, part(triples[1][1], 2), banks[6])
         h_last = sbuf("h_last", [3 * PASS], BF16, "y_mid")
         hidden_on_gpsimd(h_last[:], *triples[1])
 
         quantize_h(part(h_bf, 4, 3), [(0, 5), (0, 6), (0, 7)], "picked1")
         quantize_h(h_last[:], [(1, 5), (1, 6), (1, 7)])
         held = triples[1][0]
-        nc.scalar.copy(held[:, P:PASS], banks[4][:, P:PASS])
+        nc.scalar.copy(held[:, P:PASS], banks[2][:, P:PASS])
         for n in range(1, 4):
             put_fused(held[:, n * P : (n + 1) * P], n, 4, 1)
         for n in range(4):
-            bank = banks[(1, 2, 3, 5)[n]]
-            for a in range(2):
-                down(bank, 0, n, a, 5, 2, a == 0, False)
-                down(bank, 2 * P, n, a, 7, 1, False, a == 1)
+            bank = banks[(1, 3, 5, 7)[n]]
+            for step, a in enumerate((0, 1) if n == 0 else (1, 0)):
+                down(bank, 0, n, a, 5, 2, step == 0, False)
+                down(bank, 2 * P, n, a, 7, 1, False, step == 1)
             y = ys[n % len(ys)][:, 0 : 3 * P]
             nc.scalar.copy(y, bank[:, 0 : 3 * P])
             put_fused(y, n, 5, 3)

@@ -110,9 +110,9 @@ def tile_list_sigm_scat_kernel(
         pick(2, 0, J)
         for h in range(2):
             pick(3, h * HALF, HALF)
-        weave_x(nc.scalar.copy, 1, 0)
-        weave_x(nc.scalar.copy, 1, 1, LOW)
-        weave_x(nc.vector.tensor_copy, 1, 1, HIGH)
+        for h in range(2):
+            weave_x(nc.scalar.copy, 1, h, LOW)
+            weave_x(nc.vector.tensor_copy, 1, h, HIGH)
 
         def part(tile, first, count=1):
             return tile[:, first * PASS : (first + count) * PASS]
@@ -123,7 +123,7 @@ def tile_list_sigm_scat_kernel(
             nc.vector.quantize_mx(out=codes[:].bitcast(FP8X4), scales=scales[:], in_=src)
             return codes, scales
 
-        w_bf = {("u", 1, 1): h_early[:], ("u", 1, 0): part(h_bf, 0, 2)}
+        w_bf = {("u", 1, 0): h_early[:], ("u", 1, 1): part(h_bf, 0, 2)}
         for key in (("g", 0, 0), ("g", 0, 1), ("u", 0, 0), ("u", 0, 1), ("g", 1, 0), ("g", 1, 1)):
             w_bf[key] = sbuf(f"w_bf{key[0]}{key[1]}{key[2]}", [2 * PASS], BF16)[:]
 
@@ -232,24 +232,23 @@ def tile_list_sigm_scat_kernel(
         quantize_x(1, "w_bfg00")
         quantize_w("g", 0, 1)
         quantize_w("g", 1, 0)
-        weave_w(on_scalar, "u", 0, 1, HIGH)
-        weave_w(on_vector, "u", 0, 1, LOW)
-        quantize_w("g", 1, 1)
+        weave_w(on_scalar, "u", 0, 1)
         weave_w(on_vector, "u", 0, 0)
-        quantize_w("u", 0, 1)
+        quantize_w("g", 1, 1)
         quantize_w("u", 0, 0)
+        quantize_w("u", 0, 1)
         early = sbuf("early", [3 * PASS], F32, "w_bfg10")
         late = sbuf("late", [3 * PASS], F32, "rawu1")
         pairs = [inputs("pair0", 2, "w_bfu00"), inputs("pair1", 2)]
         gate(0, 0, part(early, 0), banks[0])
         gate(0, 1, part(early, 1), banks[1])
-        gate(1, 0, part(early, 2), banks[6])
         ups = {(0, s): first_product("u", 0, s, banks[2 + s]) for s in range(3)}
         weave_w(on_scalar, "u", 1, 1, HIGH)
-        weave_w(on_vector, "u", 1, 1, LOW)
+        gate(1, 0, part(early, 2), banks[6])
         weave_w(on_vector, "u", 1, 0)
-        quantize_w("u", 1, 1)
+        weave_w(on_vector, "u", 1, 1, LOW)
         quantize_w("u", 1, 0)
+        quantize_w("u", 1, 1)
         gate(1, 1, part(late, 0), banks[7])
         ups[1, 0] = first_product("u", 1, 0, banks[5])
         hidden_on_vector(part(h_early, 0), ups[0, 0], part(early, 0))
@@ -258,6 +257,7 @@ def tile_list_sigm_scat_kernel(
         gate(0, 2, part(late, 1), banks[0])
         supply([(0, 3), (0, 4)], *pairs[0], (1, 7), (6, 0))
         hidden_on_vector(part(h_bf, 5), ups[1, 0], part(early, 2))
+        gate(1, 2, part(late, 2), banks[5])
         quantize_h(h_early[:], [(0, 0), (0, 1)])
         down_chunk(banks[1], 0, 0)
         quantize_h(part(h_bf, 5), [(1, 0)])
@@ -265,7 +265,6 @@ def tile_list_sigm_scat_kernel(
         hidden_on_vector(part(h_bf, 6), ups[1, 1], part(late, 0))
         hidden_on_vector(part(h_bf, 4), ups[0, 2], part(late, 1))
         quantize_h(part(h_bf, 6), [(1, 1)])
-        gate(1, 2, part(late, 2), banks[6])
         ups[1, 2] = first_product("u", 1, 2, banks[3])
 
         triples = [inputs(f"triple{b}", 3, f"plane{1 + b}", f"picked{b}") for b in range(2)]
@@ -285,7 +284,7 @@ def tile_list_sigm_scat_kernel(
         nc.scalar.copy(y_early[:], banks[7][:, 0 : 2 * P])
         weigh(nc.gpsimd, weighed[1][:, 0 : 2 * P], y_early[:], 2, 1, 1)
         put(weighed[1], (0, 1), 1, 1)
-        supply([(1, 3), (1, 4)], *pairs[1], (0, 4), (2, 6))
+        supply([(1, 3), (1, 4)], *pairs[1], (6, 0), (2, 4))
         h_pair = sbuf("h_pair", [2 * PASS], BF16, "y_early")
         hidden_on_gpsimd(h_pair[:], *pairs[1])
         nc.scalar.copy(ys[0][:, 0 : 2 * P], banks[5][:, 0 : 2 * P])
@@ -300,27 +299,27 @@ def tile_list_sigm_scat_kernel(
                 down(bank, k * 2 * P, n, 1, 2, 1, False, False)
                 down(bank, k * 2 * P + P, n, 1, 3, 1, False, k == 1)
 
-        supply([(0, 5), (0, 6), (0, 7)], *triples[0], (0, 4, 0), (2, 6, 2))
-        supply([(1, 5), (1, 6)], *triples[1], (4, 0), (6, 2))
-        gate(1, 7, part(triples[1][0], 2), banks[4])
-        down_double(banks[6], (0, 1))
-        down_double(banks[0], (2, 3))
+        supply([(0, 5), (0, 6), (0, 7)], *triples[0], (6, 0, 6), (2, 4, 2))
+        supply([(1, 5), (1, 6)], *triples[1], (0, 6), (4, 2))
+        gate(1, 7, part(triples[1][0], 2), banks[0])
+        down_double(banks[4], (0, 1))
+        down_double(banks[6], (2, 3))
         put(pairs[1][0], (2, 3), 1, 1)
         for a in range(2):
             down_chunk(banks[2], 4, a)
         for k in range(2):
             cols = slice(k * 2 * P, (k + 1) * 2 * P)
-            weigh(nc.vector, weighed[0][:, cols], banks[6][:, cols], 1, 2, 2)
+            weigh(nc.vector, weighed[0][:, cols], banks[4][:, cols], 1, 2, 2)
         put(weighed[0], (0, 1), 2, 2)
         hidden_on_gpsimd(part(h_bf, 4, 3), *triples[0])
         y_mid = sbuf("y_mid", [PASS + P], F32)
-        nc.scalar.copy(y_mid[:, 0:PASS], banks[0][:])
+        nc.scalar.copy(y_mid[:, 0:PASS], banks[6][:])
         weigh(nc.gpsimd, weighed[2][:], y_mid[:, 0:PASS], 2, 2, 2)
         put(weighed[2], (2, 3), 2, 2)
         nc.scalar.copy(y_mid[:, PASS : PASS + P], banks[2][:, 0:P])
         weigh(nc.gpsimd, weighed[1][:, 0:P], y_mid[:, PASS : PASS + P], 1, 4, 1)
         put(weighed[1], (0,), 4, 1)
-        lift(1, 7, part(triples[1][1], 2), banks[6])
+        lift(1, 7, part(triples[1][1], 2), banks[4])
         h_last = sbuf("h_last", [3 * PASS], BF16, "y_mid")
         hidden_on_gpsimd(h_last[:], *triples[1])
 

from contextlib import ExitStack

import concourse.mybir as mybir

K, R, N, T, J = 512, 1024, 512, 2048, 1024
FLOPS = 2 * K * R * J * 2 + 2 * R * N * J

F32 = mybir.dt.float32
BF16 = mybir.dt.bfloat16
I32 = mybir.dt.int32
U32 = mybir.dt.uint32
U16 = mybir.dt.uint16
U8 = mybir.dt.uint8
FP8X4 = mybir.dt.float8_e4m3fn_x4
MULT = mybir.AluOpType.mult
SIGMOID = mybir.ActivationFunctionType.Sigmoid

P = 128
PACK = 4
PASS = P * PACK
HALF = J // 2
LOW, HIGH = slice(0, P // 2), slice(P // 2, P)


def tile_list_sigm_scat_kernel(
    tc, xT, wgt, wg, wu, wd_words, wd_scales, wgo, offs, offs2, out
):
    nc = tc.nc
    with ExitStack() as ctx:
        keep = ctx.enter_context(tc.tile_pool(name="keep", bufs=1))
        psum = ctx.enter_context(tc.psum_pool(name="psum", bufs=1))

        def sbuf(name, shape, dtype, tag=None):
            return keep.tile([P] + shape, dtype, name=name, tag=tag or name, align_bytes=64)

        pick_list = keep.tile([P, J // 16], U16, name="pick_list")
        put_list = keep.tile([P, J // 16], U16, name="put_list")
        planes = [sbuf(f"plane{i}", [T], F32) for i in range(PACK)]
        wgt_sb = sbuf("wgt_sb", [J], F32)
        wgt_rows = sbuf("wgt_rows", [64], F32)
        wgt_turned = sbuf("wgt_turned", [64], F32)
        wgt_wide = [sbuf(f"wgt_wide{q}", [J // 4], F32) for q in range(4)]
        wgo_sb = sbuf("wgo_sb", [J], F32)
        g_raw = sbuf("rawg", [PACK, R], F32)
        w_raw = {("g", a): g_raw[:, :, a * PASS : (a + 1) * PASS] for a in range(2)}
        w_raw.update({("u", a): sbuf(f"rawu{a}", [PACK, PASS], F32)[:] for a in range(2)})
        wd_codes = sbuf("wd_codes", [2, N], U32)
        wd_sc = sbuf("wd_sc", [2, N], U8)
        pages = [sbuf(f"page{n}", [T], F32) for n in range(4)]
        warm = sbuf("warm", [8], F32)
        warm_out = sbuf("warm_out", [8], F32)
        banks = [psum.tile([P, PASS], F32, name=f"bank{b}") for b in range(8)]
        h_early = sbuf("h_early", [2 * PASS], BF16)
        h_bf = sbuf("h_bf", [7 * PASS], BF16)

        x_rows = xT.rearrange("(p i) t -> p i t", i=PACK)
        w_rows = {"g": wg.rearrange("(p i) r -> p i r", i=PACK), "u": wu.rearrange("(p i) r -> p i r", i=PACK)}

        nc.gpsimd.memset(warm[:], 0.0)
        nc.scalar.activation(warm_out[:], warm[:], SIGMOID)
        nc.gpsimd.memset(wd_sc[:].rearrange("p a n -> p (a n)").bitcast(U32), 0)
        for page in pages:
            nc.gpsimd.memset(page[:], 0.0)

        half_rows = wgt.rearrange("p (h e) -> (p h) e", h=2)[0 : 2 * P : 17, :]
        nc.sync.dma_start(wgt_rows[:], half_rows.rearrange("m (c e) -> m c e", e=64))
        nc.sync.dma_start(pick_list[:], offs)
        for i in range(PACK):
            nc.sync.dma_start(planes[i][:], x_rows[:, i, :])
        nc.sync.dma_start(g_raw[:], w_rows["g"])
        for a in range(2):
            nc.sync.dma_start(w_raw["u", a], w_rows["u"][:, :, a * PASS : (a + 1) * PASS])
        sc_rows = wd_scales.bitcast(I32).rearrange("a q n -> q a n")
        for quad in range(4):
            nc.sync.dma_start(
                wd_sc[32 * quad : 32 * quad + 4, :, :].bitcast(I32), sc_rows[4 * quad : 4 * quad + 4, :, :]
            )
        nc.sync.dma_start(wd_codes[:].bitcast(I32), wd_words.rearrange("a p n t -> p a (n t)").bitcast(I32))
        nc.sync.dma_start(put_list[:], offs2)
        nc.sync.dma_start(wgo_sb[:], wgo)

        for u in range(2):
            nc.vector.transpose(wgt_turned[:, 32 * u : 32 * u + 32], wgt_rows[:, 32 * u : 32 * u + 32])
        by_block = wgt_turned[:].rearrange("p (b c) -> p c b", b=4)
        for q in range(4):
            wide = wgt_wide[q][:].rearrange("p (c b i) -> p c b i", b=4, i=16)
            narrow = by_block[:, 4 * q : 4 * q + 4, :].unsqueeze(3).to_broadcast([P, 4, 4, 16])
            nc.scalar.copy(wide, narrow)
            nc.vector.transpose(wgt_sb[:, q * 256 : (q + 1) * 256], wgt_wide[q][:])

        x_bf = [sbuf(f"x_bf{h}", [HALF, PACK], BF16) for h in range(2)]
        pairs_of_planes = [sbuf(f"picked{pr}", [2 * J], F32) for pr in range(2)]

        def pick(i, first, count):
            nc.vector.tensor_tensor(
                pairs_of_planes[i // 2][:, i % 2 * J + first : i % 2 * J + first + count],
                planes[i][:].indirect(pick_list[:, first // 16 : (first + count) // 16]),
                wgt_sb[:, first : first + count],
                MULT,
            )

        def weave_x(copy, pr, h, c=slice(0, P)):
            both = pairs_of_planes[pr][:].rearrange("p (e h c f) -> p h c e f", e=2, h=2, f=4)
            copy(x_bf[h][:, :, 2 * pr : 2 * pr + 2].rearrange("p (c f) e -> p c e f", f=4)[:, c], both[:, h, c])

        pick(0, 0, J)
        pick(1, 0, J)
        for h in range(2):
            weave_x(nc.scalar.copy, 0, h)
        pick(2, 0, J)
        for h in range(2):
            pick(3, h * HALF, HALF)
        for h in range(2):
            weave_x(nc.scalar.copy, 1, h, LOW)
            weave_x(nc.vector.tensor_copy, 1, h, HIGH)

        def part(tile, first, count=1):
            return tile[:, first * PASS : (first + count) * PASS]

        def quantize(name, src, words, tag=None):
            codes = sbuf(f"codes_{name}", [words], U32, tag)
            scales = sbuf(f"scales_{name}", [words], U8)
            nc.vector.quantize_mx(out=codes[:].bitcast(FP8X4), scales=scales[:], in_=src)
            return codes, scales

        w_bf = {("u", 1, 0): h_early[:], ("u", 1, 1): part(h_bf, 0, 2)}
        for key in (("g", 0, 0), ("g", 0, 1), ("u", 0, 0), ("u", 0, 1), ("g", 1, 0), ("g", 1, 1)):
            w_bf[key] = sbuf(f"w_bf{key[0]}{key[1]}{key[2]}", [2 * PASS], BF16)[:]

        def weave_w(copy, w, a, tp, m=slice(0, P)):
            dst = w_bf[w, a, tp].rearrange("p (t m i) -> p m i t", t=2, i=PACK)[:, m, :, :]
            src = w_raw[w, a].rearrange("p i (m t) -> p m i t", t=PACK)[:, m, :, 2 * tp : 2 * tp + 2]
            copy(dst, src)

        on_vector, on_scalar = nc.vector.tensor_copy, nc.scalar.copy
        w_q, x_q, h_q = {}, {}, {}

        def quantize_w(w, a, tp):
            w_q[w, a, tp] = quantize(f"{w}{a}{tp}", w_bf[w, a, tp], 2 * P)

        def quantize_x(h, tag=None):
            x_q[h] = quantize(f"x{h}", x_bf[h][:].rearrange("p j i -> p (j i)"), HALF, tag)

        def quantize_h(src, strips, tag=None):
            codes, scales = quantize(f"h{strips[0][0]}{strips[0][1]}", src, len(strips) * P, tag)
            for k, strip in enumerate(strips):
                h_q[strip] = codes, scales, k * P

        def first_product(w, a, s, bank):
            cols = slice((s % 4) * P, (s % 4 + 1) * P)
            for t in range(PACK):
                codes, scales = w_q[w, a, t // 2]
                m = slice((t % 2) * P, (t % 2 + 1) * P)
                nc.tensor.matmul_mx(
                    out=bank[:, t * P : (t + 1) * P],
                    lhsT=codes[:, m].bitcast(FP8X4),
                    lhsT_scale=scales[:, m],
                    rhs=x_q[s // 4][0][:, cols].bitcast(FP8X4),
                    rhs_scale=x_q[s // 4][1][:, cols],
                    start=True,
                    stop=True,
                )
            return bank[:].rearrange("p (t j) -> p j t", t=PACK)

        def woven(ap):
            return ap.rearrange("p (j t) -> p j t", t=PACK)

        def gate(a, s, dst, bank):
            nc.scalar.activation(woven(dst), first_product("g", a, s, bank), SIGMOID)

        def hidden_on_vector(dst, up, sig):
            nc.vector.tensor_tensor(woven(dst), up, woven(sig), MULT)

        def lift(a, s, dst, bank):
            nc.scalar.copy(woven(dst), first_product("u", a, s, bank))

        def supply(strips, gates, ups, gate_banks, up_banks):
            for k, (a, s) in enumerate(strips):
                gate(a, s, part(gates, k), banks[gate_banks[k]])
                lift(a, s, part(ups, k), banks[up_banks[k]])

        def inputs(name, count, gate_tag=None, up_tag=None):
            return sbuf(f"gates_{name}", [count * PASS], F32, gate_tag), sbuf(f"ups_{name}", [count * PASS], F32, up_tag)

        def hidden_on_gpsimd(dst, gates, ups):
            nc.gpsimd.tensor_tensor(dst, ups[:], gates[:], MULT)

        def down(bank, col, n, a, s, count, start, stop):
            codes, scales, first = h_q[a, s]
            m = slice(n * P, (n + 1) * P)
            cols = slice(first, first + count * P)
            nc.tensor.matmul_mx(
                out=bank[:, col : col + count * P],
                lhsT=wd_codes[:, a, m].bitcast(FP8X4),
                lhsT_scale=wd_sc[:, a, m],
                rhs=codes[:, cols].bitcast(FP8X4),
                rhs_scale=scales[:, cols],
                start=start,
                stop=stop,
            )

        def down_chunk(bank, s, a):
            for n in range(4):
                down(bank, n * P, n, a, s, 1, a == 0 and n == 0, a == 1 and n == 3)

        def weigh(engine, dst, src, blocks, s, count):
            width = count * P
            engine.tensor_tensor(
                dst.rearrange("p (n j) -> p n j", n=blocks),
                src.rearrange("p (n j) -> p n j", n=blocks),
                wgo_sb[:, s * P : s * P + width].unsqueeze(1).to_broadcast([P, blocks, width]),
                MULT,
            )

        def places(n, s, count):
            return pages[n][:].indirect(put_list[:, s * 8 : (s + count) * 8])

        def put(src, rows, s, count):
            width = count * P
            for k, n in enumerate(rows):
                nc.vector.tensor_copy(places(n, s, count), src[:, k * width : (k + 1) * width])

        def put_fused(y, n, s, count):
            nc.vector.tensor_tensor(places(n, s, count), y, wgo_sb[:, s * P : (s + count) * P], MULT)

        quantize_x(0)
        weave_w(on_scalar, "g", 1, 0)
        weave_w(on_scalar, "g", 1, 1)
        weave_w(on_vector, "g", 0, 0)
        weave_w(on_vector, "g", 0, 1)
        quantize_w("g", 0, 0)
        quantize_x(1, "w_bfg00")
        quantize_w("g", 0, 1)
        quantize_w("g", 1, 0)
        weave_w(on_scalar, "u", 0, 1)
        weave_w(on_vector, "u", 0, 0)
        quantize_w("g", 1, 1)
        quantize_w("u", 0, 0)
        quantize_w("u", 0, 1)
        early = sbuf("early", [3 * PASS], F32, "w_bfg10")
        late = sbuf("late", [3 * PASS], F32, "rawu1")
        pairs = [inputs("pair0", 2, "w_bfu00"), inputs("pair1", 2)]
        gate(0, 0, part(early, 0), banks[0])
        gate(0, 1, part(early, 1), banks[1])
        ups = {(0, s): first_product("u", 0, s, banks[2 + s]) for s in range(3)}
        weave_w(on_scalar, "u", 1, 1, HIGH)
        gate(1, 0, part(early, 2), banks[6])
        weave_w(on_vector, "u", 1, 0)
        weave_w(on_vector, "u", 1, 1, LOW)
        quantize_w("u", 1, 0)
        quantize_w("u", 1, 1)
        gate(1, 1, part(late, 0), banks[7])
        ups[1, 0] = first_product("u", 1, 0, banks[5])
        hidden_on_vector(part(h_early, 0), ups[0, 0], part(early, 0))
        hidden_on_vector(part(h_early, 1), ups[0, 1], part(early, 1))
        ups[1, 1] = first_product("u", 1, 1, banks[2])
        gate(0, 2, part(late, 1), banks[0])
        supply([(0, 3), (0, 4)], *pairs[0], (1, 7), (6, 0))
        hidden_on_vector(part(h_bf, 5), ups[1, 0], part(early, 2))
        gate(1, 2, part(late, 2), banks[5])
        quantize_h(h_early[:], [(0, 0), (0, 1)])
        down_chunk(banks[1], 0, 0)
        quantize_h(part(h_bf, 5), [(1, 0)])
        down_chunk(banks[1], 0, 1)
        hidden_on_vector(part(h_bf, 6), ups[1, 1], part(late, 0))
        hidden_on_vector(part(h_bf, 4), ups[0, 2], part(late, 1))
        quantize_h(part(h_bf, 6), [(1, 1)])
        ups[1, 2] = first_product("u", 1, 2, banks[3])

        triples = [inputs(f"triple{b}", 3, f"plane{1 + b}", f"picked{b}") for b in range(2)]
        weighed = [sbuf(f"weighed{b}", [PASS], F32) for b in range(3)]
        ys = [sbuf(f"y{b}", [PASS], F32) for b in range(3)]

        for bank, rows in ((banks[7], (0, 1)), (banks[5], (2, 3))):
            for a in range(2):
                for k, n in enumerate(rows):
                    down(bank, k * P, n, 1 - a, 1, 1, a == 0 and k == 0, a == 1 and k == 1)
        weigh(nc.vector, weighed[0][:, 0:P], banks[1][:, 0:P], 1, 0, 1)
        weigh(nc.vector, weighed[0][:, P:PASS], banks[1][:, P:PASS], 3, 0, 1)
        hidden_on_vector(part(h_bf, 3), ups[1, 2], part(late, 2))
        put(weighed[0], range(4), 0, 1)
        hidden_on_gpsimd(part(h_bf, 5, 2), *pairs[0])
        y_early = sbuf("y_early", [2 * P], F32)
        nc.scalar.copy(y_early[:], banks[7][:, 0 : 2 * P])
        weigh(nc.gpsimd, weighed[1][:, 0 : 2 * P], y_early[:], 2, 1, 1)
        put(weighed[1], (0, 1), 1, 1)
        supply([(1, 3), (1, 4)], *pairs[1], (6, 0), (2, 4))
        h_pair = sbuf("h_pair", [2 * PASS], BF16, "y_early")
        hidden_on_gpsimd(h_pair[:], *pairs[1])
        nc.scalar.copy(ys[0][:, 0 : 2 * P], banks[5][:, 0 : 2 * P])
        weigh(nc.gpsimd, pairs[1][0][:, 0 : 2 * P], ys[0][:, 0 : 2 * P], 2, 1, 1)

        quantize_h(h_pair[:], [(1, 3), (1, 4)])
        quantize_h(part(h_bf, 3, 4), [(1, 2), (0, 2), (0, 3), (0, 4)], "ups_pair1")

        def down_double(bank, rows):
            for k, n in enumerate(rows):
                down(bank, k * 2 * P, n, 0, 2, 2, k == 0, False)
                down(bank, k * 2 * P, n, 1, 2, 1, False, False)
                down(bank, k * 2 * P + P, n, 1, 3, 1, False, k == 1)

        supply([(0, 5), (0, 6), (0, 7)], *triples[0], (6, 0, 6), (2, 4, 2))
        supply([(1, 5), (1, 6)], *triples[1], (0, 6), (4, 2))
        gate(1, 7, part(triples[1][0], 2), banks[0])
        down_double(banks[4], (0, 1))
        down_double(banks[6], (2, 3))
        put(pairs[1][0], (2, 3), 1, 1)
        for a in range(2):
            down_chunk(banks[2], 4, a)
        for k in range(2):
            cols = slice(k * 2 * P, (k + 1) * 2 * P)
            weigh(nc.vector, weighed[0][:, cols], banks[4][:, cols], 1, 2, 2)
        put(weighed[0], (0, 1), 2, 2)
        hidden_on_gpsimd(part(h_bf, 4, 3), *triples[0])
        y_mid = sbuf("y_mid", [PASS + P], F32)
        nc.scalar.copy(y_mid[:, 0:PASS], banks[6][:])
        weigh(nc.gpsimd, weighed[2][:], y_mid[:, 0:PASS], 2, 2, 2)
        put(weighed[2], (2, 3), 2, 2)
        nc.scalar.copy(y_mid[:, PASS : PASS + P], banks[2][:, 0:P])
        weigh(nc.gpsimd, weighed[1][:, 0:P], y_mid[:, PASS : PASS + P], 1, 4, 1)
        put(weighed[1], (0,), 4, 1)
        lift(1, 7, part(triples[1][1], 2), banks[4])
        h_last = sbuf("h_last", [3 * PASS], BF16, "y_mid")
        hidden_on_gpsimd(h_last[:], *triples[1])

        quantize_h(part(h_bf, 4, 3), [(0, 5), (0, 6), (0, 7)], "picked1")
        quantize_h(h_last[:], [(1, 5), (1, 6), (1, 7)])
        held = triples[1][0]
        nc.scalar.copy(held[:, P:PASS], banks[2][:, P:PASS])
        for n in range(1, 4):
            put_fused(held[:, n * P : (n + 1) * P], n, 4, 1)
        for n in range(4):
            bank = banks[(1, 3, 5, 7)[n]]
            for step, a in enumerate((0, 1) if n == 0 else (1, 0)):
                down(bank, 0, n, a, 5, 2, step == 0, False)
                down(bank, 2 * P, n, a, 7, 1, False, step == 1)
            y = ys[n % len(ys)][:, 0 : 3 * P]
            nc.scalar.copy(y, bank[:, 0 : 3 * P])
            put_fused(y, n, 5, 3)
            nc.sync.dma_start(out[n * P : (n + 1) * P, :], pages[n][:])
